import numpy as np
import ml_dtypes


def mxq(x, axis, fmt="e4m3"):
    dtype, down = {"e4m3": (ml_dtypes.float8_e4m3fn, 7), "e5m2": (ml_dtypes.float8_e5m2, 14)}[fmt]
    v = np.moveaxis(np.asarray(x, np.float32).astype(ml_dtypes.bfloat16).astype(np.float64), axis, -1)
    blocks = v.reshape(v.shape[:-1] + (-1, 32))
    amax = np.abs(blocks).max(-1, keepdims=True)
    byte = np.maximum(np.where(amax > 0, np.frexp(amax)[1] - 1 + 127, 0) - down, 1)
    scale = np.exp2(byte - 127.0)
    codes = (blocks / scale).astype(np.float32).astype(dtype).astype(np.float64)
    return np.moveaxis((codes * scale).reshape(v.shape), -1, axis)


WIDE = False


def mx_kscale(k):
    if not WIDE:
        return np.ones(k)
    levels = np.array([10, -10, 5, -5, 0])
    if k % 512:
        return np.exp2(np.random.permutation(np.resize(levels, k // 32))).repeat(32)
    a = np.empty((k // 512, 16))
    for p in range(k // 512):
        a[p, :8] = np.random.permutation(np.resize(levels, 8))
        for g in range(8):
            far = levels[np.abs(levels - a[p, g]) >= 10]
            a[p, g + 8] = far[np.random.randint(len(far))]
    return np.exp2(a.ravel()).repeat(32)


def f64(x):
    return np.asarray(x).astype(np.float64)


def striped(idx):
    return np.tile(idx.reshape(-1, 16).T, (8, 1)).astype(np.uint16)


def unstriped(offs):
    return offs[:16].T.reshape(-1).astype(np.int64)


def relu(v):
    return np.maximum(v, 0.0)


K, T, E, C, H, N = 1024, 512, 4, 256, 512, 256


def by_expert(wq, xq):
    return np.concatenate([wq[e].T @ xq[:, e * C:(e + 1) * C] for e in range(E)], axis=1)


def setup_inputs():
    n = np.random.standard_normal
    s = mx_kscale(K)[:, None]
    u = mx_kscale(H)
    first = np.random.permutation(np.repeat(np.arange(E), T // E))
    second = (first + 1 + np.random.permutation(np.repeat(np.arange(E - 1), -(-T // (E - 1)))[:T])) % E
    while np.bincount(second, minlength=E).max() != T // E:
        load = np.bincount(second, minlength=E); hi, lo = int(load.argmax()), int(load.argmin())
        t = np.flatnonzero((second == hi) & (first != lo))[0]; second[t] = lo
    slot_token = np.empty(E * C, np.int64); pos = np.empty((2, T), np.int64); fill = np.zeros(E, np.int64)
    place = np.stack([np.random.permutation(C) for _ in range(E)])
    for r, deal in enumerate((first, second)):
        for t in np.random.permutation(T):
            e = deal[t]; j = e * C + place[e, fill[e]]; fill[e] += 1; slot_token[j] = t; pos[r, t] = j
    g = np.random.uniform(0.2, 0.8, T)
    return {
        "xT": (n((K, T)) * s).astype(np.float32),
        "w1": (n((E + 1, K, H)) / np.sqrt(K) / s[None]).astype(np.float32),
        "w3": (n((E + 1, K, H)) / np.sqrt(K) / s[None] * u[None, None, :]).astype(np.float32),
        "w2": (n((E + 1, H, N)) / np.sqrt(H) / u[None, :, None]).astype(np.float32),
        "gate": np.stack([np.tile(g, (N, 1)), np.tile(1.0 - g, (N, 1))]).astype(np.float32),
        "offs": striped(slot_token),
        "pos1": striped(pos[0]),
        "pos2": striped(pos[1]),
    }


def reference(xT, w1, w3, w2, gate, offs, pos1, pos2):
    idx = unstriped(offs)
    w1q, w3q, w2q = mxq(f64(w1), 1, "e4m3"), mxq(f64(w3), 1, "e4m3"), mxq(f64(w2), 1, "e4m3")
    xs = mxq(f64(xT), 0, "e4m3")
    hs = relu(w1q[E].T @ xs) * (w3q[E].T @ xs)
    ys = w2q[E].T @ mxq(hs, 0, "e4m3")
    xq = mxq(f64(xT)[:, idx], 0, "e4m3")
    h = relu(by_expert(w1q, xq))
    h = h * by_expert(w3q, xq)
    y = by_expert(w2q, mxq(h, 0, "e4m3"))
    return ys + f64(gate[0]) * y[:, unstriped(pos1)] + f64(gate[1]) * y[:, unstriped(pos2)]

@@ -1,0 +1,339 @@
+from contextlib import ExitStack
+
+import concourse.mybir as mybir
+
+K, T, E, C, H, N = 1024, 512, 4, 256, 512, 256
+
+FLOPS = 2 * (E * C + T) * (2 * K * H + H * N)
+
+F32 = mybir.dt.float32
+BF16 = mybir.dt.bfloat16
+U32 = mybir.dt.uint32
+U16 = mybir.dt.uint16
+U8 = mybir.dt.uint8
+FP8X4 = mybir.dt.float8_e4m3fn_x4
+MULT = mybir.AluOpType.mult
+RELU = mybir.ActivationFunctionType.Relu
+
+P = 128
+J = 4
+KC = K // (P * J)
+G = 128
+LOOKAHEAD = 8
+
+
+def tile_moe_shr_glu_relu_kernel(tc, xT, w1, w3, w2, gate, offs, pos1, pos2, out):
+    nc = tc.nc
+    with ExitStack() as ctx:
+        keep = ctx.enter_context(tc.tile_pool(name="keep", bufs=1))
+        rawp = ctx.enter_context(tc.tile_pool(name="rawp", bufs=7))
+        raw2p = ctx.enter_context(tc.tile_pool(name="raw2p", bufs=3))
+        grp = ctx.enter_context(tc.tile_pool(name="grp", bufs=4))
+        codep = ctx.enter_context(tc.tile_pool(name="codep", bufs=10))
+        code2p = ctx.enter_context(tc.tile_pool(name="code2p", bufs=2))
+        gxp = ctx.enter_context(tc.tile_pool(name="gxp", bufs=4))
+        tokp = ctx.enter_context(tc.tile_pool(name="tokp", bufs=2))
+        hp = ctx.enter_context(tc.tile_pool(name="hp", bufs=4))
+        psa = ctx.enter_context(tc.psum_pool(name="psa", bufs=3))
+        psb = ctx.enter_context(tc.psum_pool(name="psb", bufs=3))
+        psy = ctx.enter_context(tc.psum_pool(name="psy", bufs=2))
+
+        offs_t = keep.tile([P, E * C // 16], U16, name="offs_t")
+        pos_t = [keep.tile([P, T // 16], U16, name="pos1_t"), keep.tile([P, T // 16], U16, name="pos2_t")]
+        x_raw = [keep.tile([P, J, T], F32, name="x_raw%d" % c) for c in range(KC)]
+
+        def load_x(c, u):
+            src = xT[c * P * J : (c + 1) * P * J, :].rearrange("(p j) w -> p j w", j=J)
+            nc.sync.dma_start(out=x_raw[c][:, 2 * u : 2 * u + 2, :], in_=src[:, 2 * u : 2 * u + 2, :])
+
+        load_x(0, 0)
+        nc.sync.dma_start(offs_t[:], offs)
+
+        chunks = []
+        for e in range(E + 1):
+            chunks += [(e, "w1", 0), (e, "w1", 1), (e, "w3", 0), (e, "w3", 1), (e, "w2", 0)]
+        raws = {}
+        gates = [keep.tile([P, 2, T], F32, name="gate0"), keep.tile([P, 2, T], F32, name="gate1")]
+
+        def load(q):
+            e, which, c = chunks[q]
+            if e == E and which == "w1" and c == 0:
+                nc.sync.dma_start(pos_t[0][:], pos1)
+                nc.sync.dma_start(pos_t[1][:], pos2)
+                for r in range(2):
+                    nc.sync.dma_start(out=gates[r][:], in_=gate[r].rearrange("(h p) t -> p h t", p=P))
+            if which == "w2":
+                t = raw2p.tile([P, J, N], F32, name="raw2")
+                nc.sync.dma_start(out=t[:], in_=w2[e].rearrange("(p j) w -> p j w", j=J))
+            else:
+                w = w1 if which == "w1" else w3
+                t = rawp.tile([P, J, H], F32, name="raw")
+                nc.sync.dma_start(out=t[:], in_=w[e, c * P * J : (c + 1) * P * J, :].rearrange("(p j) w -> p j w", j=J))
+            raws[q] = t
+
+        load(0)
+        load_x(0, 1)
+        load(1)
+        load_x(1, 0)
+        load(2)
+        load_x(1, 1)
+        for q in range(3, LOOKAHEAD):
+            load(q)
+
+        x_pair = {}
+
+        def pair_tokens(c, u):
+            t = keep.tile([P, T, 2], BF16, name="x_pair%d%d" % (c, u), align_bytes=64)
+            pairs = x_raw[c][:, 2 * u : 2 * u + 2, :].rearrange("p e n -> p n e")
+            if u == 0:
+                nc.vector.tensor_copy(out=t[:], in_=pairs)
+            else:
+                nc.scalar.copy(out=t[:], in_=pairs)
+            x_pair[c, u] = t
+
+        xs_codes = keep.tile([P, KC, T], U32, name="xs_codes", align_bytes=64)
+        xs_scales = keep.tile([P, KC, T], U8, name="xs_scales", align_bytes=64)
+        xs_grp = []
+        for c in range(KC):
+            t = keep.tile([P, T, J], BF16, name="xs_grp%d" % c, align_bytes=64)
+            xs_grp.append(t)
+
+        def group_shared_tokens(c, part):
+            cols = slice(part * T // XPARTS, (part + 1) * T // XPARTS)
+            nc.gpsimd.tensor_scalar(
+                out=xs_grp[c][:, cols, :].rearrange("p (n i) j -> p n j i", i=4), in0=x_raw[c][:, :, cols].rearrange("p j (n i) -> p n j i", i=4),
+                scalar1=1.0, scalar2=0.0, op0=MULT, op1=mybir.AluOpType.add,
+            )
+
+        gx = {}
+
+        def gather(e, c, u):
+            if e not in gx:
+                gx[e] = gxp.tile([P, KC * C * J], BF16, name="gx", align_bytes=64)
+            words = gx[e][:].bitcast(U32).rearrange("p (c n u) -> p c n u", c=KC, u=2)
+            window = x_pair[c, u][:].rearrange("p n e -> p (n e)").bitcast(U32)
+            nc.vector.tensor_copy(words[:, c, :, u], window.indirect(offs_t[:, e * C // 16 : (e + 1) * C // 16]))
+
+        xcodes = {}
+
+        def quantise_tokens(e):
+            codes = tokp.tile([P, KC, C], U32, name="x_codes", align_bytes=64)
+            scales = tokp.tile([P, KC, C], U8, name="x_scales", align_bytes=64)
+            nc.vector.quantize_mx(
+                out=codes[:].rearrange("p c n -> p (c n)").bitcast(FP8X4), scales=scales[:].rearrange("p c n -> p (c n)"), in_=gx[e][:]
+            )
+            xcodes[e] = (codes, scales)
+
+        def quantise_shared_tokens(c):
+            nc.vector.quantize_mx(out=xs_codes[:, c, :].bitcast(FP8X4), scales=xs_scales[:, c, :], in_=xs_grp[c][:].rearrange("p n j -> p (n j)"))
+            xcodes[E] = (xs_codes, xs_scales)
+
+        grouped = {}
+        wcodes = {}
+
+        def copy_weights(q):
+            e, which, c = chunks[q]
+            if which == "w2":
+                g = grp.tile([P, N * J], BF16, name="grp2", align_bytes=64)
+                dst = g[:].rearrange("p (n i j) -> p n j i", i=4, j=J)
+                src = raws[q][:].rearrange("p j (n i) -> p n j i", i=4)
+                count = N // 4
+            else:
+                g = grp.tile([P, H * J], BF16, name="grp", align_bytes=64)
+                dst = g[:].rearrange("p (t m j) -> p m j t", t=J, j=J)
+                src = raws[q][:].rearrange("p j (m t) -> p m j t", t=J)
+                count = P
+            share = VECTOR_SHARE[e][which, c] * count // 128
+            if share < count:
+                nc.scalar.copy(out=dst[:, share:], in_=src[:, share:])
+            if share > 0:
+                nc.vector.tensor_copy(out=dst[:, :share], in_=src[:, :share])
+            grouped[q] = g
+
+        def quantise_weights(q):
+            e, which, c = chunks[q]
+            if which == "w2":
+                codes = code2p.tile([P, N], U32, name="w2_codes", align_bytes=64)
+                scales = code2p.tile([P, N], U8, name="w2_scales", align_bytes=64)
+            else:
+                codes = codep.tile([P, H], U32, name="w_codes", align_bytes=64)
+                scales = codep.tile([P, H], U8, name="w_scales", align_bytes=64)
+            nc.vector.quantize_mx(out=codes[:].bitcast(FP8X4), scales=scales[:], in_=grouped[q][:])
+            wcodes[e, which, c] = (codes, scales)
+
+        def first_layer(e, which, g, pool):
+            bank = pool.tile([P, J, G], F32, name="bank_" + which)
+            xc, xsc = xcodes[e]
+            for t in range(J):
+                for c in range(KC):
+                    wc, wsc = wcodes[e, which, c]
+                    nc.tensor.matmul_mx(
+                        out=bank[:, t, :],
+                        lhsT=wc[:, t * P : (t + 1) * P].bitcast(FP8X4),
+                        lhsT_scale=wsc[:, t * P : (t + 1) * P],
+                        rhs=xc[:, c, g * G : (g + 1) * G].bitcast(FP8X4),
+                        rhs_scale=xsc[:, c, g * G : (g + 1) * G],
+                        start=(c == 0),
+                        stop=(c == KC - 1),
+                    )
+            return bank
+
+        relus = {}
+        hgrp = {}
+        hcodes = {}
+
+        banks = {}
+
+        def gate_matmuls(e, g):
+            banks[e, "w1", g] = first_layer(e, "w1", g, psa)
+
+        def up_matmuls(e, g):
+            banks[e, "w3", g] = first_layer(e, "w3", g, psb)
+
+        def gate_half(e, g):
+            bank = banks[e, "w1", g]
+            r = hp.tile([P, G, J], F32, name="relu_a")
+            nc.scalar.activation(out=r[:], in_=bank[:].rearrange("p t n -> p n t"), func=RELU)
+            relus[e, g] = r
+
+        def up_half(e, g):
+            bank = banks[e, "w3", g]
+            if g % 2 == 0:
+                hgrp[e, g // 2] = hp.tile([P, 2 * G, J], BF16, name="h_grp", align_bytes=64)
+            h = hgrp[e, g // 2]
+            nc.vector.tensor_tensor(
+                out=h[:, (g % 2) * G : (g % 2 + 1) * G, :], in0=bank[:].rearrange("p t n -> p n t"), in1=relus[e, g][:], op=MULT
+            )
+
+        def quantise_hidden(e, pair, lo, hi):
+            if (e, pair) not in hcodes:
+                codes = hp.tile([P, 2 * G], U32, name="h_codes", align_bytes=64)
+                scales = hp.tile([P, 2 * G], U8, name="h_scales", align_bytes=64)
+                hcodes[e, pair] = (codes, scales)
+            codes, scales = hcodes[e, pair]
+            nc.vector.quantize_mx(
+                out=codes[:, lo:hi].bitcast(FP8X4), scales=scales[:, lo:hi], in_=hgrp[e, pair][:, lo:hi, :].rearrange("p n j -> p (n j)")
+            )
+
+        ybank = {}
+
+        def second_layer(e, pair, lo, hi):
+            wc, wsc = wcodes[e, "w2", 0]
+            if (e, pair) not in ybank:
+                ybank[e, pair] = psy.tile([P, 2, 2 * G], F32, name="bank_y")
+            bank = ybank[e, pair]
+            codes, scales = hcodes[e, pair]
+            for half in range(2):
+                nc.tensor.matmul_mx(
+                    out=bank[:, half, lo:hi],
+                    lhsT=wc[:, half * P : (half + 1) * P].bitcast(FP8X4),
+                    lhsT_scale=wsc[:, half * P : (half + 1) * P],
+                    rhs=codes[:, lo:hi].bitcast(FP8X4),
+                    rhs_scale=scales[:, lo:hi],
+                    start=True,
+                    stop=True,
+                )
+
+        y_sb = [keep.tile([P, E * C], F32, name="y_sb0"), keep.tile([P, E * C], F32, name="y_sb1")]
+
+        def store_slots(e):
+            for half in range(2):
+                nc.scalar.copy(out=y_sb[half][:, e * C : (e + 1) * C], in_=ybank[e, 0][:, half, :])
+
+        picked = [keep.tile([P, 2, T], F32, name="picked0"), keep.tile([P, 2, T], F32, name="picked1")]
+        combined = keep.tile([P, 2, T], F32, name="combined")
+        result = keep.tile([P, 2, T], F32, name="result")
+
+        def pick(r, half):
+            nc.vector.tensor_tensor(out=picked[r][:, half, :], in0=y_sb[half][:].indirect(pos_t[r][:]), in1=gates[r][:, half, :], op=MULT)
+
+        def finish(pair):
+            cols = slice(pair * 2 * G, (pair + 1) * 2 * G)
+            nc.vector.tensor_add(out=result[:, :, cols], in0=ybank[E, pair][:], in1=combined[:, :, cols])
+            for half in range(2):
+                nc.sync.dma_start(out=out[half * P : (half + 1) * P, cols], in_=result[:, half, cols])
+
+        def shared_group(g):
+            up_half(E, g)
+
+        def shared_out(g):
+            lo, hi = (g % 2) * G, (g % 2 + 1) * G
+            quantise_hidden(E, g // 2, lo, hi)
+            second_layer(E, g // 2, lo, hi)
+            if g % 2 == 1:
+                finish(g // 2)
+
+        def combine():
+            nc.vector.tensor_add(out=combined[:], in0=picked[0][:], in1=picked[1][:])
+
+        later = {}
+
+        def at(step, rank, *call):
+            later.setdefault(step, []).append((rank, len(later.get(step, [])), call))
+
+        LQ, LR, LB, LH, LY = LAGS
+        nq = len(chunks)
+        for c in range(KC):
+            for u in range(2):
+                at(2 * c + u, -2, pair_tokens, c, u)
+                for e in range(E):
+                    at(2 * c + u + GATHER[e][0], GATHER[e][1], gather, e, c, u)
+        for e in range(E):
+            at(3 + GATHER[e][0] + (e > 0), GATHER[e][1], quantise_tokens, e)
+        for c in range(KC):
+            for part in range(XPARTS):
+                at(XSTEP[c], 7, group_shared_tokens, c, part)
+        for q in range(nq):
+            e, which, c = chunks[q]
+            groups = T // G if e == E else C // G
+            if q + LOOKAHEAD < nq:
+                at(q, -9, load, q + LOOKAHEAD)
+            at(q, 1, copy_weights, q)
+            at(q + LQ, 2, quantise_weights, q)
+            if c == 1:
+                base = q + LQ
+                if e < E:
+                    ready = 3 + GATHER[e][0] + (e > 0) + (GATHER[e][1] > 2.9)
+                    base = max(base, ready)
+                for g in range(groups):
+                    if which == "w1":
+                        at(base, 3, gate_matmuls, e, g) if e < E or g < 3 else at(base + LR, 4, gate_matmuls, e, g)
+                        at(base + LR, 4, gate_half, e, g)
+                    elif e < E:
+                        at(base, 3, up_matmuls, e, g)
+                        at(base + LB, 5, up_half, e, g)
+                if which == "w3" and e < E:
+                    at(base + LB + LH, RH, quantise_hidden, e, 0, 0, C)
+                    at(base + LB + LH, RH, second_layer, e, 0, 0, C)
+                    at(base + LB + LH + LY, RY, store_slots, e)
+        at(XSTEP[0] + 5, 6, quantise_shared_tokens, 0)
+        at(XSTEP[1] + 5, 6, quantise_shared_tokens, 1)
+        s0 = 5 * E
+        for r in range(2):
+            for half in range(2):
+                at(s0 + PICK[2 * r + half], 6, pick, r, half)
+        at(s0 + PICK[4], 6, combine)
+        n = nq + LQ
+        for g in range(3):
+            at(n - 1, 3, up_matmuls, E, g)
+        at(n, 0, shared_group, 0)
+        at(n, 0, shared_group, 1)
+        at(n, 1, up_matmuls, E, 3)
+        at(n, 1, shared_out, 0)
+        at(n, 2, shared_group, 2)
+        at(n, 3, shared_out, 1)
+        at(n, 4, shared_group, 3)
+        at(n, 5, shared_out, 2)
+        at(n, 6, shared_out, 3)
+        for step in sorted(later):
+            for rank, order, call in sorted(later[step], key=lambda item: item[:2]):
+                call[0](*call[1:])
+
+
+XPARTS, XSTEP = 4, (11, 5)
+GATHER = [[0, 4.5], [1, 1.5], [4, 4.5], [9, 6]]
+LAGS = (1, 1, 1, 1, 1)
+RH, RY, RG = (2, 1, 6)
+PICK = (4, 2, 2, 3, 4)
+
+VECTOR_SHARE = [{('w1', 0): 96, ('w1', 1): 0, ('w3', 0): 80, ('w3', 1): 0, ('w2', 0): 0}, {('w1', 0): 0, ('w1', 1): 0, ('w3', 0): 48, ('w3', 1): 0, ('w2', 0): 96}, {('w1', 0): 16, ('w1', 1): 0, ('w3', 0): 128, ('w3', 1): 0, ('w2', 0): 16}, {('w1', 0): 80, ('w1', 1): 96, ('w3', 0): 32, ('w3', 1): 80, ('w2', 0): 64}, {('w1', 0): 80, ('w1', 1): 48, ('w3', 0): 0, ('w3', 1): 32, ('w2', 0): 0}]

@@ -1,6 +1,7 @@
 from contextlib import ExitStack
 
 import concourse.mybir as mybir
+from concourse.masks import make_identity
 
 K, T, E, C, H, N = 1024, 512, 4, 256, 512, 256
 
@@ -19,321 +20,290 @@ P = 128
 J = 4
 KC = K // (P * J)
 G = 128
-LOOKAHEAD = 8
+BLOCKS = 2 * KC
+RAW_SETS = 3
+
+GATHERING_SHARE = (0, 0, 0, 96)
+LAST_ROUTED_SHARE = (64, 64, 64, 64)
+SHARED_SHARE = (0, 0, 0, 64)
 
 
 def tile_moe_shr_glu_relu_kernel(tc, xT, w1, w3, w2, gate, offs, pos1, pos2, out):
     nc = tc.nc
     with ExitStack() as ctx:
         keep = ctx.enter_context(tc.tile_pool(name="keep", bufs=1))
-        rawp = ctx.enter_context(tc.tile_pool(name="rawp", bufs=7))
-        raw2p = ctx.enter_context(tc.tile_pool(name="raw2p", bufs=3))
-        grp = ctx.enter_context(tc.tile_pool(name="grp", bufs=4))
-        codep = ctx.enter_context(tc.tile_pool(name="codep", bufs=10))
-        code2p = ctx.enter_context(tc.tile_pool(name="code2p", bufs=2))
-        gxp = ctx.enter_context(tc.tile_pool(name="gxp", bufs=4))
-        tokp = ctx.enter_context(tc.tile_pool(name="tokp", bufs=2))
-        hp = ctx.enter_context(tc.tile_pool(name="hp", bufs=4))
-        psa = ctx.enter_context(tc.psum_pool(name="psa", bufs=3))
-        psb = ctx.enter_context(tc.psum_pool(name="psb", bufs=3))
-        psy = ctx.enter_context(tc.psum_pool(name="psy", bufs=2))
+        twice = ctx.enter_context(tc.tile_pool(name="twice", bufs=1))
+        psum = ctx.enter_context(tc.psum_pool(name="psum", bufs=1))
+
+        def sbuf(name, shape, dtype):
+            return keep.tile(shape, dtype, name=name, align_bytes=64)
+
+        def mx_tiles(name, width):
+            return sbuf(name + "_codes", [P, width], U32), sbuf(name + "_scales", [P, width], U8)
+
+        def quantise(mx, cols, values):
+            nc.vector.quantize_mx(out=mx[0][:, cols].bitcast(FP8X4), scales=mx[1][:, cols], in_=values)
+
+        def matmul(acc, lhs, lhs_cols, rhs, rhs_cols, start, stop):
+            nc.tensor.matmul_mx(
+                out=acc,
+                lhsT=lhs[0][:, lhs_cols].bitcast(FP8X4),
+                lhsT_scale=lhs[1][:, lhs_cols],
+                rhs=rhs[0][:, rhs_cols].bitcast(FP8X4),
+                rhs_scale=rhs[1][:, rhs_cols],
+                start=start,
+                stop=stop,
+            )
 
         offs_t = keep.tile([P, E * C // 16], U16, name="offs_t")
         pos_t = [keep.tile([P, T // 16], U16, name="pos1_t"), keep.tile([P, T // 16], U16, name="pos2_t")]
-        x_raw = [keep.tile([P, J, T], F32, name="x_raw%d" % c) for c in range(KC)]
+        banks = [psum.tile([P, 512], F32, name="bank%d" % b) for b in range(8)]
+        planes = [(c, u) for c in range(KC) for u in range(2)]
+        x_raw = dict([(cu, sbuf("x_raw%d%d" % cu, [P, 2, T], F32)) for cu in planes])
+        x_pair = [sbuf("x_pair%d" % c, [P, 2 * T * 2], BF16) for c in range(KC)]
+        raw = [[sbuf("raw%d%d" % (s, b), [P, J * H], F32) for b in range(BLOCKS)] for s in range(RAW_SETS)]
+        rounded = [sbuf("rounded%d" % b, [P, H * J], BF16) for b in range(BLOCKS)]
+        w_mx = [mx_tiles("w%d" % b, H) for b in range(BLOCKS)]
+        raw_set = [raw[0], raw[1], raw[2], raw[0], raw[2]]
+        last_w2 = twice.tile([P, 2 * J * N], F32, name="last_w2", offset=0)
+        y_sb = [twice.tile([P, E * C], F32, name="y_sb%d" % half, offset=half * E * C * 4) for half in range(2)]
+        raw2 = [raw[1][1][:, 0 : J * N], raw[1][1][:, J * N : 2 * J * N], last_w2[:, 0 : J * N], last_w2[:, J * N : 2 * J * N], raw[0][1][:, 0 : J * N]]
+        rounded2 = [sbuf("rounded2_%d" % e, [P, N * J], BF16) for e in range(E + 1)]
+        w2_mx = [mx_tiles("second%d" % e, N) for e in range(E + 1)]
+        woven = [sbuf("woven%d" % s, [P, KC * C * J], BF16) for s in range(2)]
+        first_words = [sbuf("first_words%d" % e, [P, KC * C * J], BF16) for e in range(2)]
+        slot_mx = [(sbuf("slot_codes%d" % s, [P, KC * C], U32), w_mx[1][1][4 * (s + 1) : P, :]) for s in range(2)]
+        all_woven = [sbuf("all_woven%d" % c, [P, T * J], BF16) for c in range(KC)]
+        all_mx = mx_tiles("all", KC * T)
+        hidden = sbuf("hidden", [P, T * J], BF16)
+        h_mx = [mx_tiles("h%d" % e, T if e == E else C) for e in range(E + 1)]
+        gate_row = sbuf("gate_row", [P, 2, J], F32)
+        gates = [sbuf("gates%d" % r, [P, T], F32) for r in range(2)]
+        identity = sbuf("identity", [P, P], F32)
+        first_term = sbuf("first_term", [P, T], F32)
+        result = sbuf("result", [P, 2, T], F32)
 
         def load_x(c, u):
             src = xT[c * P * J : (c + 1) * P * J, :].rearrange("(p j) w -> p j w", j=J)
-            nc.sync.dma_start(out=x_raw[c][:, 2 * u : 2 * u + 2, :], in_=src[:, 2 * u : 2 * u + 2, :])
+            nc.sync.dma_start(out=x_raw[c, u][:], in_=src[:, 2 * u : 2 * u + 2, :])
 
-        load_x(0, 0)
-        nc.sync.dma_start(offs_t[:], offs)
+        def load_block(e, b):
+            w = (w1, w3)[b // KC]
+            c = b % KC
+            nc.sync.dma_start(out=raw_set[e][b][:], in_=w[e, c * P * J : (c + 1) * P * J, :].rearrange("(p j) w -> p (j w)", j=J))
 
-        chunks = []
-        for e in range(E + 1):
-            chunks += [(e, "w1", 0), (e, "w1", 1), (e, "w3", 0), (e, "w3", 1), (e, "w2", 0)]
-        raws = {}
-        gates = [keep.tile([P, 2, T], F32, name="gate0"), keep.tile([P, 2, T], F32, name="gate1")]
+        def load_w2(e):
+            nc.sync.dma_start(out=raw2[e], in_=w2[e].rearrange("(p j) w -> p (j w)", j=J))
 
-        def load(q):
-            e, which, c = chunks[q]
-            if e == E and which == "w1" and c == 0:
-                nc.sync.dma_start(pos_t[0][:], pos1)
-                nc.sync.dma_start(pos_t[1][:], pos2)
-                for r in range(2):
-                    nc.sync.dma_start(out=gates[r][:], in_=gate[r].rearrange("(h p) t -> p h t", p=P))
-            if which == "w2":
-                t = raw2p.tile([P, J, N], F32, name="raw2")
-                nc.sync.dma_start(out=t[:], in_=w2[e].rearrange("(p j) w -> p j w", j=J))
-            else:
-                w = w1 if which == "w1" else w3
-                t = rawp.tile([P, J, H], F32, name="raw")
-                nc.sync.dma_start(out=t[:], in_=w[e, c * P * J : (c + 1) * P * J, :].rearrange("(p j) w -> p j w", j=J))
-            raws[q] = t
+        def pair_plane(c, u):
+            return x_pair[c][:, u * T * 2 : (u + 1) * T * 2]
 
-        load(0)
-        load_x(0, 1)
-        load(1)
-        load_x(1, 0)
-        load(2)
-        load_x(1, 1)
-        for q in range(3, LOOKAHEAD):
-            load(q)
+        def pair_tokens(c, u, copy):
+            copy(out=pair_plane(c, u).rearrange("p (n i e) -> p n e i", i=4, e=2), in_=x_raw[c, u][:].rearrange("p e (n i) -> p n e i", i=4))
 
-        x_pair = {}
-
-        def pair_tokens(c, u):
-            t = keep.tile([P, T, 2], BF16, name="x_pair%d%d" % (c, u), align_bytes=64)
-            pairs = x_raw[c][:, 2 * u : 2 * u + 2, :].rearrange("p e n -> p n e")
-            if u == 0:
-                nc.vector.tensor_copy(out=t[:], in_=pairs)
-            else:
-                nc.scalar.copy(out=t[:], in_=pairs)
-            x_pair[c, u] = t
-
-        xs_codes = keep.tile([P, KC, T], U32, name="xs_codes", align_bytes=64)
-        xs_scales = keep.tile([P, KC, T], U8, name="xs_scales", align_bytes=64)
-        xs_grp = []
-        for c in range(KC):
-            t = keep.tile([P, T, J], BF16, name="xs_grp%d" % c, align_bytes=64)
-            xs_grp.append(t)
-
-        def group_shared_tokens(c, part):
-            cols = slice(part * T // XPARTS, (part + 1) * T // XPARTS)
-            nc.gpsimd.tensor_scalar(
-                out=xs_grp[c][:, cols, :].rearrange("p (n i) j -> p n j i", i=4), in0=x_raw[c][:, :, cols].rearrange("p j (n i) -> p n j i", i=4),
-                scalar1=1.0, scalar2=0.0, op0=MULT, op1=mybir.AluOpType.add,
-            )
-
-        gx = {}
+        def gathered(e):
+            return first_words[e][:] if e < 2 else rounded[BLOCKS - 1][:]
 
         def gather(e, c, u):
-            if e not in gx:
-                gx[e] = gxp.tile([P, KC * C * J], BF16, name="gx", align_bytes=64)
-            words = gx[e][:].bitcast(U32).rearrange("p (c n u) -> p c n u", c=KC, u=2)
-            window = x_pair[c, u][:].rearrange("p n e -> p (n e)").bitcast(U32)
-            nc.vector.tensor_copy(words[:, c, :, u], window.indirect(offs_t[:, e * C // 16 : (e + 1) * C // 16]))
+            words = gathered(e).bitcast(U32)
+            first = (2 * c + u) * C
+            nc.vector.tensor_copy(words[:, first : first + C], pair_plane(c, u).bitcast(U32).indirect(offs_t[:, e * C // 16 : (e + 1) * C // 16]))
 
-        xcodes = {}
-
-        def quantise_tokens(e):
-            codes = tokp.tile([P, KC, C], U32, name="x_codes", align_bytes=64)
-            scales = tokp.tile([P, KC, C], U8, name="x_scales", align_bytes=64)
-            nc.vector.quantize_mx(
-                out=codes[:].rearrange("p c n -> p (c n)").bitcast(FP8X4), scales=scales[:].rearrange("p c n -> p (c n)"), in_=gx[e][:]
+        def weave_slots(e):
+            nc.gpsimd.tensor_copy(
+                out=woven[e % 2][:].bitcast(U32).rearrange("p (c n u) -> p c n u", c=KC, u=2),
+                in_=gathered(e).bitcast(U32).rearrange("p (c u n) -> p c n u", c=KC, u=2),
             )
-            xcodes[e] = (codes, scales)
 
-        def quantise_shared_tokens(c):
-            nc.vector.quantize_mx(out=xs_codes[:, c, :].bitcast(FP8X4), scales=xs_scales[:, c, :], in_=xs_grp[c][:].rearrange("p n j -> p (n j)"))
-            xcodes[E] = (xs_codes, xs_scales)
+        def quantise_slots(e):
+            quantise(slot_mx[e % 2], slice(0, KC * C), woven[e % 2][:])
 
-        grouped = {}
-        wcodes = {}
+        def weave_all_tokens(c):
+            nc.vector.tensor_copy(
+                out=all_woven[c][:].rearrange("p (n u e) -> p n u e", u=2, e=2),
+                in_=x_pair[c][:].rearrange("p (u n e) -> p n u e", u=2, e=2),
+            )
 
-        def copy_weights(q):
-            e, which, c = chunks[q]
-            if which == "w2":
-                g = grp.tile([P, N * J], BF16, name="grp2", align_bytes=64)
-                dst = g[:].rearrange("p (n i j) -> p n j i", i=4, j=J)
-                src = raws[q][:].rearrange("p j (n i) -> p n j i", i=4)
-                count = N // 4
-            else:
-                g = grp.tile([P, H * J], BF16, name="grp", align_bytes=64)
-                dst = g[:].rearrange("p (t m j) -> p m j t", t=J, j=J)
-                src = raws[q][:].rearrange("p j (m t) -> p m j t", t=J)
-                count = P
-            share = VECTOR_SHARE[e][which, c] * count // 128
-            if share < count:
+        def quantise_all_tokens(c):
+            quantise(all_mx, slice(c * T, (c + 1) * T), all_woven[c][:])
+
+        def round_block(e, b):
+            dst = rounded[b][:].rearrange("p (t m j) -> p m j t", t=J, j=J)
+            src = raw_set[e][b][:].rearrange("p (j m t) -> p m j t", j=J, t=J)
+            share = (GATHERING_SHARE if e + 1 < E else LAST_ROUTED_SHARE if e < E else SHARED_SHARE)[b]
+            if share < P:
                 nc.scalar.copy(out=dst[:, share:], in_=src[:, share:])
             if share > 0:
                 nc.vector.tensor_copy(out=dst[:, :share], in_=src[:, :share])
-            grouped[q] = g
 
-        def quantise_weights(q):
-            e, which, c = chunks[q]
-            if which == "w2":
-                codes = code2p.tile([P, N], U32, name="w2_codes", align_bytes=64)
-                scales = code2p.tile([P, N], U8, name="w2_scales", align_bytes=64)
-            else:
-                codes = codep.tile([P, H], U32, name="w_codes", align_bytes=64)
-                scales = codep.tile([P, H], U8, name="w_scales", align_bytes=64)
-            nc.vector.quantize_mx(out=codes[:].bitcast(FP8X4), scales=scales[:], in_=grouped[q][:])
-            wcodes[e, which, c] = (codes, scales)
+        def quantise_block(b):
+            quantise(w_mx[b], slice(0, H), rounded[b][:])
 
-        def first_layer(e, which, g, pool):
-            bank = pool.tile([P, J, G], F32, name="bank_" + which)
-            xc, xsc = xcodes[e]
+        def round_w2(e, copy):
+            copy(out=rounded2[e][:].rearrange("p (n i j) -> p n j i", i=4, j=J), in_=raw2[e].rearrange("p (j n i) -> p n j i", j=J, i=4))
+
+        def quantise_w2(e):
+            quantise(w2_mx[e], slice(0, N), rounded2[e][:])
+
+        def first_layer(e, layer, g):
+            tokens, width = (all_mx, T) if e == E else (slot_mx[e % 2], C)
+            bank = banks[4 * layer + g]
             for t in range(J):
                 for c in range(KC):
-                    wc, wsc = wcodes[e, which, c]
-                    nc.tensor.matmul_mx(
-                        out=bank[:, t, :],
-                        lhsT=wc[:, t * P : (t + 1) * P].bitcast(FP8X4),
-                        lhsT_scale=wsc[:, t * P : (t + 1) * P],
-                        rhs=xc[:, c, g * G : (g + 1) * G].bitcast(FP8X4),
-                        rhs_scale=xsc[:, c, g * G : (g + 1) * G],
-                        start=(c == 0),
-                        stop=(c == KC - 1),
-                    )
-            return bank
+                    cols = slice(c * width + g * G, c * width + (g + 1) * G)
+                    matmul(bank[:, t * G : (t + 1) * G], w_mx[KC * layer + c], slice(t * P, (t + 1) * P), tokens, cols, c == 0, c == KC - 1)
 
-        relus = {}
-        hgrp = {}
-        hcodes = {}
+        def relu_tile(e, g):
+            if e + 1 < E:
+                room = raw_set[e + 1][0]
+            else:
+                room = raw_set[e][BLOCKS - 1] if g < 2 else raw2[E]
+            return room[:, (g % 2) * G * J : (g % 2 + 1) * G * J].rearrange("p (n t) -> p n t", t=J)
 
-        banks = {}
+        def relu(e, g):
+            nc.scalar.activation(out=relu_tile(e, g), in_=banks[g][:].rearrange("p (t n) -> p n t", t=J), func=RELU)
 
-        def gate_matmuls(e, g):
-            banks[e, "w1", g] = first_layer(e, "w1", g, psa)
-
-        def up_matmuls(e, g):
-            banks[e, "w3", g] = first_layer(e, "w3", g, psb)
-
-        def gate_half(e, g):
-            bank = banks[e, "w1", g]
-            r = hp.tile([P, G, J], F32, name="relu_a")
-            nc.scalar.activation(out=r[:], in_=bank[:].rearrange("p t n -> p n t"), func=RELU)
-            relus[e, g] = r
-
-        def up_half(e, g):
-            bank = banks[e, "w3", g]
-            if g % 2 == 0:
-                hgrp[e, g // 2] = hp.tile([P, 2 * G, J], BF16, name="h_grp", align_bytes=64)
-            h = hgrp[e, g // 2]
+        def gated(e, g):
             nc.vector.tensor_tensor(
-                out=h[:, (g % 2) * G : (g % 2 + 1) * G, :], in0=bank[:].rearrange("p t n -> p n t"), in1=relus[e, g][:], op=MULT
+                out=hidden[:, g * G * J : (g + 1) * G * J].rearrange("p (n t) -> p n t", t=J),
+                in0=banks[4 + g][:].rearrange("p (t n) -> p n t", t=J),
+                in1=relu_tile(e, g),
+                op=MULT,
             )
 
-        def quantise_hidden(e, pair, lo, hi):
-            if (e, pair) not in hcodes:
-                codes = hp.tile([P, 2 * G], U32, name="h_codes", align_bytes=64)
-                scales = hp.tile([P, 2 * G], U8, name="h_scales", align_bytes=64)
-                hcodes[e, pair] = (codes, scales)
-            codes, scales = hcodes[e, pair]
-            nc.vector.quantize_mx(
-                out=codes[:, lo:hi].bitcast(FP8X4), scales=scales[:, lo:hi], in_=hgrp[e, pair][:, lo:hi, :].rearrange("p n j -> p (n j)")
-            )
+        def quantise_hidden(e, lo, hi):
+            quantise(h_mx[e], slice(lo, hi), hidden[:, lo * J : hi * J])
 
-        ybank = {}
-
-        def second_layer(e, pair, lo, hi):
-            wc, wsc = wcodes[e, "w2", 0]
-            if (e, pair) not in ybank:
-                ybank[e, pair] = psy.tile([P, 2, 2 * G], F32, name="bank_y")
-            bank = ybank[e, pair]
-            codes, scales = hcodes[e, pair]
+        def second_layer(e, bank, lo, hi):
             for half in range(2):
-                nc.tensor.matmul_mx(
-                    out=bank[:, half, lo:hi],
-                    lhsT=wc[:, half * P : (half + 1) * P].bitcast(FP8X4),
-                    lhsT_scale=wsc[:, half * P : (half + 1) * P],
-                    rhs=codes[:, lo:hi].bitcast(FP8X4),
-                    rhs_scale=scales[:, lo:hi],
-                    start=True,
-                    stop=True,
-                )
+                first = half * C + lo % C
+                matmul(bank[:, first : first + hi - lo], w2_mx[e], slice(half * P, (half + 1) * P), h_mx[e], slice(lo, hi), True, True)
 
-        y_sb = [keep.tile([P, E * C], F32, name="y_sb0"), keep.tile([P, E * C], F32, name="y_sb1")]
+        y_banks = [banks[2], banks[3], banks[6], banks[7]]
 
-        def store_slots(e):
+        def store_slots(e, copy):
             for half in range(2):
-                nc.scalar.copy(out=y_sb[half][:, e * C : (e + 1) * C], in_=ybank[e, 0][:, half, :])
+                copy(out=y_sb[half][:, e * C : (e + 1) * C], in_=y_banks[e][:, half * C : (half + 1) * C])
 
-        picked = [keep.tile([P, 2, T], F32, name="picked0"), keep.tile([P, 2, T], F32, name="picked1")]
-        combined = keep.tile([P, 2, T], F32, name="combined")
-        result = keep.tile([P, 2, T], F32, name="result")
+        combined = rounded[BLOCKS - 1][:].bitcast(F32).rearrange("p (h n) -> p h n", h=2)
+        term = {(0, 0): first_term[:], (0, 1): rounded[0][:].bitcast(F32)[:, 0:T], (1, 0): rounded[1][:].bitcast(F32)[:, 0:T], (1, 1): combined[:, 1, :]}
 
         def pick(r, half):
-            nc.vector.tensor_tensor(out=picked[r][:, half, :], in0=y_sb[half][:].indirect(pos_t[r][:]), in1=gates[r][:, half, :], op=MULT)
+            nc.vector.tensor_tensor(out=term[r, half], in0=y_sb[half][:].indirect(pos_t[r][:]), in1=gates[r][:], op=MULT)
+
+        def combine(half):
+            nc.gpsimd.tensor_add(out=combined[:, half, :], in0=term[0, half], in1=term[1, half])
 
         def finish(pair):
-            cols = slice(pair * 2 * G, (pair + 1) * 2 * G)
-            nc.vector.tensor_add(out=result[:, :, cols], in0=ybank[E, pair][:], in1=combined[:, :, cols])
-            for half in range(2):
-                nc.sync.dma_start(out=out[half * P : (half + 1) * P, cols], in_=result[:, half, cols])
+            cols = slice(pair * C, (pair + 1) * C)
+            nc.vector.tensor_add(out=result[:, :, cols], in0=banks[pair][:].rearrange("p (h n) -> p h n", h=2), in1=combined[:, :, cols])
+            nc.sync.dma_start(out=out.rearrange("(h p) t -> p h t", p=P)[:, :, cols], in_=result[:, :, cols])
 
-        def shared_group(g):
-            up_half(E, g)
+        load_x(0, 0)
+        nc.sync.dma_start(offs_t[:], offs)
+        nc.sync.dma_start(out=gate_row[:], in_=gate[:, 0, :].rearrange("r (p m) -> p r m", m=J))
+        load_x(0, 1)
+        load_block(0, 0)
+        load_x(1, 0)
+        load_x(1, 1)
+        load_block(0, 1)
+        load_block(0, 2)
+        load_block(0, 3)
+        nc.sync.dma_start(pos_t[0][:], pos1)
+        nc.sync.dma_start(pos_t[1][:], pos2)
+        for e in range(1, RAW_SETS):
+            for b in range(BLOCKS):
+                load_block(e, b)
 
-        def shared_out(g):
-            lo, hi = (g % 2) * G, (g % 2 + 1) * G
-            quantise_hidden(E, g // 2, lo, hi)
-            second_layer(E, g // 2, lo, hi)
-            if g % 2 == 1:
-                finish(g // 2)
-
-        def combine():
-            nc.vector.tensor_add(out=combined[:], in0=picked[0][:], in1=picked[1][:])
-
-        later = {}
-
-        def at(step, rank, *call):
-            later.setdefault(step, []).append((rank, len(later.get(step, [])), call))
-
-        LQ, LR, LB, LH, LY = LAGS
-        nq = len(chunks)
-        for c in range(KC):
-            for u in range(2):
-                at(2 * c + u, -2, pair_tokens, c, u)
-                for e in range(E):
-                    at(2 * c + u + GATHER[e][0], GATHER[e][1], gather, e, c, u)
-        for e in range(E):
-            at(3 + GATHER[e][0] + (e > 0), GATHER[e][1], quantise_tokens, e)
-        for c in range(KC):
-            for part in range(XPARTS):
-                at(XSTEP[c], 7, group_shared_tokens, c, part)
-        for q in range(nq):
-            e, which, c = chunks[q]
-            groups = T // G if e == E else C // G
-            if q + LOOKAHEAD < nq:
-                at(q, -9, load, q + LOOKAHEAD)
-            at(q, 1, copy_weights, q)
-            at(q + LQ, 2, quantise_weights, q)
-            if c == 1:
-                base = q + LQ
-                if e < E:
-                    ready = 3 + GATHER[e][0] + (e > 0) + (GATHER[e][1] > 2.9)
-                    base = max(base, ready)
-                for g in range(groups):
-                    if which == "w1":
-                        at(base, 3, gate_matmuls, e, g) if e < E or g < 3 else at(base + LR, 4, gate_matmuls, e, g)
-                        at(base + LR, 4, gate_half, e, g)
-                    elif e < E:
-                        at(base, 3, up_matmuls, e, g)
-                        at(base + LB, 5, up_half, e, g)
-                if which == "w3" and e < E:
-                    at(base + LB + LH, RH, quantise_hidden, e, 0, 0, C)
-                    at(base + LB + LH, RH, second_layer, e, 0, 0, C)
-                    at(base + LB + LH + LY, RY, store_slots, e)
-        at(XSTEP[0] + 5, 6, quantise_shared_tokens, 0)
-        at(XSTEP[1] + 5, 6, quantise_shared_tokens, 1)
-        s0 = 5 * E
+        make_identity(nc, identity[:])
         for r in range(2):
-            for half in range(2):
-                at(s0 + PICK[2 * r + half], 6, pick, r, half)
-        at(s0 + PICK[4], 6, combine)
-        n = nq + LQ
-        for g in range(3):
-            at(n - 1, 3, up_matmuls, E, g)
-        at(n, 0, shared_group, 0)
-        at(n, 0, shared_group, 1)
-        at(n, 1, up_matmuls, E, 3)
-        at(n, 1, shared_out, 0)
-        at(n, 2, shared_group, 2)
-        at(n, 3, shared_out, 1)
-        at(n, 4, shared_group, 3)
-        at(n, 5, shared_out, 2)
-        at(n, 6, shared_out, 3)
-        for step in sorted(later):
-            for rank, order, call in sorted(later[step], key=lambda item: item[:2]):
-                call[0](*call[1:])
+            for m in range(J):
+                nc.tensor.transpose(banks[2 + r][:, m * P : (m + 1) * P], gate_row[:, r, m : m + 1].to_broadcast([P, P]), identity[:])
+            nc.scalar.copy(out=gates[r][:].rearrange("p (n m) -> p n m", m=J), in_=banks[2 + r][:].rearrange("p (m n) -> p n m", m=J))
 
+        for c, u in planes:
+            pair_tokens(c, u, nc.scalar.copy)
+            gather(0, c, u)
+            gather(1, c, u)
+        weave_slots(0)
+        quantise_slots(0)
+        weave_slots(1)
 
-XPARTS, XSTEP = 4, (11, 5)
-GATHER = [[0, 4.5], [1, 1.5], [4, 4.5], [9, 6]]
-LAGS = (1, 1, 1, 1, 1)
-RH, RY, RG = (2, 1, 6)
-PICK = (4, 2, 2, 3, 4)
+        for e in range(E):
+            for b in range(BLOCKS):
+                round_block(e, b)
+                if b == 0 and e > 0:
+                    for g in range(C // G):
+                        relu(e - 1, g)
+                quantise_block(b)
+                if b == 0 and e > 0:
+                    for g in range(C // G):
+                        gated(e - 1, g)
+                    quantise_hidden(e - 1, 0, C)
+                if b == 1 and e + 1 < E:
+                    quantise_slots(e + 1)
+                if b % KC == KC - 1:
+                    for g in range(C // G):
+                        first_layer(e, b // KC, g)
+            if e + 2 < E:
+                for c, u in planes:
+                    gather(e + 2, c, u)
+                weave_slots(e + 2)
+            if e + 1 == E:
+                for g in range(C // G):
+                    relu(e, g)
+                for other in range(2):
+                    round_w2(other, nc.vector.tensor_copy)
+                for other in range(2):
+                    quantise_w2(other)
+                for g in range(C // G):
+                    gated(e, g)
+            if e == 0:
+                for c in range(KC):
+                    weave_all_tokens(c)
+                    quantise_all_tokens(c)
+                for b in range(BLOCKS):
+                    load_block(E - 1, b)
+            if e == 1:
+                for other in range(E):
+                    load_w2(other)
+            if e == 2:
+                for b in range(BLOCKS):
+                    load_block(E, b)
+            if e == 3:
+                load_w2(E)
 
-VECTOR_SHARE = [{('w1', 0): 96, ('w1', 1): 0, ('w3', 0): 80, ('w3', 1): 0, ('w2', 0): 0}, {('w1', 0): 0, ('w1', 1): 0, ('w3', 0): 48, ('w3', 1): 0, ('w2', 0): 96}, {('w1', 0): 16, ('w1', 1): 0, ('w3', 0): 128, ('w3', 1): 0, ('w2', 0): 16}, {('w1', 0): 80, ('w1', 1): 96, ('w3', 0): 32, ('w3', 1): 80, ('w2', 0): 64}, {('w1', 0): 80, ('w1', 1): 48, ('w3', 0): 0, ('w3', 1): 32, ('w2', 0): 0}]
+        for e in range(2, E):
+            round_w2(e, nc.scalar.copy)
+        quantise_hidden(E - 1, 0, C)
+        for e in range(2, E):
+            quantise_w2(e)
+        for e in range(E):
+            second_layer(e, y_banks[e], 0, C)
+            store_slots(e, nc.vector.tensor_copy if e == E - 1 else nc.scalar.copy)
+
+        pick(0, 0)
+        for b in range(BLOCKS):
+            round_block(E, b)
+            quantise_block(b)
+            if b != 2:
+                pick(*{0: (0, 1), 1: (1, 0), 3: (1, 1)}[b])
+            if b % KC == KC - 1:
+                for g in range(T // G):
+                    first_layer(E, b // KC, g)
+        relu(E, 0)
+        relu(E, 1)
+        round_w2(E, nc.scalar.copy)
+        relu(E, 2)
+        relu(E, 3)
+        combine(0)
+        combine(1)
+        for pair in range(2):
+            gated(E, 2 * pair)
+            gated(E, 2 * pair + 1)
+            if pair == 0:
+                quantise_w2(E)
+            quantise_hidden(E, pair * C, (pair + 1) * C)
+            second_layer(E, banks[pair], pair * C, (pair + 1) * C)
+        for pair in range(2):
+            finish(pair)

@@ -23,9 +23,9 @@ G = 128
 BLOCKS = 2 * KC
 RAW_SETS = 3
 
-GATHERING_SHARE = (0, 0, 0, 96)
-LAST_ROUTED_SHARE = (64, 64, 64, 64)
-SHARED_SHARE = (0, 0, 0, 64)
+GATHERING_SHARE = (0, 0, 0, 48)
+LAST_ROUTED_SHARE = (0, 32, 32, 32)
+SHARED_SHARE = (0, 0, 0, 32)
 
 
 def tile_moe_shr_glu_relu_kernel(tc, xT, w1, w3, w2, gate, offs, pos1, pos2, out):
@@ -81,7 +81,6 @@ def tile_moe_shr_glu_relu_kernel(tc, xT, w1, w3, w2, gate, offs, pos1, pos2, out
         gates = [sbuf("gates%d" % r, [P, T], F32) for r in range(2)]
         identity = sbuf("identity", [P, P], F32)
         first_term = sbuf("first_term", [P, T], F32)
-        result = sbuf("result", [P, 2, T], F32)
 
         def load_x(c, u):
             src = xT[c * P * J : (c + 1) * P * J, :].rearrange("(p j) w -> p j w", j=J)
@@ -93,7 +92,9 @@ def tile_moe_shr_glu_relu_kernel(tc, xT, w1, w3, w2, gate, offs, pos1, pos2, out
             nc.sync.dma_start(out=raw_set[e][b][:], in_=w[e, c * P * J : (c + 1) * P * J, :].rearrange("(p j) w -> p (j w)", j=J))
 
         def load_w2(e):
-            nc.sync.dma_start(out=raw2[e], in_=w2[e].rearrange("(p j) w -> p (j w)", j=J))
+            rows = w2[e].rearrange("(u t v) n -> v u t n", t=J, v=2)
+            for v in range(2):
+                nc.sync.dma_start(out=raw2[e][v:P:2, :].rearrange("p (t n) -> p t n", t=J), in_=rows[v])
 
         def pair_plane(c, u):
             return x_pair[c][:, u * T * 2 : (u + 1) * T * 2]
@@ -128,19 +129,19 @@ def tile_moe_shr_glu_relu_kernel(tc, xT, w1, w3, w2, gate, offs, pos1, pos2, out
             quantise(all_mx, slice(c * T, (c + 1) * T), all_woven[c][:])
 
         def round_block(e, b):
-            dst = rounded[b][:].rearrange("p (t m j) -> p m j t", t=J, j=J)
-            src = raw_set[e][b][:].rearrange("p (j m t) -> p m j t", j=J, t=J)
+            dst = rounded[b][:].rearrange("p (t u v j) -> p t u j v", t=J, v=2, j=J)
+            src = raw_set[e][b][:].rearrange("p (j u t v) -> p t u j v", j=J, t=J, v=2)
             share = (GATHERING_SHARE if e + 1 < E else LAST_ROUTED_SHARE if e < E else SHARED_SHARE)[b]
-            if share < P:
-                nc.scalar.copy(out=dst[:, share:], in_=src[:, share:])
+            if share < P // 2:
+                nc.scalar.copy(out=dst[:, :, share:], in_=src[:, :, share:])
             if share > 0:
-                nc.vector.tensor_copy(out=dst[:, :share], in_=src[:, :share])
+                nc.vector.tensor_copy(out=dst[:, :, :share], in_=src[:, :, :share])
 
         def quantise_block(b):
             quantise(w_mx[b], slice(0, H), rounded[b][:])
 
         def round_w2(e, copy):
-            copy(out=rounded2[e][:].rearrange("p (n i j) -> p n j i", i=4, j=J), in_=raw2[e].rearrange("p (j n i) -> p n j i", j=J, i=4))
+            copy(out=rounded2[e][:].rearrange("p (n i j) -> p n j i", i=2, j=J), in_=raw2[e].rearrange("p (j n i) -> p n j i", j=J, i=2))
 
         def quantise_w2(e):
             quantise(w2_mx[e], slice(0, N), rounded2[e][:])
@@ -194,10 +195,11 @@ def tile_moe_shr_glu_relu_kernel(tc, xT, w1, w3, w2, gate, offs, pos1, pos2, out
         def combine(half):
             nc.gpsimd.tensor_add(out=combined[:, half, :], in0=term[0, half], in1=term[1, half])
 
-        def finish(pair):
-            cols = slice(pair * C, (pair + 1) * C)
-            nc.vector.tensor_add(out=result[:, :, cols], in0=banks[pair][:].rearrange("p (h n) -> p h n", h=2), in1=combined[:, :, cols])
-            nc.sync.dma_start(out=out.rearrange("(h p) t -> p h t", p=P)[:, :, cols], in_=result[:, :, cols])
+        def finish(bank, lo, hi):
+            first = {0: 2 * C, C: 0, C + G: C}[lo]
+            result = hidden[:].bitcast(F32)[:, first : first + 2 * (hi - lo)].rearrange("p (h n) -> p h n", h=2)
+            nc.vector.tensor_add(out=result, in0=bank[:].rearrange("p (h n) -> p h n", h=2)[:, :, lo % C : lo % C + hi - lo], in1=combined[:, :, lo:hi])
+            nc.sync.dma_start(out=out.rearrange("(h p) t -> p h t", p=P)[:, :, lo:hi], in_=result)
 
         load_x(0, 0)
         nc.sync.dma_start(offs_t[:], offs)
@@ -303,7 +305,11 @@ def tile_moe_shr_glu_relu_kernel(tc, xT, w1, w3, w2, gate, offs, pos1, pos2, out
             gated(E, 2 * pair + 1)
             if pair == 0:
                 quantise_w2(E)
-            quantise_hidden(E, pair * C, (pair + 1) * C)
-            second_layer(E, banks[pair], pair * C, (pair + 1) * C)
-        for pair in range(2):
-            finish(pair)
+                quantise_hidden(E, 0, C)
+                second_layer(E, banks[0], 0, C)
+        for g in range(2, 4):
+            quantise_hidden(E, g * G, (g + 1) * G)
+            second_layer(E, banks[g - 1], g * G, (g + 1) * G)
+        finish(banks[0], 0, C)
+        for g in range(2, 4):
+            finish(banks[g - 1], g * G, (g + 1) * G)

@@ -23,9 +23,9 @@ G = 128
 BLOCKS = 2 * KC
 RAW_SETS = 3
 
-GATHERING_SHARE = (0, 0, 0, 48)
+GATHERING_SHARE = (0, 0, 0, 32)
 LAST_ROUTED_SHARE = (0, 32, 32, 32)
-SHARED_SHARE = (0, 0, 0, 32)
+SHARED_SHARE = (0, 0, 0, 16)
 
 
 def tile_moe_shr_glu_relu_kernel(tc, xT, w1, w3, w2, gate, offs, pos1, pos2, out):
@@ -67,7 +67,8 @@ def tile_moe_shr_glu_relu_kernel(tc, xT, w1, w3, w2, gate, offs, pos1, pos2, out
         raw_set = [raw[0], raw[1], raw[2], raw[0], raw[2]]
         last_w2 = twice.tile([P, 2 * J * N], F32, name="last_w2", offset=0)
         y_sb = [twice.tile([P, E * C], F32, name="y_sb%d" % half, offset=half * E * C * 4) for half in range(2)]
-        raw2 = [raw[1][1][:, 0 : J * N], raw[1][1][:, J * N : 2 * J * N], last_w2[:, 0 : J * N], last_w2[:, J * N : 2 * J * N], raw[0][1][:, 0 : J * N]]
+        raw2 = [raw[1][1][:, 0 : J * N], raw[1][1][:, J * N : 2 * J * N], last_w2[:, 0 : J * N], last_w2[:, J * N : 2 * J * N], ]
+        raw2 = [r.rearrange("p (j n) -> p j n", j=J) for r in raw2] + [raw[0][1][:].rearrange("p (j n) -> p j n", j=J)[:, :, 0:N]]
         rounded2 = [sbuf("rounded2_%d" % e, [P, N * J], BF16) for e in range(E + 1)]
         w2_mx = [mx_tiles("second%d" % e, N) for e in range(E + 1)]
         woven = [sbuf("woven%d" % s, [P, KC * C * J], BF16) for s in range(2)]
@@ -80,7 +81,7 @@ def tile_moe_shr_glu_relu_kernel(tc, xT, w1, w3, w2, gate, offs, pos1, pos2, out
         gate_row = sbuf("gate_row", [P, 2, J], F32)
         gates = [sbuf("gates%d" % r, [P, T], F32) for r in range(2)]
         identity = sbuf("identity", [P, P], F32)
-        first_term = sbuf("first_term", [P, T], F32)
+        first_term = sbuf("first_term", [P, 2, T], F32)
 
         def load_x(c, u):
             src = xT[c * P * J : (c + 1) * P * J, :].rearrange("(p j) w -> p j w", j=J)
@@ -92,9 +93,7 @@ def tile_moe_shr_glu_relu_kernel(tc, xT, w1, w3, w2, gate, offs, pos1, pos2, out
             nc.sync.dma_start(out=raw_set[e][b][:], in_=w[e, c * P * J : (c + 1) * P * J, :].rearrange("(p j) w -> p (j w)", j=J))
 
         def load_w2(e):
-            rows = w2[e].rearrange("(u t v) n -> v u t n", t=J, v=2)
-            for v in range(2):
-                nc.sync.dma_start(out=raw2[e][v:P:2, :].rearrange("p (t n) -> p t n", t=J), in_=rows[v])
+            nc.sync.dma_start(out=raw2[e], in_=w2[e].rearrange("(p j) w -> p j w", j=J))
 
         def pair_plane(c, u):
             return x_pair[c][:, u * T * 2 : (u + 1) * T * 2]
@@ -111,9 +110,9 @@ def tile_moe_shr_glu_relu_kernel(tc, xT, w1, w3, w2, gate, offs, pos1, pos2, out
             nc.vector.tensor_copy(words[:, first : first + C], pair_plane(c, u).bitcast(U32).indirect(offs_t[:, e * C // 16 : (e + 1) * C // 16]))
 
         def weave_slots(e):
-            nc.gpsimd.tensor_copy(
-                out=woven[e % 2][:].bitcast(U32).rearrange("p (c n u) -> p c n u", c=KC, u=2),
-                in_=gathered(e).bitcast(U32).rearrange("p (c u n) -> p c n u", c=KC, u=2),
+            nc.vector.tensor_copy(
+                out=woven[e % 2][:].rearrange("p (c n u e) -> p c n u e", c=KC, u=2, e=2),
+                in_=gathered(e).rearrange("p (c u n e) -> p c n u e", c=KC, u=2, e=2),
             )
 
         def quantise_slots(e):
@@ -129,19 +128,19 @@ def tile_moe_shr_glu_relu_kernel(tc, xT, w1, w3, w2, gate, offs, pos1, pos2, out
             quantise(all_mx, slice(c * T, (c + 1) * T), all_woven[c][:])
 
         def round_block(e, b):
-            dst = rounded[b][:].rearrange("p (t u v j) -> p t u j v", t=J, v=2, j=J)
-            src = raw_set[e][b][:].rearrange("p (j u t v) -> p t u j v", j=J, t=J, v=2)
+            dst = rounded[b][:].rearrange("p (t u v j) -> p u v j t", t=J, v=2, j=J)
+            src = raw_set[e][b][:].rearrange("p (j u v t) -> p u v j t", j=J, t=J, v=2)
             share = (GATHERING_SHARE if e + 1 < E else LAST_ROUTED_SHARE if e < E else SHARED_SHARE)[b]
             if share < P // 2:
-                nc.scalar.copy(out=dst[:, :, share:], in_=src[:, :, share:])
+                nc.scalar.copy(out=dst[:, share:], in_=src[:, share:])
             if share > 0:
-                nc.vector.tensor_copy(out=dst[:, :, :share], in_=src[:, :, :share])
+                nc.vector.tensor_copy(out=dst[:, :share], in_=src[:, :share])
 
         def quantise_block(b):
             quantise(w_mx[b], slice(0, H), rounded[b][:])
 
         def round_w2(e, copy):
-            copy(out=rounded2[e][:].rearrange("p (n i j) -> p n j i", i=2, j=J), in_=raw2[e].rearrange("p (j n i) -> p n j i", j=J, i=2))
+            copy(out=rounded2[e][:].rearrange("p (n i j) -> p n j i", i=2, j=J), in_=raw2[e].rearrange("p j (n i) -> p n j i", i=2))
 
         def quantise_w2(e):
             quantise(w2_mx[e], slice(0, N), rounded2[e][:])
@@ -158,16 +157,16 @@ def tile_moe_shr_glu_relu_kernel(tc, xT, w1, w3, w2, gate, offs, pos1, pos2, out
             if e + 1 < E:
                 room = raw_set[e + 1][0]
             else:
-                room = raw_set[e][BLOCKS - 1] if g < 2 else raw2[E]
-            return room[:, (g % 2) * G * J : (g % 2 + 1) * G * J].rearrange("p (n t) -> p n t", t=J)
+                room = raw_set[e][BLOCKS - 1] if e < E else raw[0][1]
+            return room[:, g * G * J : (g + 1) * G * J].rearrange("p (n t i) -> p n t i", t=J, i=2)
 
         def relu(e, g):
-            nc.scalar.activation(out=relu_tile(e, g), in_=banks[g][:].rearrange("p (t n) -> p n t", t=J), func=RELU)
+            nc.scalar.activation(out=relu_tile(e, g), in_=banks[g][:].rearrange("p (t n i) -> p n t i", t=J, i=2), func=RELU)
 
         def gated(e, g):
             nc.vector.tensor_tensor(
-                out=hidden[:, g * G * J : (g + 1) * G * J].rearrange("p (n t) -> p n t", t=J),
-                in0=banks[4 + g][:].rearrange("p (t n) -> p n t", t=J),
+                out=hidden[:, g * G * J : (g + 1) * G * J].rearrange("p (n i t) -> p n t i", t=J, i=2),
+                in0=banks[4 + g][:].rearrange("p (t n i) -> p n t i", t=J, i=2),
                 in1=relu_tile(e, g),
                 op=MULT,
             )
@@ -182,18 +181,17 @@ def tile_moe_shr_glu_relu_kernel(tc, xT, w1, w3, w2, gate, offs, pos1, pos2, out
 
         y_banks = [banks[2], banks[3], banks[6], banks[7]]
 
-        def store_slots(e, copy):
-            for half in range(2):
-                copy(out=y_sb[half][:, e * C : (e + 1) * C], in_=y_banks[e][:, half * C : (half + 1) * C])
+        def store_slots(e, half, copy):
+            copy(out=y_sb[half][:, e * C : (e + 1) * C], in_=y_banks[e][:, half * C : (half + 1) * C])
 
         combined = rounded[BLOCKS - 1][:].bitcast(F32).rearrange("p (h n) -> p h n", h=2)
-        term = {(0, 0): first_term[:], (0, 1): rounded[0][:].bitcast(F32)[:, 0:T], (1, 0): rounded[1][:].bitcast(F32)[:, 0:T], (1, 1): combined[:, 1, :]}
+        term = {(0, 0): first_term[:, 0, :], (1, 0): first_term[:, 1, :], (0, 1): rounded[0][:].bitcast(F32)[:, 0:T], (1, 1): rounded[1][:].bitcast(F32)[:, 0:T]}
 
         def pick(r, half):
             nc.vector.tensor_tensor(out=term[r, half], in0=y_sb[half][:].indirect(pos_t[r][:]), in1=gates[r][:], op=MULT)
 
         def combine(half):
-            nc.gpsimd.tensor_add(out=combined[:, half, :], in0=term[0, half], in1=term[1, half])
+            nc.vector.tensor_add(out=combined[:, half, :], in0=term[0, half], in1=term[1, half])
 
         def finish(bank, lo, hi):
             first = {0: 2 * C, C: 0, C + G: C}[lo]
@@ -224,7 +222,7 @@ def tile_moe_shr_glu_relu_kernel(tc, xT, w1, w3, w2, gate, offs, pos1, pos2, out
             nc.scalar.copy(out=gates[r][:].rearrange("p (n m) -> p n m", m=J), in_=banks[2 + r][:].rearrange("p (m n) -> p n m", m=J))
 
         for c, u in planes:
-            pair_tokens(c, u, nc.scalar.copy)
+            pair_tokens(c, u, nc.vector.tensor_copy if (c, u) == (0, 0) else nc.scalar.copy)
             gather(0, c, u)
             gather(1, c, u)
         weave_slots(0)
@@ -282,22 +280,24 @@ def tile_moe_shr_glu_relu_kernel(tc, xT, w1, w3, w2, gate, offs, pos1, pos2, out
             quantise_w2(e)
         for e in range(E):
             second_layer(e, y_banks[e], 0, C)
-            store_slots(e, nc.vector.tensor_copy if e == E - 1 else nc.scalar.copy)
+        for experts in (range(1), range(1, E)):
+            for half in range(2):
+                for e in experts:
+                    store_slots(e, half, nc.vector.tensor_copy if (e, half) == (E - 1, 0) else nc.scalar.copy)
 
         pick(0, 0)
+        pick(1, 0)
         for b in range(BLOCKS):
             round_block(E, b)
             quantise_block(b)
-            if b != 2:
-                pick(*{0: (0, 1), 1: (1, 0), 3: (1, 1)}[b])
+            if b < 2:
+                pick(b, 1)
             if b % KC == KC - 1:
                 for g in range(T // G):
                     first_layer(E, b // KC, g)
-        relu(E, 0)
-        relu(E, 1)
         round_w2(E, nc.scalar.copy)
-        relu(E, 2)
-        relu(E, 3)
+        for g in range(T // G):
+            relu(E, g)
         combine(0)
         combine(1)
         for pair in range(2):

@@ -10,6 +10,7 @@ FLOPS = 2 * (E * C + T) * (2 * K * H + H * N)
 F32 = mybir.dt.float32
 BF16 = mybir.dt.bfloat16
 U32 = mybir.dt.uint32
+I32 = mybir.dt.int32
 U16 = mybir.dt.uint16
 U8 = mybir.dt.uint8
 FP8X4 = mybir.dt.float8_e4m3fn_x4
@@ -23,9 +24,9 @@ G = 128
 BLOCKS = 2 * KC
 RAW_SETS = 3
 
-GATHERING_SHARE = (0, 0, 0, 32)
-LAST_ROUTED_SHARE = (0, 32, 32, 32)
-SHARED_SHARE = (0, 0, 0, 16)
+GATHERING_SHARE = (0, 24, 0, 32)
+LAST_ROUTED_SHARE = (16, 32, 16, 40)
+SHARED_SHARE = (0, 0, 24, 24)
 
 
 def tile_moe_shr_glu_relu_kernel(tc, xT, w1, w3, w2, gate, offs, pos1, pos2, out):
@@ -68,7 +69,7 @@ def tile_moe_shr_glu_relu_kernel(tc, xT, w1, w3, w2, gate, offs, pos1, pos2, out
         last_w2 = twice.tile([P, 2 * J * N], F32, name="last_w2", offset=0)
         y_sb = [twice.tile([P, E * C], F32, name="y_sb%d" % half, offset=half * E * C * 4) for half in range(2)]
         raw2 = [raw[1][1][:, 0 : J * N], raw[1][1][:, J * N : 2 * J * N], last_w2[:, 0 : J * N], last_w2[:, J * N : 2 * J * N], ]
-        raw2 = [r.rearrange("p (j n) -> p j n", j=J) for r in raw2] + [raw[0][1][:].rearrange("p (j n) -> p j n", j=J)[:, :, 0:N]]
+        raw2 = [r.rearrange("p (j n) -> p j n", j=J) for r in raw2 + [raw[0][1][:, 0 : J * N]]]
         rounded2 = [sbuf("rounded2_%d" % e, [P, N * J], BF16) for e in range(E + 1)]
         w2_mx = [mx_tiles("second%d" % e, N) for e in range(E + 1)]
         woven = [sbuf("woven%d" % s, [P, KC * C * J], BF16) for s in range(2)]
@@ -109,10 +110,10 @@ def tile_moe_shr_glu_relu_kernel(tc, xT, w1, w3, w2, gate, offs, pos1, pos2, out
             first = (2 * c + u) * C
             nc.vector.tensor_copy(words[:, first : first + C], pair_plane(c, u).bitcast(U32).indirect(offs_t[:, e * C // 16 : (e + 1) * C // 16]))
 
-        def weave_slots(e):
-            nc.vector.tensor_copy(
-                out=woven[e % 2][:].rearrange("p (c n u e) -> p c n u e", c=KC, u=2, e=2),
-                in_=gathered(e).rearrange("p (c u n e) -> p c n u e", c=KC, u=2, e=2),
+        def weave_slots(e, copy):
+            copy(
+                out=woven[e % 2][:].bitcast(I32).rearrange("p (c n u) -> p c n u", c=KC, u=2),
+                in_=gathered(e).bitcast(I32).rearrange("p (c u n) -> p c n u", c=KC, u=2),
             )
 
         def quantise_slots(e):
@@ -157,7 +158,7 @@ def tile_moe_shr_glu_relu_kernel(tc, xT, w1, w3, w2, gate, offs, pos1, pos2, out
             if e + 1 < E:
                 room = raw_set[e + 1][0]
             else:
-                room = raw_set[e][BLOCKS - 1] if e < E else raw[0][1]
+                room = raw_set[e][BLOCKS - 1]
             return room[:, g * G * J : (g + 1) * G * J].rearrange("p (n t i) -> p n t i", t=J, i=2)
 
         def relu(e, g):
@@ -185,13 +186,13 @@ def tile_moe_shr_glu_relu_kernel(tc, xT, w1, w3, w2, gate, offs, pos1, pos2, out
             copy(out=y_sb[half][:, e * C : (e + 1) * C], in_=y_banks[e][:, half * C : (half + 1) * C])
 
         combined = rounded[BLOCKS - 1][:].bitcast(F32).rearrange("p (h n) -> p h n", h=2)
-        term = {(0, 0): first_term[:, 0, :], (1, 0): first_term[:, 1, :], (0, 1): rounded[0][:].bitcast(F32)[:, 0:T], (1, 1): rounded[1][:].bitcast(F32)[:, 0:T]}
+        term = {(0, 0): first_term[:, 0, :], (1, 0): first_term[:, 1, :], (0, 1): rounded[0][:].bitcast(F32)[:, 0:T], (1, 1): combined[:, 1, :]}
 
         def pick(r, half):
             nc.vector.tensor_tensor(out=term[r, half], in0=y_sb[half][:].indirect(pos_t[r][:]), in1=gates[r][:], op=MULT)
 
         def combine(half):
-            nc.vector.tensor_add(out=combined[:, half, :], in0=term[0, half], in1=term[1, half])
+            nc.gpsimd.tensor_add(out=combined[:, half, :], in0=term[0, half], in1=term[1, half])
 
         def finish(bank, lo, hi):
             first = {0: 2 * C, C: 0, C + G: C}[lo]
@@ -203,31 +204,29 @@ def tile_moe_shr_glu_relu_kernel(tc, xT, w1, w3, w2, gate, offs, pos1, pos2, out
         nc.sync.dma_start(offs_t[:], offs)
         nc.sync.dma_start(out=gate_row[:], in_=gate[:, 0, :].rearrange("r (p m) -> p r m", m=J))
         load_x(0, 1)
-        load_block(0, 0)
         load_x(1, 0)
         load_x(1, 1)
+        load_block(0, 0)
         load_block(0, 1)
         load_block(0, 2)
         load_block(0, 3)
-        nc.sync.dma_start(pos_t[0][:], pos1)
-        nc.sync.dma_start(pos_t[1][:], pos2)
         for e in range(1, RAW_SETS):
             for b in range(BLOCKS):
                 load_block(e, b)
 
+        for c, u in planes:
+            pair_tokens(c, u, nc.vector.tensor_copy if c == 0 else nc.scalar.copy)
+            gather(0, c, u)
+            gather(1, c, u)
         make_identity(nc, identity[:])
         for r in range(2):
             for m in range(J):
                 nc.tensor.transpose(banks[2 + r][:, m * P : (m + 1) * P], gate_row[:, r, m : m + 1].to_broadcast([P, P]), identity[:])
             nc.scalar.copy(out=gates[r][:].rearrange("p (n m) -> p n m", m=J), in_=banks[2 + r][:].rearrange("p (m n) -> p n m", m=J))
 
-        for c, u in planes:
-            pair_tokens(c, u, nc.vector.tensor_copy if (c, u) == (0, 0) else nc.scalar.copy)
-            gather(0, c, u)
-            gather(1, c, u)
-        weave_slots(0)
+        weave_slots(0, nc.vector.tensor_copy)
         quantise_slots(0)
-        weave_slots(1)
+        weave_slots(1, nc.vector.tensor_copy)
 
         for e in range(E):
             for b in range(BLOCKS):
@@ -248,7 +247,7 @@ def tile_moe_shr_glu_relu_kernel(tc, xT, w1, w3, w2, gate, offs, pos1, pos2, out
             if e + 2 < E:
                 for c, u in planes:
                     gather(e + 2, c, u)
-                weave_slots(e + 2)
+                weave_slots(e + 2, nc.gpsimd.tensor_copy)
             if e + 1 == E:
                 for g in range(C // G):
                     relu(e, g)
@@ -267,6 +266,8 @@ def tile_moe_shr_glu_relu_kernel(tc, xT, w1, w3, w2, gate, offs, pos1, pos2, out
             if e == 1:
                 for other in range(E):
                     load_w2(other)
+                nc.sync.dma_start(pos_t[0][:], pos1)
+                nc.sync.dma_start(pos_t[1][:], pos2)
             if e == 2:
                 for b in range(BLOCKS):
                     load_block(E, b)
@@ -290,14 +291,14 @@ def tile_moe_shr_glu_relu_kernel(tc, xT, w1, w3, w2, gate, offs, pos1, pos2, out
         for b in range(BLOCKS):
             round_block(E, b)
             quantise_block(b)
-            if b < 2:
-                pick(b, 1)
+            if b in (0, BLOCKS - 1):
+                pick(b // (BLOCKS - 1), 1)
             if b % KC == KC - 1:
                 for g in range(T // G):
                     first_layer(E, b // KC, g)
-        round_w2(E, nc.scalar.copy)
         for g in range(T // G):
             relu(E, g)
+        round_w2(E, nc.scalar.copy)
         combine(0)
         combine(1)
         for pair in range(2):

@@ -23,10 +23,11 @@ KC = K // (P * J)
 G = 128
 BLOCKS = 2 * KC
 RAW_SETS = 3
+WINDOW = 704
 
-GATHERING_SHARE = (0, 24, 0, 32)
-LAST_ROUTED_SHARE = (16, 32, 16, 40)
-SHARED_SHARE = (0, 0, 24, 24)
+GATHERING_SHARE = (0, 48, 0, 0)
+LAST_ROUTED_SHARE = (0, 32, 16, 32)
+SHARED_SHARE = (0, 0, 0, 0)
 
 
 def tile_moe_shr_glu_relu_kernel(tc, xT, w1, w3, w2, gate, offs, pos1, pos2, out):
@@ -59,30 +60,33 @@ def tile_moe_shr_glu_relu_kernel(tc, xT, w1, w3, w2, gate, offs, pos1, pos2, out
         offs_t = keep.tile([P, E * C // 16], U16, name="offs_t")
         pos_t = [keep.tile([P, T // 16], U16, name="pos1_t"), keep.tile([P, T // 16], U16, name="pos2_t")]
         banks = [psum.tile([P, 512], F32, name="bank%d" % b) for b in range(8)]
-        planes = [(c, u) for c in range(KC) for u in range(2)]
+        planes = [(c, u) for c in reversed(range(KC)) for u in reversed(range(2))]
         x_raw = dict([(cu, sbuf("x_raw%d%d" % cu, [P, 2, T], F32)) for cu in planes])
-        x_pair = [sbuf("x_pair%d" % c, [P, 2 * T * 2], BF16) for c in range(KC)]
+        x_pair = sbuf("x_pair", [P, (3 * T + WINDOW) * 2], BF16)
         raw = [[sbuf("raw%d%d" % (s, b), [P, J * H], F32) for b in range(BLOCKS)] for s in range(RAW_SETS)]
-        rounded = [sbuf("rounded%d" % b, [P, H * J], BF16) for b in range(BLOCKS)]
-        w_mx = [mx_tiles("w%d" % b, H) for b in range(BLOCKS)]
+        work = sbuf("work", [P, (1 + BLOCKS) * H * J], BF16)
+        rounded_matrix = [work[:, (1 + KC * layer) * H * J : (1 + KC * layer + KC) * H * J] for layer in range(2)]
+        rounded = [rounded_matrix[b // KC][:, (b % KC) * H * J : (b % KC + 1) * H * J] for b in range(BLOCKS)]
+        w_mx = [mx_tiles("w%d" % layer, KC * H) for layer in range(2)]
         raw_set = [raw[0], raw[1], raw[2], raw[0], raw[2]]
         last_w2 = twice.tile([P, 2 * J * N], F32, name="last_w2", offset=0)
         y_sb = [twice.tile([P, E * C], F32, name="y_sb%d" % half, offset=half * E * C * 4) for half in range(2)]
         raw2 = [raw[1][1][:, 0 : J * N], raw[1][1][:, J * N : 2 * J * N], last_w2[:, 0 : J * N], last_w2[:, J * N : 2 * J * N], ]
         raw2 = [r.rearrange("p (j n) -> p j n", j=J) for r in raw2 + [raw[0][1][:, 0 : J * N]]]
-        rounded2 = [sbuf("rounded2_%d" % e, [P, N * J], BF16) for e in range(E + 1)]
-        w2_mx = [mx_tiles("second%d" % e, N) for e in range(E + 1)]
-        woven = [sbuf("woven%d" % s, [P, KC * C * J], BF16) for s in range(2)]
-        first_words = [sbuf("first_words%d" % e, [P, KC * C * J], BF16) for e in range(2)]
-        slot_mx = [(sbuf("slot_codes%d" % s, [P, KC * C], U32), w_mx[1][1][4 * (s + 1) : P, :]) for s in range(2)]
-        all_woven = [sbuf("all_woven%d" % c, [P, T * J], BF16) for c in range(KC)]
+        rounded2 = sbuf("rounded2", [P, (E + 1) * N * J], BF16)
+        w2_mx = mx_tiles("second", (E + 1) * N)
+        woven = sbuf("woven", [P, 2 * KC * C * J], BF16)
+        first_words = sbuf("first_words", [P, 2 * KC * C * J], BF16)
+        first_slots_mx = mx_tiles("first_slots", 2 * KC * C)
+        slot_mx = [(first_slots_mx[0][:, e * KC * C : (e + 1) * KC * C], first_slots_mx[1][:, e * KC * C : (e + 1) * KC * C]) for e in range(2)]
+        slot_mx = slot_mx + [(slot_mx[s][0], w_mx[0][1][4 * (s + 1) : P, H : H + KC * C]) for s in range(2)]
+        all_woven = sbuf("all_woven", [P, KC * T * J], BF16)
         all_mx = mx_tiles("all", KC * T)
         hidden = sbuf("hidden", [P, T * J], BF16)
         h_mx = [mx_tiles("h%d" % e, T if e == E else C) for e in range(E + 1)]
         gate_row = sbuf("gate_row", [P, 2, J], F32)
         gates = [sbuf("gates%d" % r, [P, T], F32) for r in range(2)]
         identity = sbuf("identity", [P, P], F32)
-        first_term = sbuf("first_term", [P, 2, T], F32)
 
         def load_x(c, u):
             src = xT[c * P * J : (c + 1) * P * J, :].rearrange("(p j) w -> p j w", j=J)
@@ -96,40 +100,45 @@ def tile_moe_shr_glu_relu_kernel(tc, xT, w1, w3, w2, gate, offs, pos1, pos2, out
         def load_w2(e):
             nc.sync.dma_start(out=raw2[e], in_=w2[e].rearrange("(p j) w -> p j w", j=J))
 
-        def pair_plane(c, u):
-            return x_pair[c][:, u * T * 2 : (u + 1) * T * 2]
+        def pair_plane(c, u, width):
+            first = (2 * c + u) * T
+            return x_pair[:, first * 2 : (first + width) * 2]
 
         def pair_tokens(c, u, copy):
-            copy(out=pair_plane(c, u).rearrange("p (n i e) -> p n e i", i=4, e=2), in_=x_raw[c, u][:].rearrange("p e (n i) -> p n e i", i=4))
+            copy(out=pair_plane(c, u, T).rearrange("p (n i e) -> p n e i", i=4, e=2), in_=x_raw[c, u][:].rearrange("p e (n i) -> p n e i", i=4))
 
-        def gathered(e):
-            return first_words[e][:] if e < 2 else rounded[BLOCKS - 1][:]
+        def gather(e, experts, c, u, words):
+            count = experts * C
+            first = (2 * c + u) * count
+            window = pair_plane(c, u, WINDOW if experts == 2 else T).bitcast(U32)
+            nc.vector.tensor_copy(words.bitcast(U32)[:, first : first + count], window.indirect(offs_t[:, e * C // 16 : (e * C + count) // 16]))
 
-        def gather(e, c, u):
-            words = gathered(e).bitcast(U32)
-            first = (2 * c + u) * C
-            nc.vector.tensor_copy(words[:, first : first + C], pair_plane(c, u).bitcast(U32).indirect(offs_t[:, e * C // 16 : (e + 1) * C // 16]))
+        def weave_first_slots():
+            nc.vector.tensor_copy(
+                out=woven[:].bitcast(I32).rearrange("p (e c n u) -> p e c n u", e=2, c=KC, u=2),
+                in_=first_words[:].bitcast(I32).rearrange("p (c u e n) -> p e c n u", c=KC, u=2, e=2),
+            )
 
-        def weave_slots(e, copy):
-            copy(
-                out=woven[e % 2][:].bitcast(I32).rearrange("p (c n u) -> p c n u", c=KC, u=2),
-                in_=gathered(e).bitcast(I32).rearrange("p (c u n) -> p c n u", c=KC, u=2),
+        def woven_slots(e):
+            return woven[:, (e % 2) * KC * C * J : (e % 2 + 1) * KC * C * J]
+
+        def weave_slots(e):
+            nc.gpsimd.tensor_copy(
+                out=woven_slots(e).bitcast(I32).rearrange("p (c n u) -> p c n u", c=KC, u=2),
+                in_=rounded[BLOCKS - 1].bitcast(I32).rearrange("p (c u n) -> p c n u", c=KC, u=2),
             )
 
         def quantise_slots(e):
-            quantise(slot_mx[e % 2], slice(0, KC * C), woven[e % 2][:])
+            quantise(slot_mx[e], slice(0, KC * C), woven_slots(e))
 
-        def weave_all_tokens(c):
+        def weave_all_tokens():
             nc.vector.tensor_copy(
-                out=all_woven[c][:].rearrange("p (n u e) -> p n u e", u=2, e=2),
-                in_=x_pair[c][:].rearrange("p (u n e) -> p n u e", u=2, e=2),
+                out=all_woven[:].bitcast(I32).rearrange("p (c n u) -> p c n u", c=KC, u=2),
+                in_=x_pair[:, 0 : 4 * T * 2].bitcast(I32).rearrange("p (c u n) -> p c n u", c=KC, u=2),
             )
 
-        def quantise_all_tokens(c):
-            quantise(all_mx, slice(c * T, (c + 1) * T), all_woven[c][:])
-
         def round_block(e, b):
-            dst = rounded[b][:].rearrange("p (t u v j) -> p u v j t", t=J, v=2, j=J)
+            dst = rounded[b].rearrange("p (t u v j) -> p u v j t", t=J, v=2, j=J)
             src = raw_set[e][b][:].rearrange("p (j u v t) -> p u v j t", j=J, t=J, v=2)
             share = (GATHERING_SHARE if e + 1 < E else LAST_ROUTED_SHARE if e < E else SHARED_SHARE)[b]
             if share < P // 2:
@@ -138,21 +147,29 @@ def tile_moe_shr_glu_relu_kernel(tc, xT, w1, w3, w2, gate, offs, pos1, pos2, out
                 nc.vector.tensor_copy(out=dst[:, :share], in_=src[:, :share])
 
         def quantise_block(b):
-            quantise(w_mx[b], slice(0, H), rounded[b][:])
+            quantise(w_mx[b // KC], slice((b % KC) * H, (b % KC + 1) * H), rounded[b])
 
-        def round_w2(e, copy):
-            copy(out=rounded2[e][:].rearrange("p (n i j) -> p n j i", i=2, j=J), in_=raw2[e].rearrange("p j (n i) -> p n j i", i=2))
+        def quantise_matrix(layer):
+            quantise(w_mx[layer], slice(0, KC * H), rounded_matrix[layer])
 
-        def quantise_w2(e):
-            quantise(w2_mx[e], slice(0, N), rounded2[e][:])
+        def round_w2(e, share):
+            dst = rounded2[:, e * N * J : (e + 1) * N * J].rearrange("p (n i j) -> p n j i", i=2, j=J)
+            src = raw2[e].rearrange("p j (n i) -> p n j i", i=2)
+            if share < N // 2:
+                nc.scalar.copy(out=dst[:, share:], in_=src[:, share:])
+            if share > 0:
+                nc.vector.tensor_copy(out=dst[:, :share], in_=src[:, :share])
+
+        def quantise_w2(e, count):
+            quantise(w2_mx, slice(e * N, (e + count) * N), rounded2[:, e * N * J : (e + count) * N * J])
 
         def first_layer(e, layer, g):
-            tokens, width = (all_mx, T) if e == E else (slot_mx[e % 2], C)
+            tokens, width = (all_mx, T) if e == E else (slot_mx[e], C)
             bank = banks[4 * layer + g]
             for t in range(J):
                 for c in range(KC):
                     cols = slice(c * width + g * G, c * width + (g + 1) * G)
-                    matmul(bank[:, t * G : (t + 1) * G], w_mx[KC * layer + c], slice(t * P, (t + 1) * P), tokens, cols, c == 0, c == KC - 1)
+                    matmul(bank[:, t * G : (t + 1) * G], w_mx[layer], slice(c * H + t * P, c * H + (t + 1) * P), tokens, cols, c == 0, c == KC - 1)
 
         def relu_tile(e, g):
             if e + 1 < E:
@@ -175,37 +192,37 @@ def tile_moe_shr_glu_relu_kernel(tc, xT, w1, w3, w2, gate, offs, pos1, pos2, out
         def quantise_hidden(e, lo, hi):
             quantise(h_mx[e], slice(lo, hi), hidden[:, lo * J : hi * J])
 
-        def second_layer(e, bank, lo, hi):
+        def second_layer(e, sums, lo, hi):
             for half in range(2):
-                first = half * C + lo % C
-                matmul(bank[:, first : first + hi - lo], w2_mx[e], slice(half * P, (half + 1) * P), h_mx[e], slice(lo, hi), True, True)
+                matmul(sums[half], w2_mx, slice(e * N + half * P, e * N + (half + 1) * P), h_mx[e], slice(lo, hi), True, True)
 
-        y_banks = [banks[2], banks[3], banks[6], banks[7]]
+
+        def shared_sums(bank, width):
+            return [bank[:, half * width : (half + 1) * width] for half in range(2)]
 
         def store_slots(e, half, copy):
-            copy(out=y_sb[half][:, e * C : (e + 1) * C], in_=y_banks[e][:, half * C : (half + 1) * C])
+            copy(out=y_sb[half][:, e * C : (e + 1) * C], in_=banks[2 * e + half][:, 0:C])
 
-        combined = rounded[BLOCKS - 1][:].bitcast(F32).rearrange("p (h n) -> p h n", h=2)
-        term = {(0, 0): first_term[:, 0, :], (1, 0): first_term[:, 1, :], (0, 1): rounded[0][:].bitcast(F32)[:, 0:T], (1, 1): combined[:, 1, :]}
+        combined = rounded[BLOCKS - 1].bitcast(F32).rearrange("p (h n) -> p h n", h=2)
+        term = [work[:, 0 : 4 * H * J].bitcast(F32).rearrange("p (h n) -> p h n", h=2)[:, :, r * T : (r + 1) * T] for r in range(2)]
 
         def pick(r, half):
-            nc.vector.tensor_tensor(out=term[r, half], in0=y_sb[half][:].indirect(pos_t[r][:]), in1=gates[r][:], op=MULT)
+            nc.vector.tensor_tensor(out=term[r][:, half, :], in0=y_sb[half][:].indirect(pos_t[r][:]), in1=gates[r][:], op=MULT)
 
-        def combine(half):
-            nc.gpsimd.tensor_add(out=combined[:, half, :], in0=term[0, half], in1=term[1, half])
+        def combine():
+            nc.vector.tensor_add(out=combined, in0=term[0], in1=term[1])
 
         def finish(bank, lo, hi):
             first = {0: 2 * C, C: 0, C + G: C}[lo]
             result = hidden[:].bitcast(F32)[:, first : first + 2 * (hi - lo)].rearrange("p (h n) -> p h n", h=2)
-            nc.vector.tensor_add(out=result, in0=bank[:].rearrange("p (h n) -> p h n", h=2)[:, :, lo % C : lo % C + hi - lo], in1=combined[:, :, lo:hi])
+            nc.vector.tensor_add(out=result, in0=bank[:, 0 : 2 * (hi - lo)].rearrange("p (h n) -> p h n", h=2), in1=combined[:, :, lo:hi])
             nc.sync.dma_start(out=out.rearrange("(h p) t -> p h t", p=P)[:, :, lo:hi], in_=result)
 
-        load_x(0, 0)
+        load_x(*planes[0])
         nc.sync.dma_start(offs_t[:], offs)
         nc.sync.dma_start(out=gate_row[:], in_=gate[:, 0, :].rearrange("r (p m) -> p r m", m=J))
-        load_x(0, 1)
-        load_x(1, 0)
-        load_x(1, 1)
+        for c, u in planes[1:]:
+            load_x(c, u)
         load_block(0, 0)
         load_block(0, 1)
         load_block(0, 2)
@@ -214,19 +231,20 @@ def tile_moe_shr_glu_relu_kernel(tc, xT, w1, w3, w2, gate, offs, pos1, pos2, out
             for b in range(BLOCKS):
                 load_block(e, b)
 
+        nc.gpsimd.memset(x_pair[:, 4 * T * 2 :], 0.0)
         for c, u in planes:
-            pair_tokens(c, u, nc.vector.tensor_copy if c == 0 else nc.scalar.copy)
-            gather(0, c, u)
-            gather(1, c, u)
+            pair_tokens(c, u, nc.vector.tensor_copy if c == KC - 1 else nc.scalar.copy)
+            gather(0, 2, c, u, first_words[:])
         make_identity(nc, identity[:])
         for r in range(2):
             for m in range(J):
                 nc.tensor.transpose(banks[2 + r][:, m * P : (m + 1) * P], gate_row[:, r, m : m + 1].to_broadcast([P, P]), identity[:])
             nc.scalar.copy(out=gates[r][:].rearrange("p (n m) -> p n m", m=J), in_=banks[2 + r][:].rearrange("p (m n) -> p n m", m=J))
 
-        weave_slots(0, nc.vector.tensor_copy)
-        quantise_slots(0)
-        weave_slots(1, nc.vector.tensor_copy)
+        weave_first_slots()
+        weave_all_tokens()
+        quantise(first_slots_mx, slice(0, 2 * KC * C), woven[:])
+        quantise(all_mx, slice(0, KC * T), all_woven[:])
 
         for e in range(E):
             for b in range(BLOCKS):
@@ -234,33 +252,31 @@ def tile_moe_shr_glu_relu_kernel(tc, xT, w1, w3, w2, gate, offs, pos1, pos2, out
                 if b == 0 and e > 0:
                     for g in range(C // G):
                         relu(e - 1, g)
-                quantise_block(b)
-                if b == 0 and e > 0:
                     for g in range(C // G):
                         gated(e - 1, g)
+                if b == 1 and e > 0:
                     quantise_hidden(e - 1, 0, C)
-                if b == 1 and e + 1 < E:
+                if e + 1 == E:
+                    quantise_block(b)
+                elif b % KC == KC - 1:
+                    quantise_matrix(b // KC)
+                if b == 1 and 2 <= e + 1 < E:
                     quantise_slots(e + 1)
                 if b % KC == KC - 1:
                     for g in range(C // G):
                         first_layer(e, b // KC, g)
             if e + 2 < E:
                 for c, u in planes:
-                    gather(e + 2, c, u)
-                weave_slots(e + 2, nc.gpsimd.tensor_copy)
+                    gather(e + 2, 1, c, u, rounded[BLOCKS - 1])
+                weave_slots(e + 2)
             if e + 1 == E:
                 for g in range(C // G):
                     relu(e, g)
-                for other in range(2):
-                    round_w2(other, nc.vector.tensor_copy)
-                for other in range(2):
-                    quantise_w2(other)
+                round_w2(0, N // 2)
+                quantise_w2(0, 1)
                 for g in range(C // G):
                     gated(e, g)
             if e == 0:
-                for c in range(KC):
-                    weave_all_tokens(c)
-                    quantise_all_tokens(c)
                 for b in range(BLOCKS):
                     load_block(E - 1, b)
             if e == 1:
@@ -274,43 +290,44 @@ def tile_moe_shr_glu_relu_kernel(tc, xT, w1, w3, w2, gate, offs, pos1, pos2, out
             if e == 3:
                 load_w2(E)
 
-        for e in range(2, E):
-            round_w2(e, nc.scalar.copy)
-        quantise_hidden(E - 1, 0, C)
-        for e in range(2, E):
-            quantise_w2(e)
+        for e in range(1, E):
+            round_w2(e, 0)
+            quantise_w2(e, 1)
+            if e == 1:
+                quantise_hidden(E - 1, 0, C)
         for e in range(E):
-            second_layer(e, y_banks[e], 0, C)
-        for experts in (range(1), range(1, E)):
-            for half in range(2):
-                for e in experts:
-                    store_slots(e, half, nc.vector.tensor_copy if (e, half) == (E - 1, 0) else nc.scalar.copy)
+            second_layer(e, [banks[2 * e + half][:, 0:C] for half in range(2)], 0, C)
+        for half in range(2):
+            for e in range(E - 1 - half):
+                store_slots(e, half, nc.scalar.copy)
+        for e, half in ((E - 2, 1), (E - 1, 0), (E - 1, 1)):
+            store_slots(e, half, nc.vector.tensor_copy)
 
         pick(0, 0)
         pick(1, 0)
         for b in range(BLOCKS):
             round_block(E, b)
             quantise_block(b)
-            if b in (0, BLOCKS - 1):
-                pick(b // (BLOCKS - 1), 1)
+            if b == 1:
+                pick(0, 1)
+                pick(1, 1)
             if b % KC == KC - 1:
                 for g in range(T // G):
                     first_layer(E, b // KC, g)
         for g in range(T // G):
             relu(E, g)
-        round_w2(E, nc.scalar.copy)
-        combine(0)
-        combine(1)
+        round_w2(E, 0)
+        combine()
         for pair in range(2):
             gated(E, 2 * pair)
             gated(E, 2 * pair + 1)
             if pair == 0:
-                quantise_w2(E)
+                quantise_w2(E, 1)
                 quantise_hidden(E, 0, C)
-                second_layer(E, banks[0], 0, C)
+                second_layer(E, shared_sums(banks[0], C), 0, C)
         for g in range(2, 4):
             quantise_hidden(E, g * G, (g + 1) * G)
-            second_layer(E, banks[g - 1], g * G, (g + 1) * G)
+            second_layer(E, shared_sums(banks[g - 1], G), g * G, (g + 1) * G)
         finish(banks[0], 0, C)
         for g in range(2, 4):
             finish(banks[g - 1], g * G, (g + 1) * G)

@@ -22,12 +22,14 @@ J = 4
 KC = K // (P * J)
 G = 128
 BLOCKS = 2 * KC
-RAW_SETS = 3
+SHARED = E
+LAST = E - 1
+EARLY = 2
 WINDOW = 704
 
-GATHERING_SHARE = (0, 48, 0, 0)
-LAST_ROUTED_SHARE = (0, 32, 16, 32)
-SHARED_SHARE = (0, 0, 0, 0)
+QUARTERS_GATHERING = (0, 2, 0, 2)
+QUARTERS_LAST = (1, 2, 2, 2)
+QUARTERS_SHARED = (0, 0, 0, 1)
 
 
 def tile_moe_shr_glu_relu_kernel(tc, xT, w1, w3, w2, gate, offs, pos1, pos2, out):
@@ -60,30 +62,35 @@ def tile_moe_shr_glu_relu_kernel(tc, xT, w1, w3, w2, gate, offs, pos1, pos2, out
         offs_t = keep.tile([P, E * C // 16], U16, name="offs_t")
         pos_t = [keep.tile([P, T // 16], U16, name="pos1_t"), keep.tile([P, T // 16], U16, name="pos2_t")]
         banks = [psum.tile([P, 512], F32, name="bank%d" % b) for b in range(8)]
+
         planes = [(c, u) for c in reversed(range(KC)) for u in reversed(range(2))]
         x_raw = dict([(cu, sbuf("x_raw%d%d" % cu, [P, 2, T], F32)) for cu in planes])
         x_pair = sbuf("x_pair", [P, (3 * T + WINDOW) * 2], BF16)
-        raw = [[sbuf("raw%d%d" % (s, b), [P, J * H], F32) for b in range(BLOCKS)] for s in range(RAW_SETS)]
-        work = sbuf("work", [P, (1 + BLOCKS) * H * J], BF16)
-        rounded_matrix = [work[:, (1 + KC * layer) * H * J : (1 + KC * layer + KC) * H * J] for layer in range(2)]
-        rounded = [rounded_matrix[b // KC][:, (b % KC) * H * J : (b % KC + 1) * H * J] for b in range(BLOCKS)]
-        w_mx = [mx_tiles("w%d" % layer, KC * H) for layer in range(2)]
+
+        raw = [[sbuf("raw%d%d" % (s, b), [P, J * H], F32) for b in range(BLOCKS)] for s in range(3)]
         raw_set = [raw[0], raw[1], raw[2], raw[0], raw[2]]
+
+        work = sbuf("work", [P, (1 + BLOCKS) * H * J], BF16)
+        rounded = [work[:, (1 + b) * H * J : (2 + b) * H * J] for b in range(BLOCKS)]
+        w_mx = [mx_tiles("w%d" % layer, KC * H) for layer in range(2)]
+
         last_w2 = twice.tile([P, 2 * J * N], F32, name="last_w2", offset=0)
         y_sb = [twice.tile([P, E * C], F32, name="y_sb%d" % half, offset=half * E * C * 4) for half in range(2)]
-        raw2 = [raw[1][1][:, 0 : J * N], raw[1][1][:, J * N : 2 * J * N], last_w2[:, 0 : J * N], last_w2[:, J * N : 2 * J * N], ]
-        raw2 = [r.rearrange("p (j n) -> p j n", j=J) for r in raw2 + [raw[0][1][:, 0 : J * N]]]
+        raw2 = [raw[1][1][:, 0 : J * N], raw[1][1][:, J * N :], last_w2[:, 0 : J * N], last_w2[:, J * N :], raw[0][1][:, 0 : J * N]]
         rounded2 = sbuf("rounded2", [P, (E + 1) * N * J], BF16)
         w2_mx = mx_tiles("second", (E + 1) * N)
-        woven = sbuf("woven", [P, 2 * KC * C * J], BF16)
-        first_words = sbuf("first_words", [P, 2 * KC * C * J], BF16)
-        first_slots_mx = mx_tiles("first_slots", 2 * KC * C)
-        slot_mx = [(first_slots_mx[0][:, e * KC * C : (e + 1) * KC * C], first_slots_mx[1][:, e * KC * C : (e + 1) * KC * C]) for e in range(2)]
-        slot_mx = slot_mx + [(slot_mx[s][0], w_mx[0][1][4 * (s + 1) : P, H : H + KC * C]) for s in range(2)]
+
+        woven = sbuf("woven", [P, EARLY * KC * C * J], BF16)
+        early_words = sbuf("early_words", [P, EARLY * KC * C * J], BF16)
+        early_mx = mx_tiles("early", EARLY * KC * C)
+        slot_codes = [early_mx[0][:, s * KC * C : (s + 1) * KC * C] for s in range(EARLY)]
+        slot_mx = [(slot_codes[s], early_mx[1][:, s * KC * C : (s + 1) * KC * C]) for s in range(EARLY)]
+        slot_mx = slot_mx + [(slot_codes[s], w_mx[0][1][4 * (s + 1) : P, H : H + KC * C]) for s in range(E - EARLY)]
         all_woven = sbuf("all_woven", [P, KC * T * J], BF16)
         all_mx = mx_tiles("all", KC * T)
+
         hidden = sbuf("hidden", [P, T * J], BF16)
-        h_mx = [mx_tiles("h%d" % e, T if e == E else C) for e in range(E + 1)]
+        h_mx = [mx_tiles("h%d" % e, T if e == SHARED else C) for e in range(E + 1)]
         gate_row = sbuf("gate_row", [P, 2, J], F32)
         gates = [sbuf("gates%d" % r, [P, T], F32) for r in range(2)]
         identity = sbuf("identity", [P, P], F32)
@@ -92,13 +99,13 @@ def tile_moe_shr_glu_relu_kernel(tc, xT, w1, w3, w2, gate, offs, pos1, pos2, out
             src = xT[c * P * J : (c + 1) * P * J, :].rearrange("(p j) w -> p j w", j=J)
             nc.sync.dma_start(out=x_raw[c, u][:], in_=src[:, 2 * u : 2 * u + 2, :])
 
-        def load_block(e, b):
-            w = (w1, w3)[b // KC]
-            c = b % KC
-            nc.sync.dma_start(out=raw_set[e][b][:], in_=w[e, c * P * J : (c + 1) * P * J, :].rearrange("(p j) w -> p (j w)", j=J))
+        def load_first_layer(e):
+            for b in range(BLOCKS):
+                rows = (w1, w3)[b // KC][e, (b % KC) * P * J : (b % KC + 1) * P * J, :]
+                nc.sync.dma_start(out=raw_set[e][b][:], in_=rows.rearrange("(p j) w -> p (j w)", j=J))
 
         def load_w2(e):
-            nc.sync.dma_start(out=raw2[e], in_=w2[e].rearrange("(p j) w -> p j w", j=J))
+            nc.sync.dma_start(out=raw2[e].rearrange("p (j n) -> p j n", j=J), in_=w2[e].rearrange("(p j) w -> p j w", j=J))
 
         def pair_plane(c, u, width):
             first = (2 * c + u) * T
@@ -110,26 +117,23 @@ def tile_moe_shr_glu_relu_kernel(tc, xT, w1, w3, w2, gate, offs, pos1, pos2, out
         def gather(e, experts, c, u, words):
             count = experts * C
             first = (2 * c + u) * count
-            window = pair_plane(c, u, WINDOW if experts == 2 else T).bitcast(U32)
+            window = pair_plane(c, u, WINDOW if experts == EARLY else T).bitcast(U32)
             nc.vector.tensor_copy(words.bitcast(U32)[:, first : first + count], window.indirect(offs_t[:, e * C // 16 : (e * C + count) // 16]))
 
-        def weave_first_slots():
+        def weave_early_slots():
             nc.vector.tensor_copy(
-                out=woven[:].bitcast(I32).rearrange("p (e c n u) -> p e c n u", e=2, c=KC, u=2),
-                in_=first_words[:].bitcast(I32).rearrange("p (c u e n) -> p e c n u", c=KC, u=2, e=2),
+                out=woven[:].bitcast(I32).rearrange("p (e c n u) -> p e c n u", e=EARLY, c=KC, u=2),
+                in_=early_words[:].bitcast(I32).rearrange("p (c u e n) -> p e c n u", c=KC, u=2, e=EARLY),
             )
 
         def woven_slots(e):
-            return woven[:, (e % 2) * KC * C * J : (e % 2 + 1) * KC * C * J]
+            return woven[:, (e % EARLY) * KC * C * J : (e % EARLY + 1) * KC * C * J]
 
         def weave_slots(e):
             nc.gpsimd.tensor_copy(
                 out=woven_slots(e).bitcast(I32).rearrange("p (c n u) -> p c n u", c=KC, u=2),
                 in_=rounded[BLOCKS - 1].bitcast(I32).rearrange("p (c u n) -> p c n u", c=KC, u=2),
             )
-
-        def quantise_slots(e):
-            quantise(slot_mx[e], slice(0, KC * C), woven_slots(e))
 
         def weave_all_tokens():
             nc.vector.tensor_copy(
@@ -138,33 +142,27 @@ def tile_moe_shr_glu_relu_kernel(tc, xT, w1, w3, w2, gate, offs, pos1, pos2, out
             )
 
         def round_block(e, b):
-            dst = rounded[b].rearrange("p (t u v j) -> p u v j t", t=J, v=2, j=J)
-            src = raw_set[e][b][:].rearrange("p (j u v t) -> p u v j t", j=J, t=J, v=2)
-            share = (GATHERING_SHARE if e + 1 < E else LAST_ROUTED_SHARE if e < E else SHARED_SHARE)[b]
-            if share < P // 2:
-                nc.scalar.copy(out=dst[:, share:], in_=src[:, share:])
+            dst = rounded[b].rearrange("p (t m j) -> p m j t", t=J, j=J)
+            src = raw_set[e][b][:].rearrange("p (j m t) -> p m j t", j=J, t=J)
+            share = (QUARTERS_SHARED if e == SHARED else QUARTERS_LAST if e == LAST else QUARTERS_GATHERING)[b] * P // 4
+            nc.scalar.copy(out=dst[:, share:], in_=src[:, share:])
             if share > 0:
                 nc.vector.tensor_copy(out=dst[:, :share], in_=src[:, :share])
 
         def quantise_block(b):
             quantise(w_mx[b // KC], slice((b % KC) * H, (b % KC + 1) * H), rounded[b])
 
-        def quantise_matrix(layer):
-            quantise(w_mx[layer], slice(0, KC * H), rounded_matrix[layer])
+        def round_w2(e, copy):
+            copy(
+                out=rounded2[:, e * N * J : (e + 1) * N * J].rearrange("p (n i j) -> p n j i", i=2, j=J),
+                in_=raw2[e].rearrange("p (j n i) -> p n j i", j=J, i=2),
+            )
 
-        def round_w2(e, share):
-            dst = rounded2[:, e * N * J : (e + 1) * N * J].rearrange("p (n i j) -> p n j i", i=2, j=J)
-            src = raw2[e].rearrange("p j (n i) -> p n j i", i=2)
-            if share < N // 2:
-                nc.scalar.copy(out=dst[:, share:], in_=src[:, share:])
-            if share > 0:
-                nc.vector.tensor_copy(out=dst[:, :share], in_=src[:, :share])
-
-        def quantise_w2(e, count):
-            quantise(w2_mx, slice(e * N, (e + count) * N), rounded2[:, e * N * J : (e + count) * N * J])
+        def quantise_w2(e):
+            quantise(w2_mx, slice(e * N, (e + 1) * N), rounded2[:, e * N * J : (e + 1) * N * J])
 
         def first_layer(e, layer, g):
-            tokens, width = (all_mx, T) if e == E else (slot_mx[e], C)
+            tokens, width = (all_mx, T) if e == SHARED else (slot_mx[e], C)
             bank = banks[4 * layer + g]
             for t in range(J):
                 for c in range(KC):
@@ -172,22 +170,18 @@ def tile_moe_shr_glu_relu_kernel(tc, xT, w1, w3, w2, gate, offs, pos1, pos2, out
                     matmul(bank[:, t * G : (t + 1) * G], w_mx[layer], slice(c * H + t * P, c * H + (t + 1) * P), tokens, cols, c == 0, c == KC - 1)
 
         def relu_tile(e, g):
-            if e + 1 < E:
-                room = raw_set[e + 1][0]
-            else:
-                room = raw_set[e][BLOCKS - 1]
+            room = raw_set[e + 1][0] if e < LAST else raw_set[e][BLOCKS - 1]
             return room[:, g * G * J : (g + 1) * G * J].rearrange("p (n t i) -> p n t i", t=J, i=2)
 
+        def in_pairs(bank):
+            return bank[:].rearrange("p (t n i) -> p n t i", t=J, i=2)
+
         def relu(e, g):
-            nc.scalar.activation(out=relu_tile(e, g), in_=banks[g][:].rearrange("p (t n i) -> p n t i", t=J, i=2), func=RELU)
+            nc.scalar.activation(out=relu_tile(e, g), in_=in_pairs(banks[g]), func=RELU)
 
         def gated(e, g):
-            nc.vector.tensor_tensor(
-                out=hidden[:, g * G * J : (g + 1) * G * J].rearrange("p (n i t) -> p n t i", t=J, i=2),
-                in0=banks[4 + g][:].rearrange("p (t n i) -> p n t i", t=J, i=2),
-                in1=relu_tile(e, g),
-                op=MULT,
-            )
+            h = hidden[:, g * G * J : (g + 1) * G * J].rearrange("p (n i t) -> p n t i", t=J, i=2)
+            nc.vector.tensor_tensor(out=h, in0=in_pairs(banks[4 + g]), in1=relu_tile(e, g), op=MULT)
 
         def quantise_hidden(e, lo, hi):
             quantise(h_mx[e], slice(lo, hi), hidden[:, lo * J : hi * J])
@@ -196,24 +190,25 @@ def tile_moe_shr_glu_relu_kernel(tc, xT, w1, w3, w2, gate, offs, pos1, pos2, out
             for half in range(2):
                 matmul(sums[half], w2_mx, slice(e * N + half * P, e * N + (half + 1) * P), h_mx[e], slice(lo, hi), True, True)
 
-
-        def shared_sums(bank, width):
-            return [bank[:, half * width : (half + 1) * width] for half in range(2)]
+        def slot_sums(e, half):
+            return banks[2 * e + half][:, 0:C]
 
         def store_slots(e, half, copy):
-            copy(out=y_sb[half][:, e * C : (e + 1) * C], in_=banks[2 * e + half][:, 0:C])
+            copy(out=y_sb[half][:, e * C : (e + 1) * C], in_=slot_sums(e, half))
 
+        columns = work[:].bitcast(F32)
+        term = [columns[:, r * T : (r + 4 + 2 * r) * T].rearrange("p (h n) -> p h n", h=2)[:, :, 0:T] for r in range(2)]
         combined = rounded[BLOCKS - 1].bitcast(F32).rearrange("p (h n) -> p h n", h=2)
-        term = [work[:, 0 : 4 * H * J].bitcast(F32).rearrange("p (h n) -> p h n", h=2)[:, :, r * T : (r + 1) * T] for r in range(2)]
 
         def pick(r, half):
             nc.vector.tensor_tensor(out=term[r][:, half, :], in0=y_sb[half][:].indirect(pos_t[r][:]), in1=gates[r][:], op=MULT)
 
-        def combine():
-            nc.vector.tensor_add(out=combined, in0=term[0], in1=term[1])
+        def shared_second_layer(bank, lo, hi):
+            quantise_hidden(SHARED, lo, hi)
+            second_layer(SHARED, [bank[:, half * (hi - lo) : (half + 1) * (hi - lo)] for half in range(2)], lo, hi)
 
         def finish(bank, lo, hi):
-            first = {0: 2 * C, C: 0, C + G: C}[lo]
+            first = 2 * ((lo + C) % T)
             result = hidden[:].bitcast(F32)[:, first : first + 2 * (hi - lo)].rearrange("p (h n) -> p h n", h=2)
             nc.vector.tensor_add(out=result, in0=bank[:, 0 : 2 * (hi - lo)].rearrange("p (h n) -> p h n", h=2), in1=combined[:, :, lo:hi])
             nc.sync.dma_start(out=out.rearrange("(h p) t -> p h t", p=P)[:, :, lo:hi], in_=result)
@@ -223,111 +218,103 @@ def tile_moe_shr_glu_relu_kernel(tc, xT, w1, w3, w2, gate, offs, pos1, pos2, out
         nc.sync.dma_start(out=gate_row[:], in_=gate[:, 0, :].rearrange("r (p m) -> p r m", m=J))
         for c, u in planes[1:]:
             load_x(c, u)
-        load_block(0, 0)
-        load_block(0, 1)
-        load_block(0, 2)
-        load_block(0, 3)
-        for e in range(1, RAW_SETS):
-            for b in range(BLOCKS):
-                load_block(e, b)
+        for e in range(len(raw)):
+            load_first_layer(e)
 
         nc.gpsimd.memset(x_pair[:, 4 * T * 2 :], 0.0)
         for c, u in planes:
             pair_tokens(c, u, nc.vector.tensor_copy if c == KC - 1 else nc.scalar.copy)
-            gather(0, 2, c, u, first_words[:])
+            gather(0, EARLY, c, u, early_words[:])
+
         make_identity(nc, identity[:])
         for r in range(2):
+            bank = banks[2 + r]
             for m in range(J):
-                nc.tensor.transpose(banks[2 + r][:, m * P : (m + 1) * P], gate_row[:, r, m : m + 1].to_broadcast([P, P]), identity[:])
-            nc.scalar.copy(out=gates[r][:].rearrange("p (n m) -> p n m", m=J), in_=banks[2 + r][:].rearrange("p (m n) -> p n m", m=J))
+                nc.tensor.transpose(bank[:, m * P : (m + 1) * P], gate_row[:, r, m : m + 1].to_broadcast([P, P]), identity[:])
+            nc.scalar.copy(out=gates[r][:].rearrange("p (n m) -> p n m", m=J), in_=bank[:].rearrange("p (m n) -> p n m", m=J))
 
-        weave_first_slots()
+        weave_early_slots()
         weave_all_tokens()
-        quantise(first_slots_mx, slice(0, 2 * KC * C), woven[:])
+        quantise(early_mx, slice(0, EARLY * KC * C), woven[:])
         quantise(all_mx, slice(0, KC * T), all_woven[:])
 
+        groups = range(C // G)
         for e in range(E):
             for b in range(BLOCKS):
                 round_block(e, b)
-                if b == 0 and e > 0:
-                    for g in range(C // G):
+                if e > 0 and b == 0:
+                    for g in groups:
                         relu(e - 1, g)
-                    for g in range(C // G):
-                        gated(e - 1, g)
-                if b == 1 and e > 0:
+                if e > 0 and b == 1:
                     quantise_hidden(e - 1, 0, C)
-                if e + 1 == E:
-                    quantise_block(b)
-                elif b % KC == KC - 1:
-                    quantise_matrix(b // KC)
-                if b == 1 and 2 <= e + 1 < E:
-                    quantise_slots(e + 1)
+                quantise_block(b)
+                if e > 0 and b == 0:
+                    for g in groups:
+                        gated(e - 1, g)
+                if EARLY <= e + 1 < E and b == 1:
+                    quantise(slot_mx[e + 1], slice(0, KC * C), woven_slots(e + 1))
                 if b % KC == KC - 1:
-                    for g in range(C // G):
+                    for g in groups:
                         first_layer(e, b // KC, g)
-            if e + 2 < E:
+            if e + EARLY < E:
                 for c, u in planes:
-                    gather(e + 2, 1, c, u, rounded[BLOCKS - 1])
-                weave_slots(e + 2)
-            if e + 1 == E:
-                for g in range(C // G):
-                    relu(e, g)
-                round_w2(0, N // 2)
-                quantise_w2(0, 1)
-                for g in range(C // G):
-                    gated(e, g)
+                    gather(e + EARLY, 1, c, u, rounded[BLOCKS - 1])
+                weave_slots(e + EARLY)
             if e == 0:
-                for b in range(BLOCKS):
-                    load_block(E - 1, b)
+                load_first_layer(LAST)
             if e == 1:
-                for other in range(E):
-                    load_w2(other)
+                for routed in range(E):
+                    load_w2(routed)
                 nc.sync.dma_start(pos_t[0][:], pos1)
                 nc.sync.dma_start(pos_t[1][:], pos2)
             if e == 2:
-                for b in range(BLOCKS):
-                    load_block(E, b)
-            if e == 3:
-                load_w2(E)
+                load_first_layer(SHARED)
 
-        for e in range(1, E):
-            round_w2(e, 0)
-            quantise_w2(e, 1)
-            if e == 1:
-                quantise_hidden(E - 1, 0, C)
+        for g in groups:
+            relu(LAST, g)
+        round_w2(0, nc.vector.tensor_copy)
+        quantise_w2(0)
+        for g in groups:
+            gated(LAST, g)
+        load_w2(SHARED)
+        round_w2(1, nc.scalar.copy)
+        quantise_w2(1)
+        quantise_hidden(LAST, 0, C)
+        for e in range(2, E):
+            round_w2(e, nc.scalar.copy)
+            quantise_w2(e)
         for e in range(E):
-            second_layer(e, [banks[2 * e + half][:, 0:C] for half in range(2)], 0, C)
+            second_layer(e, [slot_sums(e, half) for half in range(2)], 0, C)
         for half in range(2):
-            for e in range(E - 1 - half):
+            for e in range(LAST - half):
                 store_slots(e, half, nc.scalar.copy)
-        for e, half in ((E - 2, 1), (E - 1, 0), (E - 1, 1)):
+        for e, half in ((LAST - 1, 1), (LAST, 0), (LAST, 1)):
             store_slots(e, half, nc.vector.tensor_copy)
 
+        groups = range(T // G)
         pick(0, 0)
         pick(1, 0)
         for b in range(BLOCKS):
-            round_block(E, b)
+            round_block(SHARED, b)
             quantise_block(b)
-            if b == 1:
-                pick(0, 1)
-                pick(1, 1)
+            if b < 2:
+                pick(b, 1)
             if b % KC == KC - 1:
-                for g in range(T // G):
-                    first_layer(E, b // KC, g)
-        for g in range(T // G):
-            relu(E, g)
-        round_w2(E, 0)
-        combine()
-        for pair in range(2):
-            gated(E, 2 * pair)
-            gated(E, 2 * pair + 1)
-            if pair == 0:
-                quantise_w2(E, 1)
-                quantise_hidden(E, 0, C)
-                second_layer(E, shared_sums(banks[0], C), 0, C)
-        for g in range(2, 4):
-            quantise_hidden(E, g * G, (g + 1) * G)
-            second_layer(E, shared_sums(banks[g - 1], G), g * G, (g + 1) * G)
-        finish(banks[0], 0, C)
-        for g in range(2, 4):
-            finish(banks[g - 1], g * G, (g + 1) * G)
+                for g in groups:
+                    first_layer(SHARED, b // KC, g)
+        for g in groups:
+            relu(SHARED, g)
+        round_w2(SHARED, nc.scalar.copy)
+        nc.vector.tensor_add(out=combined, in0=term[0], in1=term[1])
+
+        pieces = [(banks[0], 0, 2 * G), (banks[1], 2 * G, 3 * G), (banks[2], 3 * G, 4 * G)]
+        gated(SHARED, 0)
+        gated(SHARED, 1)
+        quantise_w2(SHARED)
+        shared_second_layer(*pieces[0])
+        gated(SHARED, 2)
+        gated(SHARED, 3)
+        for piece in pieces[1:]:
+            shared_second_layer(*piece)
+        for piece in pieces:
+            finish(*piece)

@@ -27,9 +27,9 @@ LAST = E - 1
 EARLY = 2
 WINDOW = 704
 
-QUARTERS_GATHERING = (0, 2, 0, 2)
-QUARTERS_LAST = (1, 2, 2, 2)
-QUARTERS_SHARED = (0, 0, 0, 1)
+EIGHTHS_GATHERING = (0, 4, 0, 4)
+EIGHTHS_LAST = (2, 4, 2, 5)
+EIGHTHS_SHARED = (4, 2, 0, 3)
 
 
 def tile_moe_shr_glu_relu_kernel(tc, xT, w1, w3, w2, gate, offs, pos1, pos2, out):
@@ -76,7 +76,7 @@ def tile_moe_shr_glu_relu_kernel(tc, xT, w1, w3, w2, gate, offs, pos1, pos2, out
 
         last_w2 = twice.tile([P, 2 * J * N], F32, name="last_w2", offset=0)
         y_sb = [twice.tile([P, E * C], F32, name="y_sb%d" % half, offset=half * E * C * 4) for half in range(2)]
-        raw2 = [raw[1][1][:, 0 : J * N], raw[1][1][:, J * N :], last_w2[:, 0 : J * N], last_w2[:, J * N :], raw[0][1][:, 0 : J * N]]
+        raw2 = [raw[1][1][:, 0 : J * N], last_w2[:, 0 : J * N], last_w2[:, J * N :], raw[1][1][:, J * N :], raw[0][1][:, 0 : J * N]]
         rounded2 = sbuf("rounded2", [P, (E + 1) * N * J], BF16)
         w2_mx = mx_tiles("second", (E + 1) * N)
 
@@ -99,8 +99,8 @@ def tile_moe_shr_glu_relu_kernel(tc, xT, w1, w3, w2, gate, offs, pos1, pos2, out
             src = xT[c * P * J : (c + 1) * P * J, :].rearrange("(p j) w -> p j w", j=J)
             nc.sync.dma_start(out=x_raw[c, u][:], in_=src[:, 2 * u : 2 * u + 2, :])
 
-        def load_first_layer(e):
-            for b in range(BLOCKS):
+        def load_first_layer(e, blocks):
+            for b in blocks:
                 rows = (w1, w3)[b // KC][e, (b % KC) * P * J : (b % KC + 1) * P * J, :]
                 nc.sync.dma_start(out=raw_set[e][b][:], in_=rows.rearrange("(p j) w -> p (j w)", j=J))
 
@@ -144,7 +144,7 @@ def tile_moe_shr_glu_relu_kernel(tc, xT, w1, w3, w2, gate, offs, pos1, pos2, out
         def round_block(e, b):
             dst = rounded[b].rearrange("p (t m j) -> p m j t", t=J, j=J)
             src = raw_set[e][b][:].rearrange("p (j m t) -> p m j t", j=J, t=J)
-            share = (QUARTERS_SHARED if e == SHARED else QUARTERS_LAST if e == LAST else QUARTERS_GATHERING)[b] * P // 4
+            share = (EIGHTHS_SHARED if e == SHARED else EIGHTHS_LAST if e == LAST else EIGHTHS_GATHERING)[b] * P // 8
             nc.scalar.copy(out=dst[:, share:], in_=src[:, share:])
             if share > 0:
                 nc.vector.tensor_copy(out=dst[:, :share], in_=src[:, :share])
@@ -158,58 +158,66 @@ def tile_moe_shr_glu_relu_kernel(tc, xT, w1, w3, w2, gate, offs, pos1, pos2, out
                 in_=raw2[e].rearrange("p (j n i) -> p n j i", j=J, i=2),
             )
 
-        def quantise_w2(e):
-            quantise(w2_mx, slice(e * N, (e + 1) * N), rounded2[:, e * N * J : (e + 1) * N * J])
+        def quantise_w2(e, count):
+            quantise(w2_mx, slice(e * N, (e + count) * N), rounded2[:, e * N * J : (e + count) * N * J])
 
-        def first_layer(e, layer, g):
+        def first_bank(e, layer, g):
+            return banks[4 * layer + g + (0 if e == SHARED else 2 * (e % 2))]
+
+        def first_layer(e, b, g):
+            layer, c = divmod(b, KC)
             tokens, width = (all_mx, T) if e == SHARED else (slot_mx[e], C)
-            bank = banks[4 * layer + g]
+            cols = slice(c * width + g * G, c * width + (g + 1) * G)
             for t in range(J):
-                for c in range(KC):
-                    cols = slice(c * width + g * G, c * width + (g + 1) * G)
-                    matmul(bank[:, t * G : (t + 1) * G], w_mx[layer], slice(c * H + t * P, c * H + (t + 1) * P), tokens, cols, c == 0, c == KC - 1)
+                acc = first_bank(e, layer, g)[:, t * G : (t + 1) * G]
+                matmul(acc, w_mx[layer], slice(c * H + t * P, c * H + (t + 1) * P), tokens, cols, c == 0 and t == 0, c == KC - 1 and t == J - 1)
 
         def relu_tile(e, g):
-            room = raw_set[e + 1][0] if e < LAST else raw_set[e][BLOCKS - 1]
-            return room[:, g * G * J : (g + 1) * G * J].rearrange("p (n t i) -> p n t i", t=J, i=2)
+            if e == SHARED:
+                room = raw_set[e][BLOCKS - 1] if g < 2 else raw2[SHARED]
+            else:
+                room = raw_set[e + 1][0] if e < LAST else raw_set[e][BLOCKS - 1]
+            return room[:, (g % 2) * G * J : (g % 2 + 1) * G * J].rearrange("p (n t i) -> p n t i", t=J, i=2)
 
         def in_pairs(bank):
             return bank[:].rearrange("p (t n i) -> p n t i", t=J, i=2)
 
         def relu(e, g):
-            nc.scalar.activation(out=relu_tile(e, g), in_=in_pairs(banks[g]), func=RELU)
+            nc.scalar.activation(out=relu_tile(e, g), in_=in_pairs(first_bank(e, 0, g)), func=RELU)
 
         def gated(e, g):
             h = hidden[:, g * G * J : (g + 1) * G * J].rearrange("p (n i t) -> p n t i", t=J, i=2)
-            nc.vector.tensor_tensor(out=h, in0=in_pairs(banks[4 + g]), in1=relu_tile(e, g), op=MULT)
+            nc.vector.tensor_tensor(out=h, in0=in_pairs(first_bank(e, 1, g)), in1=relu_tile(e, g), op=MULT)
 
         def quantise_hidden(e, lo, hi):
             quantise(h_mx[e], slice(lo, hi), hidden[:, lo * J : hi * J])
 
-        def second_layer(e, sums, lo, hi):
-            for half in range(2):
+        def second_layer(e, sums, lo, hi, halves):
+            for half in halves:
                 matmul(sums[half], w2_mx, slice(e * N + half * P, e * N + (half + 1) * P), h_mx[e], slice(lo, hi), True, True)
 
+        sums_at = {(0, 0): (0, 0), (1, 0): (0, C), (0, 1): (1, 0), (1, 1): (1, C), (2, 0): (4, 0), (3, 0): (5, 0), (2, 1): (2, 0), (3, 1): (2, C)}
+
         def slot_sums(e, half):
-            return banks[2 * e + half][:, 0:C]
+            bank, first = sums_at[e, half]
+            return banks[bank][:, first : first + C]
 
-        def store_slots(e, half, copy):
-            copy(out=y_sb[half][:, e * C : (e + 1) * C], in_=slot_sums(e, half))
+        def store_slots(e, count, half, copy):
+            bank, first = sums_at[e, half]
+            copy(out=y_sb[half][:, e * C : (e + count) * C], in_=banks[bank][:, first : first + count * C])
 
-        columns = work[:].bitcast(F32)
-        term = [columns[:, r * T : (r + 4 + 2 * r) * T].rearrange("p (h n) -> p h n", h=2)[:, :, 0:T] for r in range(2)]
-        combined = rounded[BLOCKS - 1].bitcast(F32).rearrange("p (h n) -> p h n", h=2)
+        term = [[raw[1][2][:, 0:T], raw[1][2][:, T : 2 * T]], [raw[1][3][:, 0:T], raw_set[SHARED][1][:, 0:T]]]
+        combined = raw_set[SHARED][BLOCKS - 1][:, 2 * T :].rearrange("p (h n) -> p h n", h=2)
 
         def pick(r, half):
-            nc.vector.tensor_tensor(out=term[r][:, half, :], in0=y_sb[half][:].indirect(pos_t[r][:]), in1=gates[r][:], op=MULT)
+            nc.vector.tensor_tensor(out=term[r][half], in0=y_sb[half][:].indirect(pos_t[r][:]), in1=gates[r][:], op=MULT)
 
         def shared_second_layer(bank, lo, hi):
             quantise_hidden(SHARED, lo, hi)
-            second_layer(SHARED, [bank[:, half * (hi - lo) : (half + 1) * (hi - lo)] for half in range(2)], lo, hi)
+            second_layer(SHARED, [bank[:, half * (hi - lo) : (half + 1) * (hi - lo)] for half in range(2)], lo, hi, range(2))
 
         def finish(bank, lo, hi):
-            first = 2 * ((lo + C) % T)
-            result = hidden[:].bitcast(F32)[:, first : first + 2 * (hi - lo)].rearrange("p (h n) -> p h n", h=2)
+            result = raw_set[SHARED][2][:, 2 * lo : 2 * hi].rearrange("p (h n) -> p h n", h=2)
             nc.vector.tensor_add(out=result, in0=bank[:, 0 : 2 * (hi - lo)].rearrange("p (h n) -> p h n", h=2), in1=combined[:, :, lo:hi])
             nc.sync.dma_start(out=out.rearrange("(h p) t -> p h t", p=P)[:, :, lo:hi], in_=result)
 
@@ -219,7 +227,7 @@ def tile_moe_shr_glu_relu_kernel(tc, xT, w1, w3, w2, gate, offs, pos1, pos2, out
         for c, u in planes[1:]:
             load_x(c, u)
         for e in range(len(raw)):
-            load_first_layer(e)
+            load_first_layer(e, range(BLOCKS))
 
         nc.gpsimd.memset(x_pair[:, 4 * T * 2 :], 0.0)
         for c, u in planes:
@@ -253,66 +261,74 @@ def tile_moe_shr_glu_relu_kernel(tc, xT, w1, w3, w2, gate, offs, pos1, pos2, out
                         gated(e - 1, g)
                 if EARLY <= e + 1 < E and b == 1:
                     quantise(slot_mx[e + 1], slice(0, KC * C), woven_slots(e + 1))
-                if b % KC == KC - 1:
-                    for g in groups:
-                        first_layer(e, b // KC, g)
+                for g in groups:
+                    first_layer(e, b, g)
             if e + EARLY < E:
                 for c, u in planes:
                     gather(e + EARLY, 1, c, u, rounded[BLOCKS - 1])
                 weave_slots(e + EARLY)
             if e == 0:
-                load_first_layer(LAST)
+                load_first_layer(LAST, range(BLOCKS))
             if e == 1:
                 for routed in range(E):
                     load_w2(routed)
-                nc.sync.dma_start(pos_t[0][:], pos1)
-                nc.sync.dma_start(pos_t[1][:], pos2)
             if e == 2:
-                load_first_layer(SHARED)
+                load_first_layer(SHARED, [0])
+                nc.sync.dma_start(pos_t[0][:], pos1)
+                load_first_layer(SHARED, [1])
+                nc.sync.dma_start(pos_t[1][:], pos2)
+                load_first_layer(SHARED, [2, 3])
 
         for g in groups:
             relu(LAST, g)
         round_w2(0, nc.vector.tensor_copy)
-        quantise_w2(0)
+        quantise_w2(0, 1)
         for g in groups:
             gated(LAST, g)
         load_w2(SHARED)
         round_w2(1, nc.scalar.copy)
-        quantise_w2(1)
+        quantise_w2(1, 1)
         quantise_hidden(LAST, 0, C)
-        for e in range(2, E):
-            round_w2(e, nc.scalar.copy)
-            quantise_w2(e)
-        for e in range(E):
-            second_layer(e, [slot_sums(e, half) for half in range(2)], 0, C)
-        for half in range(2):
-            for e in range(LAST - half):
-                store_slots(e, half, nc.scalar.copy)
-        for e, half in ((LAST - 1, 1), (LAST, 0), (LAST, 1)):
-            store_slots(e, half, nc.vector.tensor_copy)
+        round_w2(2, nc.scalar.copy)
+        round_w2(LAST, nc.vector.tensor_copy)
+        quantise_w2(2, 2)
+        for pair in range(2):
+            for half in range(2):
+                for e in (2 * pair, 2 * pair + 1):
+                    second_layer(e, [slot_sums(e, 0), slot_sums(e, 1)], 0, C, [half])
+        store_slots(0, 2, 0, nc.scalar.copy)
+        store_slots(0, 2, 1, nc.scalar.copy)
+        store_slots(2, 1, 0, nc.scalar.copy)
+        store_slots(3, 1, 0, nc.vector.tensor_copy)
+        store_slots(2, 2, 1, nc.scalar.copy)
 
         groups = range(T // G)
-        pick(0, 0)
-        pick(1, 0)
         for b in range(BLOCKS):
             round_block(SHARED, b)
+            if b == 0:
+                pick(0, 0)
+                pick(0, 1)
+            if b == 1:
+                pick(1, 0)
             quantise_block(b)
-            if b < 2:
-                pick(b, 1)
-            if b % KC == KC - 1:
-                for g in groups:
-                    first_layer(SHARED, b // KC, g)
-        for g in groups:
-            relu(SHARED, g)
+            if b == 1:
+                pick(1, 1)
+            for g in groups:
+                first_layer(SHARED, b, g)
+        relu(SHARED, 0)
+        relu(SHARED, 1)
         round_w2(SHARED, nc.scalar.copy)
-        nc.vector.tensor_add(out=combined, in0=term[0], in1=term[1])
+        relu(SHARED, 2)
+        relu(SHARED, 3)
+        for half in range(2):
+            nc.vector.tensor_add(out=combined[:, half, :], in0=term[0][half], in1=term[1][half])
 
-        pieces = [(banks[0], 0, 2 * G), (banks[1], 2 * G, 3 * G), (banks[2], 3 * G, 4 * G)]
+        pieces = [(banks[0], 0, 2 * G), (banks[1], 2 * G, 3 * G), (banks[4], 3 * G, 4 * G)]
         gated(SHARED, 0)
         gated(SHARED, 1)
-        quantise_w2(SHARED)
-        shared_second_layer(*pieces[0])
+        quantise_w2(SHARED, 1)
         gated(SHARED, 2)
+        shared_second_layer(*pieces[0])
         gated(SHARED, 3)
         for piece in pieces[1:]:
             shared_second_layer(*piece)

@@ -27,13 +27,20 @@ LAST = E - 1
 EARLY = 2
 WINDOW = 704
 
-EIGHTHS_GATHERING = (0, 4, 0, 4)
-EIGHTHS_LAST = (2, 4, 2, 5)
-EIGHTHS_SHARED = (4, 2, 0, 3)
+SHARES = [(0, 0, 0, 0), (0, 0, 8, 0), (8, 0, 4, 4), (8, 4, 0, 4), (8, 0, 0, 2)]
+ORDER = [(0, 2, 1, 3), (0, 2, 1, 3), (0, 2, 1, 3), (0, 2, 1, 3), (0, 1, 2, 3)]
+MERGED = [(0, 1), (0, 1), (0, 1), (0, 0), (0, 0)]
+RELU_AT = [(1, 0), None, None, (3, 3)]
+HID_AT = [None, None, None]
+VPAIRS = 1
+WORDS_AT = (0, 1)
+WOVEN_AT = (0, 3)
+GATE_AT = 4
 
 
 def tile_moe_shr_glu_relu_kernel(tc, xT, w1, w3, w2, gate, offs, pos1, pos2, out):
     nc = tc.nc
+    assert WORDS_AT < WOVEN_AT and WORDS_AT not in RELU_AT and WOVEN_AT not in RELU_AT
     with ExitStack() as ctx:
         keep = ctx.enter_context(tc.tile_pool(name="keep", bufs=1))
         twice = ctx.enter_context(tc.tile_pool(name="twice", bufs=1))
@@ -70,27 +77,31 @@ def tile_moe_shr_glu_relu_kernel(tc, xT, w1, w3, w2, gate, offs, pos1, pos2, out
         raw = [[sbuf("raw%d%d" % (s, b), [P, J * H], F32) for b in range(BLOCKS)] for s in range(3)]
         raw_set = [raw[0], raw[1], raw[2], raw[0], raw[2]]
 
-        work = sbuf("work", [P, (1 + BLOCKS) * H * J], BF16)
-        rounded = [work[:, (1 + b) * H * J : (2 + b) * H * J] for b in range(BLOCKS)]
+        rounded_layer = [sbuf("rounded_layer%d" % layer, [P, KC * H * J], BF16) for layer in range(2)]
+        rounded = [rounded_layer[b // KC][:, (b % KC) * H * J : (b % KC + 1) * H * J] for b in range(BLOCKS)]
+        relu_sb = sbuf("relu_sb", [P, C * J], F32)
+
+        def raw_at(at):
+            return raw_set[at[0]][ORDER[at[0]][at[1]]]
+
         w_mx = [mx_tiles("w%d" % layer, KC * H) for layer in range(2)]
 
         last_w2 = twice.tile([P, 2 * J * N], F32, name="last_w2", offset=0)
         y_sb = [twice.tile([P, E * C], F32, name="y_sb%d" % half, offset=half * E * C * 4) for half in range(2)]
         raw2 = [raw[1][1][:, 0 : J * N], last_w2[:, 0 : J * N], last_w2[:, J * N :], raw[1][1][:, J * N :], raw[0][1][:, 0 : J * N]]
-        rounded2 = sbuf("rounded2", [P, (E + 1) * N * J], BF16)
-        w2_mx = mx_tiles("second", (E + 1) * N)
+        second_in = sbuf("second_in", [P, (E * N + T + N) * J], BF16)
+        second_mx = mx_tiles("second", E * N + T + N)
+        w2_at = [0, N, 2 * N, 3 * N, E * N + T]
 
-        woven = sbuf("woven", [P, EARLY * KC * C * J], BF16)
-        early_words = sbuf("early_words", [P, EARLY * KC * C * J], BF16)
-        early_mx = mx_tiles("early", EARLY * KC * C)
-        slot_codes = [early_mx[0][:, s * KC * C : (s + 1) * KC * C] for s in range(EARLY)]
-        slot_mx = [(slot_codes[s], early_mx[1][:, s * KC * C : (s + 1) * KC * C]) for s in range(EARLY)]
-        slot_mx = slot_mx + [(slot_codes[s], w_mx[0][1][4 * (s + 1) : P, H : H + KC * C]) for s in range(E - EARLY)]
+        S = EARLY * C
+        words = [sbuf("early_words", [P, KC * 2 * S], F32), raw_at(WORDS_AT)]
+        woven = [sbuf("early_woven", [P, KC * 2 * S], F32), raw_at(WOVEN_AT)]
+        slot_mx = [mx_tiles("slots%d" % i, KC * S) for i in range(2)]
         all_woven = sbuf("all_woven", [P, KC * T * J], BF16)
         all_mx = mx_tiles("all", KC * T)
 
-        hidden = sbuf("hidden", [P, T * J], BF16)
-        h_mx = [mx_tiles("h%d" % e, T if e == SHARED else C) for e in range(E + 1)]
+        hidden = second_in[:, E * N * J : (E * N + T) * J]
+        h_mx = [mx_tiles("h_early", T), (second_mx[0][:, E * N : E * N + T], second_mx[1][:, E * N : E * N + T]), mx_tiles("h_shared", T)]
         gate_row = sbuf("gate_row", [P, 2, J], F32)
         gates = [sbuf("gates%d" % r, [P, T], F32) for r in range(2)]
         identity = sbuf("identity", [P, P], F32)
@@ -99,8 +110,8 @@ def tile_moe_shr_glu_relu_kernel(tc, xT, w1, w3, w2, gate, offs, pos1, pos2, out
             src = xT[c * P * J : (c + 1) * P * J, :].rearrange("(p j) w -> p j w", j=J)
             nc.sync.dma_start(out=x_raw[c, u][:], in_=src[:, 2 * u : 2 * u + 2, :])
 
-        def load_first_layer(e, blocks):
-            for b in blocks:
+        def load_first_layer(e, places=range(BLOCKS)):
+            for b in [ORDER[e][i] for i in places]:
                 rows = (w1, w3)[b // KC][e, (b % KC) * P * J : (b % KC + 1) * P * J, :]
                 nc.sync.dma_start(out=raw_set[e][b][:], in_=rows.rearrange("(p j) w -> p (j w)", j=J))
 
@@ -114,26 +125,19 @@ def tile_moe_shr_glu_relu_kernel(tc, xT, w1, w3, w2, gate, offs, pos1, pos2, out
         def pair_tokens(c, u, copy):
             copy(out=pair_plane(c, u, T).rearrange("p (n i e) -> p n e i", i=4, e=2), in_=x_raw[c, u][:].rearrange("p e (n i) -> p n e i", i=4))
 
-        def gather(e, experts, c, u, words):
-            count = experts * C
-            first = (2 * c + u) * count
-            window = pair_plane(c, u, WINDOW if experts == EARLY else T).bitcast(U32)
-            nc.vector.tensor_copy(words.bitcast(U32)[:, first : first + count], window.indirect(offs_t[:, e * C // 16 : (e * C + count) // 16]))
+        def gather(batch, c, u):
+            window = pair_plane(c, u, WINDOW).bitcast(U32)
+            first = (2 * c + u) * S
+            nc.vector.tensor_copy(words[batch][:].bitcast(U32)[:, first : first + S], window.indirect(offs_t[:, batch * S // 16 : (batch + 1) * S // 16]))
 
-        def weave_early_slots():
+        def weave_slots(batch):
             nc.vector.tensor_copy(
-                out=woven[:].bitcast(I32).rearrange("p (e c n u) -> p e c n u", e=EARLY, c=KC, u=2),
-                in_=early_words[:].bitcast(I32).rearrange("p (c u e n) -> p e c n u", c=KC, u=2, e=EARLY),
+                out=woven[batch][:].bitcast(I32).rearrange("p (c n u) -> p c n u", c=KC, u=2),
+                in_=words[batch][:].bitcast(I32).rearrange("p (c u n) -> p c n u", c=KC, u=2),
             )
 
-        def woven_slots(e):
-            return woven[:, (e % EARLY) * KC * C * J : (e % EARLY + 1) * KC * C * J]
-
-        def weave_slots(e):
-            nc.gpsimd.tensor_copy(
-                out=woven_slots(e).bitcast(I32).rearrange("p (c n u) -> p c n u", c=KC, u=2),
-                in_=rounded[BLOCKS - 1].bitcast(I32).rearrange("p (c u n) -> p c n u", c=KC, u=2),
-            )
+        def quantise_slots(batch):
+            quantise(slot_mx[batch], slice(0, KC * S), woven[batch][:].bitcast(BF16))
 
         def weave_all_tokens():
             nc.vector.tensor_copy(
@@ -144,39 +148,45 @@ def tile_moe_shr_glu_relu_kernel(tc, xT, w1, w3, w2, gate, offs, pos1, pos2, out
         def round_block(e, b):
             dst = rounded[b].rearrange("p (t m j) -> p m j t", t=J, j=J)
             src = raw_set[e][b][:].rearrange("p (j m t) -> p m j t", j=J, t=J)
-            share = (EIGHTHS_SHARED if e == SHARED else EIGHTHS_LAST if e == LAST else EIGHTHS_GATHERING)[b] * P // 8
-            nc.scalar.copy(out=dst[:, share:], in_=src[:, share:])
+            share = SHARES[e][b] * P // 8
+            if share < P:
+                nc.scalar.copy(out=dst[:, share:], in_=src[:, share:])
             if share > 0:
                 nc.vector.tensor_copy(out=dst[:, :share], in_=src[:, :share])
 
         def quantise_block(b):
             quantise(w_mx[b // KC], slice((b % KC) * H, (b % KC + 1) * H), rounded[b])
 
+        def quantise_layer(layer):
+            quantise(w_mx[layer], slice(0, KC * H), rounded_layer[layer][:])
+
         def round_w2(e, copy):
             copy(
-                out=rounded2[:, e * N * J : (e + 1) * N * J].rearrange("p (n i j) -> p n j i", i=2, j=J),
+                out=second_in[:, w2_at[e] * J : (w2_at[e] + N) * J].rearrange("p (n i j) -> p n j i", i=2, j=J),
                 in_=raw2[e].rearrange("p (j n i) -> p n j i", j=J, i=2),
             )
 
-        def quantise_w2(e, count):
-            quantise(w2_mx, slice(e * N, (e + count) * N), rounded2[:, e * N * J : (e + count) * N * J])
+        def quantise_second(first, width):
+            quantise(second_mx, slice(first, first + width), second_in[:, first * J : (first + width) * J])
 
         def first_bank(e, layer, g):
-            return banks[4 * layer + g + (0 if e == SHARED else 2 * (e % 2))]
+            if e == SHARED:
+                return banks[g if layer == 0 else (4 + g if g < 2 else g - 2)]
+            return banks[4 * layer + g + 2 * (e % 2)]
 
         def first_layer(e, b, g):
             layer, c = divmod(b, KC)
-            tokens, width = (all_mx, T) if e == SHARED else (slot_mx[e], C)
-            cols = slice(c * width + g * G, c * width + (g + 1) * G)
+            tokens, first = (all_mx, c * T) if e == SHARED else (slot_mx[e // EARLY], c * S + (e % EARLY) * C)
+            cols = slice(first + g * G, first + (g + 1) * G)
             for t in range(J):
                 acc = first_bank(e, layer, g)[:, t * G : (t + 1) * G]
                 matmul(acc, w_mx[layer], slice(c * H + t * P, c * H + (t + 1) * P), tokens, cols, c == 0 and t == 0, c == KC - 1 and t == J - 1)
 
         def relu_tile(e, g):
             if e == SHARED:
-                room = raw_set[e][BLOCKS - 1] if g < 2 else raw2[SHARED]
+                room = raw_set[e][BLOCKS - 1]
             else:
-                room = raw_set[e + 1][0] if e < LAST else raw_set[e][BLOCKS - 1]
+                room = relu_sb if RELU_AT[e] is None else raw_at(RELU_AT[e])
             return room[:, (g % 2) * G * J : (g % 2 + 1) * G * J].rearrange("p (n t i) -> p n t i", t=J, i=2)
 
         def in_pairs(bank):
@@ -185,18 +195,21 @@ def tile_moe_shr_glu_relu_kernel(tc, xT, w1, w3, w2, gate, offs, pos1, pos2, out
         def relu(e, g):
             nc.scalar.activation(out=relu_tile(e, g), in_=in_pairs(first_bank(e, 0, g)), func=RELU)
 
+        def hidden_of(e):
+            return hidden if e == SHARED else hidden[:, (e % 2) * C * J :]
+
         def gated(e, g):
-            h = hidden[:, g * G * J : (g + 1) * G * J].rearrange("p (n i t) -> p n t i", t=J, i=2)
+            h = hidden_of(e)[:, g * G * J : (g + 1) * G * J].rearrange("p (n i t) -> p n t i", t=J, i=2)
             nc.vector.tensor_tensor(out=h, in0=in_pairs(first_bank(e, 1, g)), in1=relu_tile(e, g), op=MULT)
 
         def quantise_hidden(e, lo, hi):
-            quantise(h_mx[e], slice(lo, hi), hidden[:, lo * J : hi * J])
+            quantise(h_mx[e // 2], slice(lo, hi), hidden[:, lo * J : hi * J])
 
-        def second_layer(e, sums, lo, hi, halves):
+        def second_layer(e, sums, lo, hi, halves=range(2)):
             for half in halves:
-                matmul(sums[half], w2_mx, slice(e * N + half * P, e * N + (half + 1) * P), h_mx[e], slice(lo, hi), True, True)
+                matmul(sums[half], second_mx, slice(w2_at[e] + half * P, w2_at[e] + (half + 1) * P), h_mx[e // 2], slice(lo, hi), True, True)
 
-        sums_at = {(0, 0): (0, 0), (1, 0): (0, C), (0, 1): (1, 0), (1, 1): (1, C), (2, 0): (4, 0), (3, 0): (5, 0), (2, 1): (2, 0), (3, 1): (2, C)}
+        sums_at = {(0, 0): (0, 0), (1, 0): (0, C), (0, 1): (1, 0), (1, 1): (1, C), (2, 0): (4, 0), (3, 0): (4, C), (2, 1): (5, 0), (3, 1): (5, C)}
 
         def slot_sums(e, half):
             bank, first = sums_at[e, half]
@@ -206,15 +219,15 @@ def tile_moe_shr_glu_relu_kernel(tc, xT, w1, w3, w2, gate, offs, pos1, pos2, out
             bank, first = sums_at[e, half]
             copy(out=y_sb[half][:, e * C : (e + count) * C], in_=banks[bank][:, first : first + count * C])
 
-        term = [[raw[1][2][:, 0:T], raw[1][2][:, T : 2 * T]], [raw[1][3][:, 0:T], raw_set[SHARED][1][:, 0:T]]]
+        term = [raw[1][2 + r][:, 0 : 2 * T].rearrange("p (h n) -> p h n", h=2) for r in range(2)]
         combined = raw_set[SHARED][BLOCKS - 1][:, 2 * T :].rearrange("p (h n) -> p h n", h=2)
 
         def pick(r, half):
-            nc.vector.tensor_tensor(out=term[r][half], in0=y_sb[half][:].indirect(pos_t[r][:]), in1=gates[r][:], op=MULT)
+            nc.vector.tensor_tensor(out=term[r][:, half, :], in0=y_sb[half][:].indirect(pos_t[r][:]), in1=gates[r][:], op=MULT)
 
         def shared_second_layer(bank, lo, hi):
             quantise_hidden(SHARED, lo, hi)
-            second_layer(SHARED, [bank[:, half * (hi - lo) : (half + 1) * (hi - lo)] for half in range(2)], lo, hi, range(2))
+            second_layer(SHARED, [bank[:, half * (hi - lo) : (half + 1) * (hi - lo)] for half in range(2)], lo, hi)
 
         def finish(bank, lo, hi):
             result = raw_set[SHARED][2][:, 2 * lo : 2 * hi].rearrange("p (h n) -> p h n", h=2)
@@ -223,16 +236,18 @@ def tile_moe_shr_glu_relu_kernel(tc, xT, w1, w3, w2, gate, offs, pos1, pos2, out
 
         load_x(*planes[0])
         nc.sync.dma_start(offs_t[:], offs)
-        nc.sync.dma_start(out=gate_row[:], in_=gate[:, 0, :].rearrange("r (p m) -> p r m", m=J))
-        for c, u in planes[1:]:
-            load_x(c, u)
+        for i in range(1, 5):
+            if i == GATE_AT:
+                nc.sync.dma_start(out=gate_row[:], in_=gate[:, 0, :].rearrange("r (p m) -> p r m", m=J))
+            if i < 4:
+                load_x(*planes[i])
         for e in range(len(raw)):
-            load_first_layer(e, range(BLOCKS))
+            load_first_layer(e)
 
         nc.gpsimd.memset(x_pair[:, 4 * T * 2 :], 0.0)
         for c, u in planes:
-            pair_tokens(c, u, nc.vector.tensor_copy if c == KC - 1 else nc.scalar.copy)
-            gather(0, EARLY, c, u, early_words[:])
+            pair_tokens(c, u, nc.vector.tensor_copy if planes.index((c, u)) < VPAIRS else nc.scalar.copy)
+            gather(0, c, u)
 
         make_identity(nc, identity[:])
         for r in range(2):
@@ -241,94 +256,98 @@ def tile_moe_shr_glu_relu_kernel(tc, xT, w1, w3, w2, gate, offs, pos1, pos2, out
                 nc.tensor.transpose(bank[:, m * P : (m + 1) * P], gate_row[:, r, m : m + 1].to_broadcast([P, P]), identity[:])
             nc.scalar.copy(out=gates[r][:].rearrange("p (n m) -> p n m", m=J), in_=bank[:].rearrange("p (m n) -> p n m", m=J))
 
-        weave_early_slots()
         weave_all_tokens()
-        quantise(early_mx, slice(0, EARLY * KC * C), woven[:])
+        weave_slots(0)
         quantise(all_mx, slice(0, KC * T), all_woven[:])
+        quantise_slots(0)
 
         groups = range(C // G)
         for e in range(E):
-            for b in range(BLOCKS):
+            for i, b in enumerate(ORDER[e]):
+                layer, c = divmod(b, KC)
                 round_block(e, b)
-                if e > 0 and b == 0:
+                if e > 0 and RELU_AT[e - 1] == (e, i):
                     for g in groups:
                         relu(e - 1, g)
-                if e > 0 and b == 1:
-                    quantise_hidden(e - 1, 0, C)
-                quantise_block(b)
-                if e > 0 and b == 0:
+                if MERGED[e][layer]:
+                    if c == KC - 1:
+                        quantise_layer(layer)
+                        for g in groups:
+                            first_layer(e, b - 1, g)
+                            first_layer(e, b, g)
+                else:
+                    quantise_block(b)
+                    for g in groups:
+                        first_layer(e, b, g)
+                if e > 0 and i == (RELU_AT[e - 1][1] if RELU_AT[e - 1] is not None and RELU_AT[e - 1][0] == e else 0):
                     for g in groups:
                         gated(e - 1, g)
-                if EARLY <= e + 1 < E and b == 1:
-                    quantise(slot_mx[e + 1], slice(0, KC * C), woven_slots(e + 1))
-                for g in groups:
-                    first_layer(e, b, g)
-            if e + EARLY < E:
-                for c, u in planes:
-                    gather(e + EARLY, 1, c, u, rounded[BLOCKS - 1])
-                weave_slots(e + EARLY)
-            if e == 0:
-                load_first_layer(LAST, range(BLOCKS))
+                    if e == 2:
+                        quantise_hidden(0, 0, T)
+                if e == LAST and i == 2:
+                    load_first_layer(SHARED, [2])
+                    nc.sync.dma_start(pos_t[1][:], pos2)
+                    load_first_layer(SHARED, [3])
+                if i == BLOCKS - 1 and (RELU_AT[e] is None or RELU_AT[e][0] == e) and e < LAST:
+                    for g in groups:
+                        relu(e, g)
+                if WORDS_AT == (e, i):
+                    for plane in planes:
+                        gather(1, *plane)
+                if WOVEN_AT == (e, i):
+                    weave_slots(1)
+                    quantise_slots(1)
             if e == 1:
+                load_first_layer(LAST)
                 for routed in range(E):
                     load_w2(routed)
             if e == 2:
-                load_first_layer(SHARED, [0])
+                load_first_layer(SHARED, [0, 1])
                 nc.sync.dma_start(pos_t[0][:], pos1)
-                load_first_layer(SHARED, [1])
-                nc.sync.dma_start(pos_t[1][:], pos2)
-                load_first_layer(SHARED, [2, 3])
 
         for g in groups:
             relu(LAST, g)
         round_w2(0, nc.vector.tensor_copy)
-        quantise_w2(0, 1)
         for g in groups:
             gated(LAST, g)
         load_w2(SHARED)
         round_w2(1, nc.scalar.copy)
-        quantise_w2(1, 1)
-        quantise_hidden(LAST, 0, C)
+        quantise_second(0, 2 * N)
         round_w2(2, nc.scalar.copy)
         round_w2(LAST, nc.vector.tensor_copy)
-        quantise_w2(2, 2)
+        quantise_second(2 * N, 2 * N + T)
         for pair in range(2):
             for half in range(2):
                 for e in (2 * pair, 2 * pair + 1):
-                    second_layer(e, [slot_sums(e, 0), slot_sums(e, 1)], 0, C, [half])
-        store_slots(0, 2, 0, nc.scalar.copy)
-        store_slots(0, 2, 1, nc.scalar.copy)
-        store_slots(2, 1, 0, nc.scalar.copy)
-        store_slots(3, 1, 0, nc.vector.tensor_copy)
-        store_slots(2, 2, 1, nc.scalar.copy)
+                    second_layer(e, [slot_sums(e, 0), slot_sums(e, 1)], (e % 2) * C, (e % 2 + 1) * C, [half])
+        for pair in range(2):
+            for half in range(2):
+                store_slots(2 * pair, 2, half, nc.scalar.copy)
 
         groups = range(T // G)
         for b in range(BLOCKS):
             round_block(SHARED, b)
-            if b == 0:
-                pick(0, 0)
-                pick(0, 1)
-            if b == 1:
-                pick(1, 0)
+            if b in (1, 2):
+                pick(b - 1, 0)
+                pick(b - 1, 1)
             quantise_block(b)
-            if b == 1:
-                pick(1, 1)
-            for g in groups:
+            for g in groups if b < KC else range(2):
                 first_layer(SHARED, b, g)
-        relu(SHARED, 0)
-        relu(SHARED, 1)
+        for g in range(2):
+            relu(SHARED, g)
+            first_layer(SHARED, 2, 2 + g)
+            first_layer(SHARED, 3, 2 + g)
         round_w2(SHARED, nc.scalar.copy)
-        relu(SHARED, 2)
-        relu(SHARED, 3)
-        for half in range(2):
-            nc.vector.tensor_add(out=combined[:, half, :], in0=term[0][half], in1=term[1][half])
+        nc.vector.tensor_add(out=combined, in0=term[0], in1=term[1])
 
-        pieces = [(banks[0], 0, 2 * G), (banks[1], 2 * G, 3 * G), (banks[4], 3 * G, 4 * G)]
+        pieces = [(banks[6], 0, 2 * G), (banks[7], 2 * G, 3 * G), (banks[4], 3 * G, 4 * G)]
         gated(SHARED, 0)
         gated(SHARED, 1)
-        quantise_w2(SHARED, 1)
-        gated(SHARED, 2)
+        relu(SHARED, 2)
+        relu(SHARED, 3)
+        quantise_second(w2_at[SHARED], N)
         shared_second_layer(*pieces[0])
+        gated(SHARED, 2)
         gated(SHARED, 3)
         for piece in pieces[1:]:
             shared_second_layer(*piece)

@@ -24,23 +24,17 @@ G = 128
 BLOCKS = 2 * KC
 SHARED = E
 LAST = E - 1
-EARLY = 2
+BATCH = 2
+S = BATCH * C
 WINDOW = 704
+ROUTED_ORDER = (0, 2, 1, 3)
 
-SHARES = [(0, 0, 0, 0), (0, 0, 8, 0), (8, 0, 4, 4), (8, 4, 0, 4), (8, 0, 0, 2)]
-ORDER = [(0, 2, 1, 3), (0, 2, 1, 3), (0, 2, 1, 3), (0, 2, 1, 3), (0, 1, 2, 3)]
-MERGED = [(0, 1), (0, 1), (0, 1), (0, 0), (0, 0)]
-RELU_AT = [(1, 0), None, None, (3, 3)]
-HID_AT = [None, None, None]
-VPAIRS = 1
-WORDS_AT = (0, 1)
-WOVEN_AT = (0, 3)
-GATE_AT = 4
+LATE_SHARE = 64
+FINAL_SHARE = 32
 
 
 def tile_moe_shr_glu_relu_kernel(tc, xT, w1, w3, w2, gate, offs, pos1, pos2, out):
     nc = tc.nc
-    assert WORDS_AT < WOVEN_AT and WORDS_AT not in RELU_AT and WOVEN_AT not in RELU_AT
     with ExitStack() as ctx:
         keep = ctx.enter_context(tc.tile_pool(name="keep", bufs=1))
         twice = ctx.enter_context(tc.tile_pool(name="twice", bufs=1))
@@ -80,23 +74,18 @@ def tile_moe_shr_glu_relu_kernel(tc, xT, w1, w3, w2, gate, offs, pos1, pos2, out
         rounded_layer = [sbuf("rounded_layer%d" % layer, [P, KC * H * J], BF16) for layer in range(2)]
         rounded = [rounded_layer[b // KC][:, (b % KC) * H * J : (b % KC + 1) * H * J] for b in range(BLOCKS)]
         relu_sb = sbuf("relu_sb", [P, C * J], F32)
-
-        def raw_at(at):
-            return raw_set[at[0]][ORDER[at[0]][at[1]]]
-
         w_mx = [mx_tiles("w%d" % layer, KC * H) for layer in range(2)]
 
-        last_w2 = twice.tile([P, 2 * J * N], F32, name="last_w2", offset=0)
+        scalar_w2 = twice.tile([P, 2 * J * N], F32, name="scalar_w2", offset=0)
         y_sb = [twice.tile([P, E * C], F32, name="y_sb%d" % half, offset=half * E * C * 4) for half in range(2)]
-        raw2 = [raw[1][1][:, 0 : J * N], last_w2[:, 0 : J * N], last_w2[:, J * N :], raw[1][1][:, J * N :], raw[0][1][:, 0 : J * N]]
+        raw2 = [raw[1][1][:, 0 : J * N], scalar_w2[:, 0 : J * N], scalar_w2[:, J * N :], raw[1][1][:, J * N :], raw[0][1][:, 0 : J * N]]
         second_in = sbuf("second_in", [P, (E * N + T + N) * J], BF16)
         second_mx = mx_tiles("second", E * N + T + N)
         w2_at = [0, N, 2 * N, 3 * N, E * N + T]
 
-        S = EARLY * C
-        words = [sbuf("early_words", [P, KC * 2 * S], F32), raw_at(WORDS_AT)]
-        woven = [sbuf("early_woven", [P, KC * 2 * S], F32), raw_at(WOVEN_AT)]
-        slot_mx = [mx_tiles("slots%d" % i, KC * S) for i in range(2)]
+        words = [sbuf("early_words", [P, KC * 2 * S], F32), raw[0][2]]
+        woven = [sbuf("early_woven", [P, KC * 2 * S], F32), raw[0][3]]
+        slot_mx = [mx_tiles("slots%d" % batch, KC * S) for batch in range(E // BATCH)]
         all_woven = sbuf("all_woven", [P, KC * T * J], BF16)
         all_mx = mx_tiles("all", KC * T)
 
@@ -110,8 +99,8 @@ def tile_moe_shr_glu_relu_kernel(tc, xT, w1, w3, w2, gate, offs, pos1, pos2, out
             src = xT[c * P * J : (c + 1) * P * J, :].rearrange("(p j) w -> p j w", j=J)
             nc.sync.dma_start(out=x_raw[c, u][:], in_=src[:, 2 * u : 2 * u + 2, :])
 
-        def load_first_layer(e, places=range(BLOCKS)):
-            for b in [ORDER[e][i] for i in places]:
+        def load_first_layer(e, blocks):
+            for b in blocks:
                 rows = (w1, w3)[b // KC][e, (b % KC) * P * J : (b % KC + 1) * P * J, :]
                 nc.sync.dma_start(out=raw_set[e][b][:], in_=rows.rearrange("(p j) w -> p (j w)", j=J))
 
@@ -145,10 +134,17 @@ def tile_moe_shr_glu_relu_kernel(tc, xT, w1, w3, w2, gate, offs, pos1, pos2, out
                 in_=x_pair[:, 0 : 4 * T * 2].bitcast(I32).rearrange("p (c u n) -> p c n u", c=KC, u=2),
             )
 
+        def vector_share(e, b):
+            if e > 0 and b == 0:
+                return P
+            if e == SHARED:
+                return FINAL_SHARE if b == BLOCKS - 1 else 0
+            return LATE_SHARE if e >= BATCH and b >= KC else 0
+
         def round_block(e, b):
             dst = rounded[b].rearrange("p (t m j) -> p m j t", t=J, j=J)
             src = raw_set[e][b][:].rearrange("p (j m t) -> p m j t", j=J, t=J)
-            share = SHARES[e][b] * P // 8
+            share = vector_share(e, b)
             if share < P:
                 nc.scalar.copy(out=dst[:, share:], in_=src[:, share:])
             if share > 0:
@@ -156,9 +152,6 @@ def tile_moe_shr_glu_relu_kernel(tc, xT, w1, w3, w2, gate, offs, pos1, pos2, out
 
         def quantise_block(b):
             quantise(w_mx[b // KC], slice((b % KC) * H, (b % KC + 1) * H), rounded[b])
-
-        def quantise_layer(layer):
-            quantise(w_mx[layer], slice(0, KC * H), rounded_layer[layer][:])
 
         def round_w2(e, copy):
             copy(
@@ -176,17 +169,14 @@ def tile_moe_shr_glu_relu_kernel(tc, xT, w1, w3, w2, gate, offs, pos1, pos2, out
 
         def first_layer(e, b, g):
             layer, c = divmod(b, KC)
-            tokens, first = (all_mx, c * T) if e == SHARED else (slot_mx[e // EARLY], c * S + (e % EARLY) * C)
+            tokens, first = (all_mx, c * T) if e == SHARED else (slot_mx[e // BATCH], c * S + (e % BATCH) * C)
             cols = slice(first + g * G, first + (g + 1) * G)
             for t in range(J):
                 acc = first_bank(e, layer, g)[:, t * G : (t + 1) * G]
                 matmul(acc, w_mx[layer], slice(c * H + t * P, c * H + (t + 1) * P), tokens, cols, c == 0 and t == 0, c == KC - 1 and t == J - 1)
 
         def relu_tile(e, g):
-            if e == SHARED:
-                room = raw_set[e][BLOCKS - 1]
-            else:
-                room = relu_sb if RELU_AT[e] is None else raw_at(RELU_AT[e])
+            room = raw_set[e][BLOCKS - 1] if e > 0 else relu_sb
             return room[:, (g % 2) * G * J : (g % 2 + 1) * G * J].rearrange("p (n t i) -> p n t i", t=J, i=2)
 
         def in_pairs(bank):
@@ -196,28 +186,20 @@ def tile_moe_shr_glu_relu_kernel(tc, xT, w1, w3, w2, gate, offs, pos1, pos2, out
             nc.scalar.activation(out=relu_tile(e, g), in_=in_pairs(first_bank(e, 0, g)), func=RELU)
 
         def hidden_of(e):
-            return hidden if e == SHARED else hidden[:, (e % 2) * C * J :]
+            return hidden if e == SHARED else hidden[:, (e % BATCH) * C * J :]
 
         def gated(e, g):
             h = hidden_of(e)[:, g * G * J : (g + 1) * G * J].rearrange("p (n i t) -> p n t i", t=J, i=2)
             nc.vector.tensor_tensor(out=h, in0=in_pairs(first_bank(e, 1, g)), in1=relu_tile(e, g), op=MULT)
 
         def quantise_hidden(e, lo, hi):
-            quantise(h_mx[e // 2], slice(lo, hi), hidden[:, lo * J : hi * J])
+            quantise(h_mx[e // BATCH], slice(lo, hi), hidden[:, lo * J : hi * J])
 
-        def second_layer(e, sums, lo, hi, halves=range(2)):
-            for half in halves:
-                matmul(sums[half], second_mx, slice(w2_at[e] + half * P, w2_at[e] + (half + 1) * P), h_mx[e // 2], slice(lo, hi), True, True)
+        def second_layer(e, half, acc, lo, hi):
+            matmul(acc, second_mx, slice(w2_at[e] + half * P, w2_at[e] + (half + 1) * P), h_mx[e // BATCH], slice(lo, hi), True, True)
 
-        sums_at = {(0, 0): (0, 0), (1, 0): (0, C), (0, 1): (1, 0), (1, 1): (1, C), (2, 0): (4, 0), (3, 0): (4, C), (2, 1): (5, 0), (3, 1): (5, C)}
-
-        def slot_sums(e, half):
-            bank, first = sums_at[e, half]
-            return banks[bank][:, first : first + C]
-
-        def store_slots(e, count, half, copy):
-            bank, first = sums_at[e, half]
-            copy(out=y_sb[half][:, e * C : (e + count) * C], in_=banks[bank][:, first : first + count * C])
+        def slot_bank(batch, half):
+            return banks[4 * batch + half]
 
         term = [raw[1][2 + r][:, 0 : 2 * T].rearrange("p (h n) -> p h n", h=2) for r in range(2)]
         combined = raw_set[SHARED][BLOCKS - 1][:, 2 * T :].rearrange("p (h n) -> p h n", h=2)
@@ -227,7 +209,8 @@ def tile_moe_shr_glu_relu_kernel(tc, xT, w1, w3, w2, gate, offs, pos1, pos2, out
 
         def shared_second_layer(bank, lo, hi):
             quantise_hidden(SHARED, lo, hi)
-            second_layer(SHARED, [bank[:, half * (hi - lo) : (half + 1) * (hi - lo)] for half in range(2)], lo, hi)
+            for half in range(2):
+                second_layer(SHARED, half, bank[:, half * (hi - lo) : (half + 1) * (hi - lo)], lo, hi)
 
         def finish(bank, lo, hi):
             result = raw_set[SHARED][2][:, 2 * lo : 2 * hi].rearrange("p (h n) -> p h n", h=2)
@@ -236,17 +219,15 @@ def tile_moe_shr_glu_relu_kernel(tc, xT, w1, w3, w2, gate, offs, pos1, pos2, out
 
         load_x(*planes[0])
         nc.sync.dma_start(offs_t[:], offs)
-        for i in range(1, 5):
-            if i == GATE_AT:
-                nc.sync.dma_start(out=gate_row[:], in_=gate[:, 0, :].rearrange("r (p m) -> p r m", m=J))
-            if i < 4:
-                load_x(*planes[i])
+        for plane in planes[1:]:
+            load_x(*plane)
+        nc.sync.dma_start(out=gate_row[:], in_=gate[:, 0, :].rearrange("r (p m) -> p r m", m=J))
         for e in range(len(raw)):
-            load_first_layer(e)
+            load_first_layer(e, ROUTED_ORDER)
 
         nc.gpsimd.memset(x_pair[:, 4 * T * 2 :], 0.0)
         for c, u in planes:
-            pair_tokens(c, u, nc.vector.tensor_copy if planes.index((c, u)) < VPAIRS else nc.scalar.copy)
+            pair_tokens(c, u, nc.vector.tensor_copy if (c, u) == planes[0] else nc.scalar.copy)
             gather(0, c, u)
 
         make_identity(nc, identity[:])
@@ -263,42 +244,37 @@ def tile_moe_shr_glu_relu_kernel(tc, xT, w1, w3, w2, gate, offs, pos1, pos2, out
 
         groups = range(C // G)
         for e in range(E):
-            for i, b in enumerate(ORDER[e]):
-                layer, c = divmod(b, KC)
+            for b in ROUTED_ORDER:
                 round_block(e, b)
-                if e > 0 and RELU_AT[e - 1] == (e, i):
-                    for g in groups:
-                        relu(e - 1, g)
-                if MERGED[e][layer]:
-                    if c == KC - 1:
-                        quantise_layer(layer)
-                        for g in groups:
-                            first_layer(e, b - 1, g)
-                            first_layer(e, b, g)
-                else:
+                if b < KC or e == LAST:
                     quantise_block(b)
                     for g in groups:
                         first_layer(e, b, g)
-                if e > 0 and i == (RELU_AT[e - 1][1] if RELU_AT[e - 1] is not None and RELU_AT[e - 1][0] == e else 0):
+                elif b == BLOCKS - 1:
+                    quantise(w_mx[1], slice(0, KC * H), rounded_layer[1][:])
+                    for g in groups:
+                        first_layer(e, b - 1, g)
+                        first_layer(e, b, g)
+                if e > 0 and b == 0:
                     for g in groups:
                         gated(e - 1, g)
-                    if e == 2:
-                        quantise_hidden(0, 0, T)
-                if e == LAST and i == 2:
+                    if e == BATCH:
+                        quantise_hidden(0, 0, S)
+                if (e, b) == (LAST, 1):
                     load_first_layer(SHARED, [2])
                     nc.sync.dma_start(pos_t[1][:], pos2)
                     load_first_layer(SHARED, [3])
-                if i == BLOCKS - 1 and (RELU_AT[e] is None or RELU_AT[e][0] == e) and e < LAST:
+                if e < LAST and b == BLOCKS - 1:
                     for g in groups:
                         relu(e, g)
-                if WORDS_AT == (e, i):
+                if (e, b) == (0, 2):
                     for plane in planes:
                         gather(1, *plane)
-                if WOVEN_AT == (e, i):
+                if (e, b) == (0, 3):
                     weave_slots(1)
                     quantise_slots(1)
             if e == 1:
-                load_first_layer(LAST)
+                load_first_layer(LAST, ROUTED_ORDER)
                 for routed in range(E):
                     load_w2(routed)
             if e == 2:
@@ -316,13 +292,13 @@ def tile_moe_shr_glu_relu_kernel(tc, xT, w1, w3, w2, gate, offs, pos1, pos2, out
         round_w2(2, nc.scalar.copy)
         round_w2(LAST, nc.vector.tensor_copy)
         quantise_second(2 * N, 2 * N + T)
-        for pair in range(2):
+        for batch in range(E // BATCH):
             for half in range(2):
-                for e in (2 * pair, 2 * pair + 1):
-                    second_layer(e, [slot_sums(e, 0), slot_sums(e, 1)], (e % 2) * C, (e % 2 + 1) * C, [half])
-        for pair in range(2):
+                for i in range(BATCH):
+                    second_layer(BATCH * batch + i, half, slot_bank(batch, half)[:, i * C : (i + 1) * C], i * C, (i + 1) * C)
+        for batch in range(E // BATCH):
             for half in range(2):
-                store_slots(2 * pair, 2, half, nc.scalar.copy)
+                nc.scalar.copy(out=y_sb[half][:, batch * S : (batch + 1) * S], in_=slot_bank(batch, half)[:])
 
         groups = range(T // G)
         for b in range(BLOCKS):

@@ -27,7 +27,6 @@ LAST = E - 1
 BATCH = 2
 S = BATCH * C
 WINDOW = 704
-ROUTED_ORDER = (0, 2, 1, 3)
 
 LATE_SHARE = 64
 FINAL_SHARE = 32
@@ -83,7 +82,7 @@ def tile_moe_shr_glu_relu_kernel(tc, xT, w1, w3, w2, gate, offs, pos1, pos2, out
         second_mx = mx_tiles("second", E * N + T + N)
         w2_at = [0, N, 2 * N, 3 * N, E * N + T]
 
-        words = [sbuf("early_words", [P, KC * 2 * S], F32), raw[0][2]]
+        words = [sbuf("early_words", [P, KC * 2 * S], F32), raw[0][1]]
         woven = [sbuf("early_woven", [P, KC * 2 * S], F32), raw[0][3]]
         slot_mx = [mx_tiles("slots%d" % batch, KC * S) for batch in range(E // BATCH)]
         all_woven = sbuf("all_woven", [P, KC * T * J], BF16)
@@ -223,7 +222,7 @@ def tile_moe_shr_glu_relu_kernel(tc, xT, w1, w3, w2, gate, offs, pos1, pos2, out
             load_x(*plane)
         nc.sync.dma_start(out=gate_row[:], in_=gate[:, 0, :].rearrange("r (p m) -> p r m", m=J))
         for e in range(len(raw)):
-            load_first_layer(e, ROUTED_ORDER)
+            load_first_layer(e, range(BLOCKS))
 
         nc.gpsimd.memset(x_pair[:, 4 * T * 2 :], 0.0)
         for c, u in planes:
@@ -244,7 +243,7 @@ def tile_moe_shr_glu_relu_kernel(tc, xT, w1, w3, w2, gate, offs, pos1, pos2, out
 
         groups = range(C // G)
         for e in range(E):
-            for b in ROUTED_ORDER:
+            for b in range(BLOCKS):
                 round_block(e, b)
                 if b < KC or e == LAST:
                     quantise_block(b)
@@ -267,14 +266,14 @@ def tile_moe_shr_glu_relu_kernel(tc, xT, w1, w3, w2, gate, offs, pos1, pos2, out
                 if e < LAST and b == BLOCKS - 1:
                     for g in groups:
                         relu(e, g)
-                if (e, b) == (0, 2):
+                if (e, b) == (0, 1):
                     for plane in planes:
                         gather(1, *plane)
                 if (e, b) == (0, 3):
                     weave_slots(1)
                     quantise_slots(1)
             if e == 1:
-                load_first_layer(LAST, ROUTED_ORDER)
+                load_first_layer(LAST, range(BLOCKS))
                 for routed in range(E):
                     load_w2(routed)
             if e == 2:

@@ -15,6 +15,7 @@ U16 = mybir.dt.uint16
 U8 = mybir.dt.uint8
 FP8X4 = mybir.dt.float8_e4m3fn_x4
 MULT = mybir.AluOpType.mult
+ADD = mybir.AluOpType.add
 RELU = mybir.ActivationFunctionType.Relu
 
 P = 128
@@ -28,8 +29,9 @@ BATCH = 2
 S = BATCH * C
 WINDOW = 704
 
-LATE_SHARE = 64
-FINAL_SHARE = 32
+HALF_SHARE = 64
+FINAL_SHARE = 40
+LAST_SHARE = 76
 
 
 def tile_moe_shr_glu_relu_kernel(tc, xT, w1, w3, w2, gate, offs, pos1, pos2, out):
@@ -64,7 +66,8 @@ def tile_moe_shr_glu_relu_kernel(tc, xT, w1, w3, w2, gate, offs, pos1, pos2, out
         banks = [psum.tile([P, 512], F32, name="bank%d" % b) for b in range(8)]
 
         planes = [(c, u) for c in reversed(range(KC)) for u in reversed(range(2))]
-        x_raw = dict([(cu, sbuf("x_raw%d%d" % cu, [P, 2, T], F32)) for cu in planes])
+        x_all = sbuf("x_all", [P, KC * 2 * 2 * T], F32)
+        x_raw = dict([((c, u), x_all[:, (2 * c + u) * 2 * T : (2 * c + u + 1) * 2 * T].rearrange("p (e n) -> p e n", e=2)) for c, u in planes])
         x_pair = sbuf("x_pair", [P, (3 * T + WINDOW) * 2], BF16)
 
         raw = [[sbuf("raw%d%d" % (s, b), [P, J * H], F32) for b in range(BLOCKS)] for s in range(3)]
@@ -72,7 +75,6 @@ def tile_moe_shr_glu_relu_kernel(tc, xT, w1, w3, w2, gate, offs, pos1, pos2, out
 
         rounded_layer = [sbuf("rounded_layer%d" % layer, [P, KC * H * J], BF16) for layer in range(2)]
         rounded = [rounded_layer[b // KC][:, (b % KC) * H * J : (b % KC + 1) * H * J] for b in range(BLOCKS)]
-        relu_sb = sbuf("relu_sb", [P, C * J], F32)
         w_mx = [mx_tiles("w%d" % layer, KC * H) for layer in range(2)]
 
         scalar_w2 = twice.tile([P, 2 * J * N], F32, name="scalar_w2", offset=0)
@@ -82,8 +84,10 @@ def tile_moe_shr_glu_relu_kernel(tc, xT, w1, w3, w2, gate, offs, pos1, pos2, out
         second_mx = mx_tiles("second", E * N + T + N)
         w2_at = [0, N, 2 * N, 3 * N, E * N + T]
 
-        words = [sbuf("early_words", [P, KC * 2 * S], F32), raw[0][1]]
-        woven = [sbuf("early_woven", [P, KC * 2 * S], F32), raw[0][3]]
+        early_words = sbuf("early_words", [P, KC * 2 * S], F32)
+        late_words = sbuf("late_words", [P, KC * 2 * S], F32)
+        words = [early_words[:].rearrange("p (c u n) -> p c u n", c=KC, u=2), late_words[:].rearrange("p (c u n) -> p c u n", c=KC, u=2)]
+        woven = [sbuf("early_woven", [P, KC * 2 * S], F32), raw[0][1]]
         slot_mx = [mx_tiles("slots%d" % batch, KC * S) for batch in range(E // BATCH)]
         all_woven = sbuf("all_woven", [P, KC * T * J], BF16)
         all_mx = mx_tiles("all", KC * T)
@@ -96,7 +100,7 @@ def tile_moe_shr_glu_relu_kernel(tc, xT, w1, w3, w2, gate, offs, pos1, pos2, out
 
         def load_x(c, u):
             src = xT[c * P * J : (c + 1) * P * J, :].rearrange("(p j) w -> p j w", j=J)
-            nc.sync.dma_start(out=x_raw[c, u][:], in_=src[:, 2 * u : 2 * u + 2, :])
+            nc.sync.dma_start(out=x_raw[c, u], in_=src[:, 2 * u : 2 * u + 2, :])
 
         def load_first_layer(e, blocks):
             for b in blocks:
@@ -111,34 +115,32 @@ def tile_moe_shr_glu_relu_kernel(tc, xT, w1, w3, w2, gate, offs, pos1, pos2, out
             return x_pair[:, first * 2 : (first + width) * 2]
 
         def pair_tokens(c, u, copy):
-            copy(out=pair_plane(c, u, T).rearrange("p (n i e) -> p n e i", i=4, e=2), in_=x_raw[c, u][:].rearrange("p e (n i) -> p n e i", i=4))
+            copy(out=pair_plane(c, u, T).rearrange("p (n i e) -> p n e i", i=4, e=2), in_=x_raw[c, u].rearrange("p e (n i) -> p n e i", i=4))
 
         def gather(batch, c, u):
             window = pair_plane(c, u, WINDOW).bitcast(U32)
-            first = (2 * c + u) * S
-            nc.vector.tensor_copy(words[batch][:].bitcast(U32)[:, first : first + S], window.indirect(offs_t[:, batch * S // 16 : (batch + 1) * S // 16]))
+            nc.vector.tensor_copy(words[batch][:, c, u, :].bitcast(U32), window.indirect(offs_t[:, batch * S // 16 : (batch + 1) * S // 16]))
 
         def weave_slots(batch):
             nc.vector.tensor_copy(
                 out=woven[batch][:].bitcast(I32).rearrange("p (c n u) -> p c n u", c=KC, u=2),
-                in_=words[batch][:].bitcast(I32).rearrange("p (c u n) -> p c n u", c=KC, u=2),
+                in_=words[batch].bitcast(I32).rearrange("p c u n -> p c n u"),
             )
 
         def quantise_slots(batch):
             quantise(slot_mx[batch], slice(0, KC * S), woven[batch][:].bitcast(BF16))
 
-        def weave_all_tokens():
-            nc.vector.tensor_copy(
-                out=all_woven[:].bitcast(I32).rearrange("p (c n u) -> p c n u", c=KC, u=2),
-                in_=x_pair[:, 0 : 4 * T * 2].bitcast(I32).rearrange("p (c u n) -> p c n u", c=KC, u=2),
-            )
+        def round_all_tokens(c):
+            span = slice(c * J * T, (c + 1) * J * T)
+            dst = all_woven[:, span].rearrange("p (n j) -> p n j", j=J)
+            nc.gpsimd.tensor_scalar(out=dst, in0=x_all[:, span].rearrange("p (j n) -> p n j", j=J), scalar1=1.0, scalar2=0.0, op0=MULT, op1=ADD)
 
         def vector_share(e, b):
-            if e > 0 and b == 0:
-                return P
             if e == SHARED:
-                return FINAL_SHARE if b == BLOCKS - 1 else 0
-            return LATE_SHARE if e >= BATCH and b >= KC else 0
+                return P if b == 0 else FINAL_SHARE if b == BLOCKS - 1 else 0
+            if e == LAST and b >= KC:
+                return LAST_SHARE if b == BLOCKS - 1 else HALF_SHARE
+            return P if e > 0 and b % KC == 0 else 0
 
         def round_block(e, b):
             dst = rounded[b].rearrange("p (t m j) -> p m j t", t=J, j=J)
@@ -175,7 +177,7 @@ def tile_moe_shr_glu_relu_kernel(tc, xT, w1, w3, w2, gate, offs, pos1, pos2, out
                 matmul(acc, w_mx[layer], slice(c * H + t * P, c * H + (t + 1) * P), tokens, cols, c == 0 and t == 0, c == KC - 1 and t == J - 1)
 
         def relu_tile(e, g):
-            room = raw_set[e][BLOCKS - 1] if e > 0 else relu_sb
+            room = raw_set[e][BLOCKS - 1]
             return room[:, (g % 2) * G * J : (g % 2 + 1) * G * J].rearrange("p (n t i) -> p n t i", t=J, i=2)
 
         def in_pairs(bank):
@@ -227,7 +229,10 @@ def tile_moe_shr_glu_relu_kernel(tc, xT, w1, w3, w2, gate, offs, pos1, pos2, out
         nc.gpsimd.memset(x_pair[:, 4 * T * 2 :], 0.0)
         for c, u in planes:
             pair_tokens(c, u, nc.vector.tensor_copy if (c, u) == planes[0] else nc.scalar.copy)
-            gather(0, c, u)
+            for batch in range(E // BATCH):
+                gather(batch, c, u)
+            if u == 0:
+                round_all_tokens(c)
 
         make_identity(nc, identity[:])
         for r in range(2):
@@ -236,16 +241,14 @@ def tile_moe_shr_glu_relu_kernel(tc, xT, w1, w3, w2, gate, offs, pos1, pos2, out
                 nc.tensor.transpose(bank[:, m * P : (m + 1) * P], gate_row[:, r, m : m + 1].to_broadcast([P, P]), identity[:])
             nc.scalar.copy(out=gates[r][:].rearrange("p (n m) -> p n m", m=J), in_=bank[:].rearrange("p (m n) -> p n m", m=J))
 
-        weave_all_tokens()
         weave_slots(0)
-        quantise(all_mx, slice(0, KC * T), all_woven[:])
         quantise_slots(0)
 
         groups = range(C // G)
         for e in range(E):
             for b in range(BLOCKS):
                 round_block(e, b)
-                if b < KC or e == LAST:
+                if b < KC or e > 0:
                     quantise_block(b)
                     for g in groups:
                         first_layer(e, b, g)
@@ -259,38 +262,36 @@ def tile_moe_shr_glu_relu_kernel(tc, xT, w1, w3, w2, gate, offs, pos1, pos2, out
                         gated(e - 1, g)
                     if e == BATCH:
                         quantise_hidden(0, 0, S)
+                    if e == LAST:
+                        quantise_hidden(BATCH, 0, C)
                 if (e, b) == (LAST, 1):
-                    load_first_layer(SHARED, [2])
-                    nc.sync.dma_start(pos_t[1][:], pos2)
-                    load_first_layer(SHARED, [3])
-                if e < LAST and b == BLOCKS - 1:
+                    load_first_layer(SHARED, [2, 3])
+                if b == BLOCKS - 1:
                     for g in groups:
                         relu(e, g)
                 if (e, b) == (0, 1):
-                    for plane in planes:
-                        gather(1, *plane)
-                if (e, b) == (0, 3):
                     weave_slots(1)
+                    quantise(all_mx, slice(0, KC * T), all_woven[:])
                     quantise_slots(1)
             if e == 1:
                 load_first_layer(LAST, range(BLOCKS))
                 for routed in range(E):
                     load_w2(routed)
             if e == 2:
-                load_first_layer(SHARED, [0, 1])
-                nc.sync.dma_start(pos_t[0][:], pos1)
+                for r in range(2):
+                    load_first_layer(SHARED, [r])
+                    nc.sync.dma_start(pos_t[r][:], (pos1, pos2)[r])
 
-        for g in groups:
-            relu(LAST, g)
         round_w2(0, nc.vector.tensor_copy)
         for g in groups:
             gated(LAST, g)
+        quantise_hidden(LAST, C, S)
         load_w2(SHARED)
         round_w2(1, nc.scalar.copy)
         quantise_second(0, 2 * N)
         round_w2(2, nc.scalar.copy)
         round_w2(LAST, nc.vector.tensor_copy)
-        quantise_second(2 * N, 2 * N + T)
+        quantise_second(2 * N, 2 * N)
         for batch in range(E // BATCH):
             for half in range(2):
                 for i in range(BATCH):
@@ -302,9 +303,9 @@ def tile_moe_shr_glu_relu_kernel(tc, xT, w1, w3, w2, gate, offs, pos1, pos2, out
         groups = range(T // G)
         for b in range(BLOCKS):
             round_block(SHARED, b)
-            if b in (1, 2):
-                pick(b - 1, 0)
-                pick(b - 1, 1)
+            if b < 2:
+                pick(b, 0)
+                pick(b, 1)
             quantise_block(b)
             for g in groups if b < KC else range(2):
                 first_layer(SHARED, b, g)

@@ -27,6 +27,7 @@ SHARED = E
 LAST = E - 1
 BATCH = 2
 S = BATCH * C
+GATE_RUN = 2 * T // P
 WINDOW = 704
 
 HALF_SHARE = 64
@@ -94,8 +95,8 @@ def tile_moe_shr_glu_relu_kernel(tc, xT, w1, w3, w2, gate, offs, pos1, pos2, out
 
         hidden = second_in[:, E * N * J : (E * N + T) * J]
         h_mx = [mx_tiles("h_early", T), (second_mx[0][:, E * N : E * N + T], second_mx[1][:, E * N : E * N + T]), mx_tiles("h_shared", T)]
-        gate_row = sbuf("gate_row", [P, 2, J], F32)
-        gates = [sbuf("gates%d" % r, [P, T], F32) for r in range(2)]
+        gate_row = sbuf("gate_row", [P, GATE_RUN], F32)
+        gates = sbuf("gates", [P, 2 * T], F32)
         identity = sbuf("identity", [P, P], F32)
 
         def load_x(c, u):
@@ -203,26 +204,37 @@ def tile_moe_shr_glu_relu_kernel(tc, xT, w1, w3, w2, gate, offs, pos1, pos2, out
             return banks[4 * batch + half]
 
         term = [raw[1][2 + r][:, 0 : 2 * T].rearrange("p (h n) -> p h n", h=2) for r in range(2)]
-        combined = raw_set[SHARED][BLOCKS - 1][:, 2 * T :].rearrange("p (h n) -> p h n", h=2)
+        combined = [
+            raw_set[SHARED][BLOCKS - 1][:, 2 * T : 3 * T].rearrange("p (h n) -> p h n", h=2),
+            rounded[BLOCKS - 1].bitcast(F32)[:, 0:T].rearrange("p (h n) -> p h n", h=2),
+        ]
 
         def pick(r, half):
-            nc.vector.tensor_tensor(out=term[r][:, half, :], in0=y_sb[half][:].indirect(pos_t[r][:]), in1=gates[r][:], op=MULT)
+            nc.vector.tensor_tensor(out=term[r][:, half, :], in0=y_sb[half][:].indirect(pos_t[r][:]), in1=gates[:, r * T : (r + 1) * T], op=MULT)
 
         def shared_second_layer(bank, lo, hi):
             quantise_hidden(SHARED, lo, hi)
             for half in range(2):
                 second_layer(SHARED, half, bank[:, half * (hi - lo) : (half + 1) * (hi - lo)], lo, hi)
 
+        out_rows = out.rearrange("(h p) t -> p h t", p=P)
+
+        def finish_half(bank, half):
+            result = raw_set[SHARED][BLOCKS - 1][:, T + half * C : T + (half + 1) * C]
+            nc.vector.tensor_add(out=result, in0=bank[:, half * C : (half + 1) * C], in1=combined[0][:, half, :])
+            nc.sync.dma_start(out=out_rows[:, half, 0:C], in_=result)
+
         def finish(bank, lo, hi):
             result = raw_set[SHARED][2][:, 2 * lo : 2 * hi].rearrange("p (h n) -> p h n", h=2)
-            nc.vector.tensor_add(out=result, in0=bank[:, 0 : 2 * (hi - lo)].rearrange("p (h n) -> p h n", h=2), in1=combined[:, :, lo:hi])
-            nc.sync.dma_start(out=out.rearrange("(h p) t -> p h t", p=P)[:, :, lo:hi], in_=result)
+            nc.vector.tensor_add(out=result, in0=bank[:, 0 : 2 * (hi - lo)].rearrange("p (h n) -> p h n", h=2), in1=combined[1][:, :, lo - C : hi - C])
+            nc.sync.dma_start(out=out_rows[:, :, lo:hi], in_=result)
 
         load_x(*planes[0])
         nc.sync.dma_start(offs_t[:], offs)
         for plane in planes[1:]:
             load_x(*plane)
-        nc.sync.dma_start(out=gate_row[:], in_=gate[:, 0, :].rearrange("r (p m) -> p r m", m=J))
+        both = gate.rearrange("r n t -> (r n t)")[(N - 1) * T : (N + 1) * T]
+        nc.sync.dma_start(out=gate_row[:], in_=both.rearrange("(p m) -> p m", m=GATE_RUN))
         for e in range(len(raw)):
             load_first_layer(e, range(BLOCKS))
 
@@ -235,11 +247,13 @@ def tile_moe_shr_glu_relu_kernel(tc, xT, w1, w3, w2, gate, offs, pos1, pos2, out
                 round_all_tokens(c)
 
         make_identity(nc, identity[:])
-        for r in range(2):
-            bank = banks[2 + r]
+        for part in range(2):
+            bank = banks[2 + part]
             for m in range(J):
-                nc.tensor.transpose(bank[:, m * P : (m + 1) * P], gate_row[:, r, m : m + 1].to_broadcast([P, P]), identity[:])
-            nc.scalar.copy(out=gates[r][:].rearrange("p (n m) -> p n m", m=J), in_=bank[:].rearrange("p (m n) -> p n m", m=J))
+                column = gate_row[:, J * part + m : J * part + m + 1]
+                nc.tensor.transpose(bank[:, m * P : (m + 1) * P], column.to_broadcast([P, P]), identity[:])
+            dst = gates[:].rearrange("p (q a m) -> p q a m", a=2, m=J)[:, :, part, :]
+            nc.scalar.copy(out=dst, in_=bank[:].rearrange("p (m q) -> p q m", m=J))
 
         weave_slots(0)
         quantise_slots(0)
@@ -314,7 +328,8 @@ def tile_moe_shr_glu_relu_kernel(tc, xT, w1, w3, w2, gate, offs, pos1, pos2, out
             first_layer(SHARED, 2, 2 + g)
             first_layer(SHARED, 3, 2 + g)
         round_w2(SHARED, nc.scalar.copy)
-        nc.vector.tensor_add(out=combined, in0=term[0], in1=term[1])
+        nc.vector.tensor_add(out=combined[0], in0=term[0][:, :, 0:C], in1=term[1][:, :, 0:C])
+        nc.gpsimd.tensor_add(out=combined[1], in0=term[0][:, :, C:], in1=term[1][:, :, C:])
 
         pieces = [(banks[6], 0, 2 * G), (banks[7], 2 * G, 3 * G), (banks[4], 3 * G, 4 * G)]
         gated(SHARED, 0)
@@ -325,7 +340,8 @@ def tile_moe_shr_glu_relu_kernel(tc, xT, w1, w3, w2, gate, offs, pos1, pos2, out
         shared_second_layer(*pieces[0])
         gated(SHARED, 2)
         gated(SHARED, 3)
+        for half in range(2):
+            shared_second_layer(*pieces[1 + half])
+            finish_half(pieces[0][0], half)
         for piece in pieces[1:]:
-            shared_second_layer(*piece)
-        for piece in pieces:
             finish(*piece)

@@ -32,7 +32,7 @@ WINDOW = 704
 
 HALF_SHARE = 64
 FINAL_SHARE = 40
-LAST_SHARE = 76
+LAST_SHARE = 88
 
 
 def tile_moe_shr_glu_relu_kernel(tc, xT, w1, w3, w2, gate, offs, pos1, pos2, out):
@@ -80,7 +80,7 @@ def tile_moe_shr_glu_relu_kernel(tc, xT, w1, w3, w2, gate, offs, pos1, pos2, out
 
         scalar_w2 = twice.tile([P, 2 * J * N], F32, name="scalar_w2", offset=0)
         y_sb = [twice.tile([P, E * C], F32, name="y_sb%d" % half, offset=half * E * C * 4) for half in range(2)]
-        raw2 = [raw[1][1][:, 0 : J * N], scalar_w2[:, 0 : J * N], scalar_w2[:, J * N :], raw[1][1][:, J * N :], raw[0][1][:, 0 : J * N]]
+        raw2 = [raw[1][1][:, 0 : J * N], raw[1][1][:, J * N :], scalar_w2[:, 0 : J * N], scalar_w2[:, J * N :], raw[0][1][:, 0 : J * N]]
         second_in = sbuf("second_in", [P, (E * N + T + N) * J], BF16)
         second_mx = mx_tiles("second", E * N + T + N)
         w2_at = [0, N, 2 * N, 3 * N, E * N + T]
@@ -155,11 +155,9 @@ def tile_moe_shr_glu_relu_kernel(tc, xT, w1, w3, w2, gate, offs, pos1, pos2, out
         def quantise_block(b):
             quantise(w_mx[b // KC], slice((b % KC) * H, (b % KC + 1) * H), rounded[b])
 
-        def round_w2(e, copy):
-            copy(
-                out=second_in[:, w2_at[e] * J : (w2_at[e] + N) * J].rearrange("p (n i j) -> p n j i", i=2, j=J),
-                in_=raw2[e].rearrange("p (j n i) -> p n j i", j=J, i=2),
-            )
+        def round_w2(e, copy, lo=0, hi=N // 2):
+            dst = second_in[:, w2_at[e] * J : (w2_at[e] + N) * J].rearrange("p (n i j) -> p n j i", i=2, j=J)
+            copy(out=dst[:, lo:hi], in_=raw2[e].rearrange("p (j n i) -> p n j i", j=J, i=2)[:, lo:hi])
 
         def quantise_second(first, width):
             quantise(second_mx, slice(first, first + width), second_in[:, first * J : (first + width) * J])
@@ -299,12 +297,14 @@ def tile_moe_shr_glu_relu_kernel(tc, xT, w1, w3, w2, gate, offs, pos1, pos2, out
         round_w2(0, nc.vector.tensor_copy)
         for g in groups:
             gated(LAST, g)
+        quantise_second(0, N)
         quantise_hidden(LAST, C, S)
         load_w2(SHARED)
         round_w2(1, nc.scalar.copy)
-        quantise_second(0, 2 * N)
+        quantise_second(N, N)
         round_w2(2, nc.scalar.copy)
-        round_w2(LAST, nc.vector.tensor_copy)
+        round_w2(LAST, nc.vector.tensor_copy, 0, LAST_SHARE)
+        round_w2(LAST, nc.scalar.copy, LAST_SHARE, N // 2)
         quantise_second(2 * N, 2 * N)
         for batch in range(E // BATCH):
             for half in range(2):

@@ -31,7 +31,7 @@ GATE_RUN = 2 * T // P
 WINDOW = 704
 
 HALF_SHARE = 64
-FINAL_SHARE = 40
+FINAL_SHARE = 52
 LAST_SHARE = 88
 
 
@@ -71,7 +71,8 @@ def tile_moe_shr_glu_relu_kernel(tc, xT, w1, w3, w2, gate, offs, pos1, pos2, out
         x_raw = dict([((c, u), x_all[:, (2 * c + u) * 2 * T : (2 * c + u + 1) * 2 * T].rearrange("p (e n) -> p e n", e=2)) for c, u in planes])
         x_pair = sbuf("x_pair", [P, (3 * T + WINDOW) * 2], BF16)
 
-        raw = [[sbuf("raw%d%d" % (s, b), [P, J * H], F32) for b in range(BLOCKS)] for s in range(3)]
+        wide = sbuf("wide_raw", [P, T + J * H], F32)
+        raw = [[wide[:, T:] if (s, b) == (2, 1) else sbuf("raw%d%d" % (s, b), [P, J * H], F32)[:] for b in range(BLOCKS)] for s in range(3)]
         raw_set = [raw[0], raw[1], raw[2], raw[0], raw[2]]
 
         rounded_layer = [sbuf("rounded_layer%d" % layer, [P, KC * H * J], BF16) for layer in range(2)]
@@ -201,7 +202,7 @@ def tile_moe_shr_glu_relu_kernel(tc, xT, w1, w3, w2, gate, offs, pos1, pos2, out
         def slot_bank(batch, half):
             return banks[4 * batch + half]
 
-        term = [raw[1][2 + r][:, 0 : 2 * T].rearrange("p (h n) -> p h n", h=2) for r in range(2)]
+        term = [raw[1][2][:, 0 : 2 * T].rearrange("p (h n) -> p h n", h=2), wide[:, 0 : 2 * T].rearrange("p (h n) -> p h n", h=2)]
         combined = [
             raw_set[SHARED][BLOCKS - 1][:, 2 * T : 3 * T].rearrange("p (h n) -> p h n", h=2),
             rounded[BLOCKS - 1].bitcast(F32)[:, 0:T].rearrange("p (h n) -> p h n", h=2),
@@ -229,8 +230,8 @@ def tile_moe_shr_glu_relu_kernel(tc, xT, w1, w3, w2, gate, offs, pos1, pos2, out
 
         load_x(*planes[0])
         nc.sync.dma_start(offs_t[:], offs)
-        for plane in planes[1:]:
-            load_x(*plane)
+        load_x(*planes[1])
+        nc.sync.dma_start(out=x_all[:, 0 : J * T], in_=xT[0 : P * J, :].rearrange("(p j) w -> p (j w)", j=J))
         both = gate.rearrange("r n t -> (r n t)")[(N - 1) * T : (N + 1) * T]
         nc.sync.dma_start(out=gate_row[:], in_=both.rearrange("(p m) -> p m", m=GATE_RUN))
         for e in range(len(raw)):
@@ -319,8 +320,11 @@ def tile_moe_shr_glu_relu_kernel(tc, xT, w1, w3, w2, gate, offs, pos1, pos2, out
             round_block(SHARED, b)
             if b < 2:
                 pick(b, 0)
-                pick(b, 1)
+            if b == 0:
+                pick(0, 1)
             quantise_block(b)
+            if b == 1:
+                pick(1, 1)
             for g in groups if b < KC else range(2):
                 first_layer(SHARED, b, g)
         for g in range(2):

@@ -32,6 +32,7 @@ WINDOW = 704
 
 HALF_SHARE = 64
 FINAL_SHARE = 52
+FIRST_SHARE = 76
 LAST_SHARE = 88
 
 
@@ -86,11 +87,8 @@ def tile_moe_shr_glu_relu_kernel(tc, xT, w1, w3, w2, gate, offs, pos1, pos2, out
         second_mx = mx_tiles("second", E * N + T + N)
         w2_at = [0, N, 2 * N, 3 * N, E * N + T]
 
-        early_words = sbuf("early_words", [P, KC * 2 * S], F32)
-        late_words = sbuf("late_words", [P, KC * 2 * S], F32)
-        words = [early_words[:].rearrange("p (c u n) -> p c u n", c=KC, u=2), late_words[:].rearrange("p (c u n) -> p c u n", c=KC, u=2)]
-        woven = [sbuf("early_woven", [P, KC * 2 * S], F32), raw[0][1]]
-        slot_mx = [mx_tiles("slots%d" % batch, KC * S) for batch in range(E // BATCH)]
+        words = [sbuf("words%d" % c, [P, 2 * E * C], F32) for c in range(KC)]
+        slot_mx = mx_tiles("slots", KC * E * C)
         all_woven = sbuf("all_woven", [P, KC * T * J], BF16)
         all_mx = mx_tiles("all", KC * T)
 
@@ -121,16 +119,17 @@ def tile_moe_shr_glu_relu_kernel(tc, xT, w1, w3, w2, gate, offs, pos1, pos2, out
 
         def gather(batch, c, u):
             window = pair_plane(c, u, WINDOW).bitcast(U32)
-            nc.vector.tensor_copy(words[batch][:, c, u, :].bitcast(U32), window.indirect(offs_t[:, batch * S // 16 : (batch + 1) * S // 16]))
+            first = u * E * C + batch * S
+            nc.vector.tensor_copy(words[c][:, first : first + S].bitcast(U32), window.indirect(offs_t[:, batch * S // 16 : (batch + 1) * S // 16]))
 
-        def weave_slots(batch):
-            nc.vector.tensor_copy(
-                out=woven[batch][:].bitcast(I32).rearrange("p (c n u) -> p c n u", c=KC, u=2),
-                in_=words[batch].bitcast(I32).rearrange("p c u n -> p c n u"),
-            )
+        def woven(c):
+            return x_all[:, (1 - c) * J * T : (2 - c) * J * T]
 
-        def quantise_slots(batch):
-            quantise(slot_mx[batch], slice(0, KC * S), woven[batch][:].bitcast(BF16))
+        def weave_slots(c, copy):
+            copy(out=woven(c).bitcast(I32).rearrange("p (n u) -> p n u", u=2), in_=words[c][:].bitcast(I32).rearrange("p (u n) -> p n u", u=2))
+
+        def quantise_slots(c):
+            quantise(slot_mx, slice(c * E * C, (c + 1) * E * C), woven(c).bitcast(BF16))
 
         def round_all_tokens(c):
             span = slice(c * J * T, (c + 1) * J * T)
@@ -139,7 +138,7 @@ def tile_moe_shr_glu_relu_kernel(tc, xT, w1, w3, w2, gate, offs, pos1, pos2, out
 
         def vector_share(e, b):
             if e == SHARED:
-                return P if b == 0 else FINAL_SHARE if b == BLOCKS - 1 else 0
+                return FIRST_SHARE if b == 0 else FINAL_SHARE if b == BLOCKS - 1 else 0
             if e == LAST and b >= KC:
                 return LAST_SHARE if b == BLOCKS - 1 else HALF_SHARE
             return P if e > 0 and b % KC == 0 else 0
@@ -170,7 +169,7 @@ def tile_moe_shr_glu_relu_kernel(tc, xT, w1, w3, w2, gate, offs, pos1, pos2, out
 
         def first_layer(e, b, g):
             layer, c = divmod(b, KC)
-            tokens, first = (all_mx, c * T) if e == SHARED else (slot_mx[e // BATCH], c * S + (e % BATCH) * C)
+            tokens, first = (all_mx, c * T) if e == SHARED else (slot_mx, c * E * C + e * C)
             cols = slice(first + g * G, first + (g + 1) * G)
             for t in range(J):
                 acc = first_bank(e, layer, g)[:, t * G : (t + 1) * G]
@@ -198,9 +197,6 @@ def tile_moe_shr_glu_relu_kernel(tc, xT, w1, w3, w2, gate, offs, pos1, pos2, out
 
         def second_layer(e, half, acc, lo, hi):
             matmul(acc, second_mx, slice(w2_at[e] + half * P, w2_at[e] + (half + 1) * P), h_mx[e // BATCH], slice(lo, hi), True, True)
-
-        def slot_bank(batch, half):
-            return banks[4 * batch + half]
 
         term = [raw[1][2][:, 0 : 2 * T].rearrange("p (h n) -> p h n", h=2), wide[:, 0 : 2 * T].rearrange("p (h n) -> p h n", h=2)]
         combined = [
@@ -254,7 +250,9 @@ def tile_moe_shr_glu_relu_kernel(tc, xT, w1, w3, w2, gate, offs, pos1, pos2, out
             dst = gates[:].rearrange("p (q a m) -> p q a m", a=2, m=J)[:, :, part, :]
             nc.scalar.copy(out=dst, in_=bank[:].rearrange("p (m q) -> p q m", m=J))
 
-        weave_slots(0)
+        weave_slots(1, nc.gpsimd.tensor_copy)
+        weave_slots(0, nc.vector.tensor_copy)
+        quantise_slots(1)
         quantise_slots(0)
 
         groups = range(C // G)
@@ -283,9 +281,7 @@ def tile_moe_shr_glu_relu_kernel(tc, xT, w1, w3, w2, gate, offs, pos1, pos2, out
                     for g in groups:
                         relu(e, g)
                 if (e, b) == (0, 1):
-                    weave_slots(1)
                     quantise(all_mx, slice(0, KC * T), all_woven[:])
-                    quantise_slots(1)
             if e == 1:
                 load_first_layer(LAST, range(BLOCKS))
                 for routed in range(E):
@@ -306,14 +302,18 @@ def tile_moe_shr_glu_relu_kernel(tc, xT, w1, w3, w2, gate, offs, pos1, pos2, out
         round_w2(2, nc.scalar.copy)
         round_w2(LAST, nc.vector.tensor_copy, 0, LAST_SHARE)
         round_w2(LAST, nc.scalar.copy, LAST_SHARE, N // 2)
-        quantise_second(2 * N, 2 * N)
-        for batch in range(E // BATCH):
-            for half in range(2):
-                for i in range(BATCH):
-                    second_layer(BATCH * batch + i, half, slot_bank(batch, half)[:, i * C : (i + 1) * C], i * C, (i + 1) * C)
-        for batch in range(E // BATCH):
-            for half in range(2):
-                nc.scalar.copy(out=y_sb[half][:, batch * S : (batch + 1) * S], in_=slot_bank(batch, half)[:])
+        for half in range(2):
+            for e in range(BATCH):
+                second_layer(e, half, banks[half][:, e * C : (e + 1) * C], e * C, (e + 1) * C)
+        for i in range(BATCH):
+            quantise_second((BATCH + i) * N, N)
+            second_layer(BATCH + i, 0, banks[4 + 2 * i][:, 0:C], i * C, (i + 1) * C)
+            second_layer(BATCH + i, 1, banks[5][:, i * C : (i + 1) * C], i * C, (i + 1) * C)
+        nc.scalar.copy(out=y_sb[0][:, 0:S], in_=banks[0][:])
+        nc.vector.tensor_copy(out=y_sb[1][:, 0:S], in_=banks[1][:])
+        for i in range(BATCH):
+            nc.scalar.copy(out=y_sb[0][:, S + i * C : S + (i + 1) * C], in_=banks[4 + 2 * i][:, 0:C])
+        nc.scalar.copy(out=y_sb[1][:, S:], in_=banks[5][:])
 
         groups = range(T // G)
         for b in range(BLOCKS):

from contextlib import ExitStack

import concourse.mybir as mybir
from concourse.masks import make_identity

K, T, E, C, H, N = 1024, 512, 4, 256, 512, 256

FLOPS = 2 * (E * C + T) * (2 * K * H + H * N)

F32 = mybir.dt.float32
BF16 = mybir.dt.bfloat16
U32 = mybir.dt.uint32
I32 = mybir.dt.int32
U16 = mybir.dt.uint16
U8 = mybir.dt.uint8
FP8X4 = mybir.dt.float8_e4m3fn_x4
MULT = mybir.AluOpType.mult
ADD = mybir.AluOpType.add
RELU = mybir.ActivationFunctionType.Relu

P = 128
J = 4
KC = K // (P * J)
G = 128
BLOCKS = 2 * KC
SHARED = E
LAST = E - 1
BATCH = 2
S = BATCH * C
GATE_RUN = 2 * T // P
WINDOW = 704

HALF_SHARE = 64
FINAL_SHARE = 52
FIRST_SHARE = 76
LAST_SHARE = 88


def tile_moe_shr_glu_relu_kernel(tc, xT, w1, w3, w2, gate, offs, pos1, pos2, out):
    nc = tc.nc
    with ExitStack() as ctx:
        keep = ctx.enter_context(tc.tile_pool(name="keep", bufs=1))
        twice = ctx.enter_context(tc.tile_pool(name="twice", bufs=1))
        psum = ctx.enter_context(tc.psum_pool(name="psum", bufs=1))

        def sbuf(name, shape, dtype):
            return keep.tile(shape, dtype, name=name, align_bytes=64)

        def mx_tiles(name, width):
            return sbuf(name + "_codes", [P, width], U32), sbuf(name + "_scales", [P, width], U8)

        def quantise(mx, cols, values):
            nc.vector.quantize_mx(out=mx[0][:, cols].bitcast(FP8X4), scales=mx[1][:, cols], in_=values)

        def matmul(acc, lhs, lhs_cols, rhs, rhs_cols, start, stop):
            nc.tensor.matmul_mx(
                out=acc,
                lhsT=lhs[0][:, lhs_cols].bitcast(FP8X4),
                lhsT_scale=lhs[1][:, lhs_cols],
                rhs=rhs[0][:, rhs_cols].bitcast(FP8X4),
                rhs_scale=rhs[1][:, rhs_cols],
                start=start,
                stop=stop,
            )

        offs_t = keep.tile([P, E * C // 16], U16, name="offs_t")
        pos_t = [keep.tile([P, T // 16], U16, name="pos1_t"), keep.tile([P, T // 16], U16, name="pos2_t")]
        banks = [psum.tile([P, 512], F32, name="bank%d" % b) for b in range(8)]

        planes = [(c, u) for c in reversed(range(KC)) for u in reversed(range(2))]
        x_all = sbuf("x_all", [P, KC * 2 * 2 * T], F32)
        x_raw = dict([((c, u), x_all[:, (2 * c + u) * 2 * T : (2 * c + u + 1) * 2 * T].rearrange("p (e n) -> p e n", e=2)) for c, u in planes])
        x_pair = sbuf("x_pair", [P, (3 * T + WINDOW) * 2], BF16)

        wide = sbuf("wide_raw", [P, T + J * H], F32)
        raw = [[wide[:, T:] if (s, b) == (2, 1) else sbuf("raw%d%d" % (s, b), [P, J * H], F32)[:] for b in range(BLOCKS)] for s in range(3)]
        raw_set = [raw[0], raw[1], raw[2], raw[0], raw[2]]

        rounded_layer = [sbuf("rounded_layer%d" % layer, [P, KC * H * J], BF16) for layer in range(2)]
        rounded = [rounded_layer[b // KC][:, (b % KC) * H * J : (b % KC + 1) * H * J] for b in range(BLOCKS)]
        w_mx = [mx_tiles("w%d" % layer, KC * H) for layer in range(2)]

        scalar_w2 = twice.tile([P, 2 * J * N], F32, name="scalar_w2", offset=0)
        y_sb = [twice.tile([P, E * C], F32, name="y_sb%d" % half, offset=half * E * C * 4) for half in range(2)]
        raw2 = [raw[1][1][:, 0 : J * N], raw[1][1][:, J * N :], scalar_w2[:, 0 : J * N], scalar_w2[:, J * N :], raw[0][1][:, 0 : J * N]]
        second_in = sbuf("second_in", [P, (E * N + T + N) * J], BF16)
        second_mx = mx_tiles("second", E * N + T + N)
        w2_at = [0, N, 2 * N, 3 * N, E * N + T]

        words = [sbuf("words%d" % c, [P, 2 * E * C], F32) for c in range(KC)]
        slot_mx = mx_tiles("slots", KC * E * C)
        all_woven = sbuf("all_woven", [P, KC * T * J], BF16)
        all_mx = mx_tiles("all", KC * T)

        hidden = second_in[:, E * N * J : (E * N + T) * J]
        h_mx = [mx_tiles("h_early", T), (second_mx[0][:, E * N : E * N + T], second_mx[1][:, E * N : E * N + T]), mx_tiles("h_shared", T)]
        gate_row = sbuf("gate_row", [P, GATE_RUN], F32)
        gates = sbuf("gates", [P, 2 * T], F32)
        identity = sbuf("identity", [P, P], F32)

        def load_x(c, u):
            src = xT[c * P * J : (c + 1) * P * J, :].rearrange("(p j) w -> p j w", j=J)
            nc.sync.dma_start(out=x_raw[c, u], in_=src[:, 2 * u : 2 * u + 2, :])

        def load_first_layer(e, blocks):
            for b in blocks:
                rows = (w1, w3)[b // KC][e, (b % KC) * P * J : (b % KC + 1) * P * J, :]
                nc.sync.dma_start(out=raw_set[e][b][:], in_=rows.rearrange("(p j) w -> p (j w)", j=J))

        def load_w2(e):
            nc.sync.dma_start(out=raw2[e].rearrange("p (j n) -> p j n", j=J), in_=w2[e].rearrange("(p j) w -> p j w", j=J))

        def pair_plane(c, u, width):
            first = (2 * c + u) * T
            return x_pair[:, first * 2 : (first + width) * 2]

        def pair_tokens(c, u, copy):
            copy(out=pair_plane(c, u, T).rearrange("p (n i e) -> p n e i", i=4, e=2), in_=x_raw[c, u].rearrange("p e (n i) -> p n e i", i=4))

        def gather(batch, c, u):
            window = pair_plane(c, u, WINDOW).bitcast(U32)
            first = u * E * C + batch * S
            nc.vector.tensor_copy(words[c][:, first : first + S].bitcast(U32), window.indirect(offs_t[:, batch * S // 16 : (batch + 1) * S // 16]))

        def woven(c):
            return x_all[:, (1 - c) * J * T : (2 - c) * J * T]

        def weave_slots(c, copy):
            copy(out=woven(c).bitcast(I32).rearrange("p (n u) -> p n u", u=2), in_=words[c][:].bitcast(I32).rearrange("p (u n) -> p n u", u=2))

        def quantise_slots(c):
            quantise(slot_mx, slice(c * E * C, (c + 1) * E * C), woven(c).bitcast(BF16))

        def round_all_tokens(c):
            span = slice(c * J * T, (c + 1) * J * T)
            dst = all_woven[:, span].rearrange("p (n j) -> p n j", j=J)
            nc.gpsimd.tensor_scalar(out=dst, in0=x_all[:, span].rearrange("p (j n) -> p n j", j=J), scalar1=1.0, scalar2=0.0, op0=MULT, op1=ADD)

        def vector_share(e, b):
            if e == SHARED:
                return FIRST_SHARE if b == 0 else FINAL_SHARE if b == BLOCKS - 1 else 0
            if e == LAST and b >= KC:
                return LAST_SHARE if b == BLOCKS - 1 else HALF_SHARE
            return P if e > 0 and b % KC == 0 else 0

        def round_block(e, b):
            dst = rounded[b].rearrange("p (t m j) -> p m j t", t=J, j=J)
            src = raw_set[e][b][:].rearrange("p (j m t) -> p m j t", j=J, t=J)
            share = vector_share(e, b)
            if share < P:
                nc.scalar.copy(out=dst[:, share:], in_=src[:, share:])
            if share > 0:
                nc.vector.tensor_copy(out=dst[:, :share], in_=src[:, :share])

        def quantise_block(b):
            quantise(w_mx[b // KC], slice((b % KC) * H, (b % KC + 1) * H), rounded[b])

        def round_w2(e, copy, lo=0, hi=N // 2):
            dst = second_in[:, w2_at[e] * J : (w2_at[e] + N) * J].rearrange("p (n i j) -> p n j i", i=2, j=J)
            copy(out=dst[:, lo:hi], in_=raw2[e].rearrange("p (j n i) -> p n j i", j=J, i=2)[:, lo:hi])

        def quantise_second(first, width):
            quantise(second_mx, slice(first, first + width), second_in[:, first * J : (first + width) * J])

        def first_bank(e, layer, g):
            if e == SHARED:
                return banks[g if layer == 0 else (4 + g if g < 2 else g - 2)]
            return banks[4 * layer + g + 2 * (e % 2)]

        def first_layer(e, b, g):
            layer, c = divmod(b, KC)
            tokens, first = (all_mx, c * T) if e == SHARED else (slot_mx, c * E * C + e * C)
            cols = slice(first + g * G, first + (g + 1) * G)
            for t in range(J):
                acc = first_bank(e, layer, g)[:, t * G : (t + 1) * G]
                matmul(acc, w_mx[layer], slice(c * H + t * P, c * H + (t + 1) * P), tokens, cols, c == 0 and t == 0, c == KC - 1 and t == J - 1)

        def relu_tile(e, g):
            room = raw_set[e][BLOCKS - 1]
            return room[:, (g % 2) * G * J : (g % 2 + 1) * G * J].rearrange("p (n t i) -> p n t i", t=J, i=2)

        def in_pairs(bank):
            return bank[:].rearrange("p (t n i) -> p n t i", t=J, i=2)

        def relu(e, g):
            nc.scalar.activation(out=relu_tile(e, g), in_=in_pairs(first_bank(e, 0, g)), func=RELU)

        def hidden_of(e):
            return hidden if e == SHARED else hidden[:, (e % BATCH) * C * J :]

        def gated(e, g):
            h = hidden_of(e)[:, g * G * J : (g + 1) * G * J].rearrange("p (n i t) -> p n t i", t=J, i=2)
            nc.vector.tensor_tensor(out=h, in0=in_pairs(first_bank(e, 1, g)), in1=relu_tile(e, g), op=MULT)

        def quantise_hidden(e, lo, hi):
            quantise(h_mx[e // BATCH], slice(lo, hi), hidden[:, lo * J : hi * J])

        def second_layer(e, half, acc, lo, hi):
            matmul(acc, second_mx, slice(w2_at[e] + half * P, w2_at[e] + (half + 1) * P), h_mx[e // BATCH], slice(lo, hi), True, True)

        term = [raw[1][2][:, 0 : 2 * T].rearrange("p (h n) -> p h n", h=2), wide[:, 0 : 2 * T].rearrange("p (h n) -> p h n", h=2)]
        combined = [
            raw_set[SHARED][BLOCKS - 1][:, 2 * T : 3 * T].rearrange("p (h n) -> p h n", h=2),
            rounded[BLOCKS - 1].bitcast(F32)[:, 0:T].rearrange("p (h n) -> p h n", h=2),
        ]

        def pick(r, half):
            nc.vector.tensor_tensor(out=term[r][:, half, :], in0=y_sb[half][:].indirect(pos_t[r][:]), in1=gates[:, r * T : (r + 1) * T], op=MULT)

        def shared_second_layer(bank, lo, hi):
            quantise_hidden(SHARED, lo, hi)
            for half in range(2):
                second_layer(SHARED, half, bank[:, half * (hi - lo) : (half + 1) * (hi - lo)], lo, hi)

        out_rows = out.rearrange("(h p) t -> p h t", p=P)

        def finish_half(bank, half):
            result = raw_set[SHARED][BLOCKS - 1][:, T + half * C : T + (half + 1) * C]
            nc.vector.tensor_add(out=result, in0=bank[:, half * C : (half + 1) * C], in1=combined[0][:, half, :])
            nc.sync.dma_start(out=out_rows[:, half, 0:C], in_=result)

        def finish(bank, lo, hi):
            result = raw_set[SHARED][2][:, 2 * lo : 2 * hi].rearrange("p (h n) -> p h n", h=2)
            nc.vector.tensor_add(out=result, in0=bank[:, 0 : 2 * (hi - lo)].rearrange("p (h n) -> p h n", h=2), in1=combined[1][:, :, lo - C : hi - C])
            nc.sync.dma_start(out=out_rows[:, :, lo:hi], in_=result)

        load_x(*planes[0])
        nc.sync.dma_start(offs_t[:], offs)
        load_x(*planes[1])
        nc.sync.dma_start(out=x_all[:, 0 : J * T], in_=xT[0 : P * J, :].rearrange("(p j) w -> p (j w)", j=J))
        both = gate.rearrange("r n t -> (r n t)")[(N - 1) * T : (N + 1) * T]
        nc.sync.dma_start(out=gate_row[:], in_=both.rearrange("(p m) -> p m", m=GATE_RUN))
        for e in range(len(raw)):
            load_first_layer(e, range(BLOCKS))

        nc.gpsimd.memset(x_pair[:, 4 * T * 2 :], 0.0)
        for c, u in planes:
            pair_tokens(c, u, nc.vector.tensor_copy if (c, u) == planes[0] else nc.scalar.copy)
            for batch in range(E // BATCH):
                gather(batch, c, u)
            if u == 0:
                round_all_tokens(c)

        make_identity(nc, identity[:])
        for part in range(2):
            bank = banks[2 + part]
            for m in range(J):
                column = gate_row[:, J * part + m : J * part + m + 1]
                nc.tensor.transpose(bank[:, m * P : (m + 1) * P], column.to_broadcast([P, P]), identity[:])
            dst = gates[:].rearrange("p (q a m) -> p q a m", a=2, m=J)[:, :, part, :]
            nc.scalar.copy(out=dst, in_=bank[:].rearrange("p (m q) -> p q m", m=J))

        weave_slots(1, nc.gpsimd.tensor_copy)
        weave_slots(0, nc.vector.tensor_copy)
        quantise_slots(1)
        quantise_slots(0)

        groups = range(C // G)
        for e in range(E):
            for b in range(BLOCKS):
                round_block(e, b)
                if b < KC or e > 0:
                    quantise_block(b)
                    for g in groups:
                        first_layer(e, b, g)
                elif b == BLOCKS - 1:
                    quantise(w_mx[1], slice(0, KC * H), rounded_layer[1][:])
                    for g in groups:
                        first_layer(e, b - 1, g)
                        first_layer(e, b, g)
                if e > 0 and b == 0:
                    for g in groups:
                        gated(e - 1, g)
                    if e == BATCH:
                        quantise_hidden(0, 0, S)
                    if e == LAST:
                        quantise_hidden(BATCH, 0, C)
                if (e, b) == (LAST, 1):
                    load_first_layer(SHARED, [2, 3])
                if b == BLOCKS - 1:
                    for g in groups:
                        relu(e, g)
                if (e, b) == (0, 1):
                    quantise(all_mx, slice(0, KC * T), all_woven[:])
            if e == 1:
                load_first_layer(LAST, range(BLOCKS))
                for routed in range(E):
                    load_w2(routed)
            if e == 2:
                for r in range(2):
                    load_first_layer(SHARED, [r])
                    nc.sync.dma_start(pos_t[r][:], (pos1, pos2)[r])

        round_w2(0, nc.vector.tensor_copy)
        for g in groups:
            gated(LAST, g)
        quantise_second(0, N)
        quantise_hidden(LAST, C, S)
        load_w2(SHARED)
        round_w2(1, nc.scalar.copy)
        quantise_second(N, N)
        round_w2(2, nc.scalar.copy)
        round_w2(LAST, nc.vector.tensor_copy, 0, LAST_SHARE)
        round_w2(LAST, nc.scalar.copy, LAST_SHARE, N // 2)
        for half in range(2):
            for e in range(BATCH):
                second_layer(e, half, banks[half][:, e * C : (e + 1) * C], e * C, (e + 1) * C)
        for i in range(BATCH):
            quantise_second((BATCH + i) * N, N)
            second_layer(BATCH + i, 0, banks[4 + 2 * i][:, 0:C], i * C, (i + 1) * C)
            second_layer(BATCH + i, 1, banks[5][:, i * C : (i + 1) * C], i * C, (i + 1) * C)
        nc.scalar.copy(out=y_sb[0][:, 0:S], in_=banks[0][:])
        nc.vector.tensor_copy(out=y_sb[1][:, 0:S], in_=banks[1][:])
        for i in range(BATCH):
            nc.scalar.copy(out=y_sb[0][:, S + i * C : S + (i + 1) * C], in_=banks[4 + 2 * i][:, 0:C])
        nc.scalar.copy(out=y_sb[1][:, S:], in_=banks[5][:])

        groups = range(T // G)
        for b in range(BLOCKS):
            round_block(SHARED, b)
            if b < 2:
                pick(b, 0)
            if b == 0:
                pick(0, 1)
            quantise_block(b)
            if b == 1:
                pick(1, 1)
            for g in groups if b < KC else range(2):
                first_layer(SHARED, b, g)
        for g in range(2):
            relu(SHARED, g)
            first_layer(SHARED, 2, 2 + g)
            first_layer(SHARED, 3, 2 + g)
        round_w2(SHARED, nc.scalar.copy)
        nc.vector.tensor_add(out=combined[0], in0=term[0][:, :, 0:C], in1=term[1][:, :, 0:C])
        nc.gpsimd.tensor_add(out=combined[1], in0=term[0][:, :, C:], in1=term[1][:, :, C:])

        pieces = [(banks[6], 0, 2 * G), (banks[7], 2 * G, 3 * G), (banks[4], 3 * G, 4 * G)]
        gated(SHARED, 0)
        gated(SHARED, 1)
        relu(SHARED, 2)
        relu(SHARED, 3)
        quantise_second(w2_at[SHARED], N)
        shared_second_layer(*pieces[0])
        gated(SHARED, 2)
        gated(SHARED, 3)
        for half in range(2):
            shared_second_layer(*pieces[1 + half])
            finish_half(pieces[0][0], half)
        for piece in pieces[1:]:
            finish(*piece)
